import numpy as np
import ml_dtypes


def mxq(x, axis, fmt="e4m3"):
    dtype, down = {"e4m3": (ml_dtypes.float8_e4m3fn, 7), "e5m2": (ml_dtypes.float8_e5m2, 14)}[fmt]
    v = np.moveaxis(np.asarray(x, np.float32).astype(ml_dtypes.bfloat16).astype(np.float64), axis, -1)
    blocks = v.reshape(v.shape[:-1] + (-1, 32))
    amax = np.abs(blocks).max(-1, keepdims=True)
    byte = np.maximum(np.where(amax > 0, np.frexp(amax)[1] - 1 + 127, 0) - down, 1)
    scale = np.exp2(byte - 127.0)
    codes = (blocks / scale).astype(np.float32).astype(dtype).astype(np.float64)
    return np.moveaxis((codes * scale).reshape(v.shape), -1, axis)


WIDE = False


def mx_kscale(k):
    if not WIDE:
        return np.ones(k)
    levels = np.array([24, -24, 12, -12, 0])
    if k % 512:
        return np.exp2(np.random.permutation(np.resize(levels, k // 32))).repeat(32)
    a = np.empty((k // 512, 16))
    for p in range(k // 512):
        a[p, :8] = np.random.permutation(np.resize(levels, 8))
        for g in range(8):
            far = levels[np.abs(levels - a[p, g]) >= 10]
            a[p, g + 8] = far[np.random.randint(len(far))]
    return np.exp2(a.ravel()).repeat(32)


def f64(x):
    return np.asarray(x).astype(np.float64)


def striped(idx):
    return np.tile(idx.reshape(-1, 16).T, (8, 1)).astype(np.uint16)


def unstriped(offs):
    return offs[:16].T.reshape(-1).astype(np.int64)


E2M1 = np.array([0.0, 0.5, 1.0, 1.5, 2.0, 3.0, 4.0, 6.0, -0.0, -0.5, -1.0, -1.5, -2.0, -3.0, -4.0, -6.0])


def pack_weight(w, fmt):
    k, n = w.shape
    w = f64(np.asarray(w, np.float32).astype(ml_dtypes.bfloat16)).reshape(k // 32, 32, n)
    amax = np.abs(w).max(1)
    if fmt == "e4m3":
        byte = np.frexp(amax)[1] - 1 + 127 - 7
    else:
        mant, ex = np.frexp(amax / 6.0)
        byte = np.where(mant > 0.5, ex, ex - 1) + 127
    byte = np.clip(np.where(amax > 0, byte, 1), 1, 254)
    scaled = (w * np.exp2(127.0 - byte)[:, None, :]).reshape(k, n).astype(np.float32)
    by_word = np.ascontiguousarray(scaled.reshape(k // 512, 128, 4, n).transpose(0, 1, 3, 2))
    if fmt == "e4m3":
        words = by_word.astype(ml_dtypes.float8_e4m3fn).view(np.uint8)
    else:
        c = by_word.astype(ml_dtypes.float4_e2m1fn).view(np.uint8) & 0xF
        words = (c[..., 0::2] | (c[..., 1::2] << 4)).reshape(k // 512, 128, 2 * n)
    return np.ascontiguousarray(words), np.ascontiguousarray(byte.astype(np.uint8).reshape(k // 512, 16, n))


def unpack_weight(words, scales, fmt):
    g, _, n = scales.shape
    words = np.ascontiguousarray(words).reshape(g, 128, n, -1)
    if fmt == "e4m3":
        vals = words.view(ml_dtypes.float8_e4m3fn).astype(np.float64)
    else:
        nib = np.empty((g, 128, n, 4), np.uint8)
        nib[..., 0::2] = words & 0xF
        nib[..., 1::2] = words >> 4
        vals = E2M1[nib]
    vals = vals * np.repeat(np.exp2(scales.astype(np.float64) - 127.0), 8, axis=1)[..., None]
    return vals.transpose(0, 1, 3, 2).reshape(g * 512, n)


def silu(f):
    return f / (1.0 + np.exp(-np.maximum(f, -700.0)))


K, R, N, T, J = 1024, 512, 512, 2048, 1024


def setup_inputs():
    n = np.random.standard_normal
    s = mx_kscale(K)[:, None]
    u = mx_kscale(R)[:, None]
    p_tab = pack_weight(n((K, T)) * s, "e4m3")
    p_ws = pack_weight(n((K, R)) / np.sqrt(2 * K) / s, "e4m3")
    p_wt = pack_weight(n((K, R)) / np.sqrt(2 * K) / s, "e2m1")
    p_wd = pack_weight(n((R, N)) / np.sqrt(R) / u, "e4m3")
    return {
        "tab_words": p_tab[0],
        "tab_scales": p_tab[1],
        "ws_words": p_ws[0],
        "ws_scales": p_ws[1],
        "wt_words": p_wt[0],
        "wt_scales": p_wt[1],
        "sm": (np.random.uniform(0.5, 2.0, R) * u[:, 0]).astype(np.float32),
        "wd_words": p_wd[0],
        "wd_scales": p_wd[1],
        "wgo": np.tile(np.random.uniform(0.5, 2.0, J), (128, 1)).astype(np.float32),
        "offs": striped(np.random.permutation(T)[:J]),
        "offs2": striped(np.random.permutation(T)[:J]),
    }


def reference(tab_words, tab_scales, ws_words, ws_scales, wt_words, wt_scales, sm, wd_words, wd_scales, wgo, offs, offs2):
    idx = unstriped(offs)
    idx2 = unstriped(offs2)
    tab_ = unpack_weight(tab_words, tab_scales, "e4m3")[:, idx]
    tabb_ = unpack_weight(tab_words, tab_scales, "e4m3")[:, idx2]
    ws_ = unpack_weight(ws_words, ws_scales, "e4m3")
    wt_ = unpack_weight(wt_words, wt_scales, "e2m1")
    a = ws_.T @ tab_ + wt_.T @ tabb_
    h = f64(sm)[:, None] * silu(a)
    h_ = mxq(h, 0, "e4m3")
    wd_ = unpack_weight(wd_words, wd_scales, "e4m3")
    y = wd_.T @ h_
    out = np.zeros((N, T))
    out[:, idx2] = f64(wgo)[0] * (y)
    return out

@@ -1,0 +1,213 @@
+from contextlib import ExitStack
+
+import concourse.mybir as mybir
+
+K, R, N, T, J = 1024, 512, 512, 2048, 1024
+FLOPS = 2 * J * (2 * K * R + R * N)
+
+F32 = mybir.dt.float32
+BF16 = mybir.dt.bfloat16
+I32 = mybir.dt.int32
+U32 = mybir.dt.uint32
+U16 = mybir.dt.uint16
+U8 = mybir.dt.uint8
+FP8X4 = mybir.dt.float8_e4m3fn_x4
+FP4X4 = mybir.dt.float4_e2m1fn_x4
+MULT = mybir.AluOpType.mult
+SILU = mybir.ActivationFunctionType.Silu
+COPY = mybir.ActivationFunctionType.Copy
+
+P = 128
+PACK = 4
+PASSES = K // (P * PACK)
+QUADS = 4
+ROWS = 4
+UNIT = 128
+CHUNK = 256
+CHUNKS = J // CHUNK
+N_TILES = N // P
+WINDOW_BYTES = 4 * T
+SRC, DST = 0, 1
+
+
+def tile_list_msg_silu_none_kernel(
+    tc, tab_words, tab_scales, ws_words, ws_scales, wt_words, wt_scales, sm, wd_words, wd_scales, wgo, offs, offs2, out
+):
+    nc = tc.nc
+    with ExitStack() as ctx:
+        keep = ctx.enter_context(tc.tile_pool(name="keep", bufs=1))
+        shared = ctx.enter_context(tc.tile_pool(name="shared", bufs=1))
+        turns = ctx.enter_context(tc.tile_pool(name="turns", bufs=1))
+        work = ctx.enter_context(tc.tile_pool(name="work", bufs=2))
+        psum = ctx.enter_context(tc.psum_pool(name="psum", bufs=1))
+
+        src_list = keep.tile([P, J // 16], U16, name="src_list")
+        dst_list = keep.tile([P, J // 16], U16, name="dst_list")
+        lists = (src_list, dst_list)
+        tab_sc = keep.tile([P, T // 4], I32, name="tab_sc", align_bytes=64)
+        tab_w = keep.tile([P, PASSES, T], I32, name="tab_w", align_bytes=64)
+        raw_ws = keep.tile([P, PASSES, R], I32, name="raw_ws")
+        raw_wt = shared.tile([P, PASSES, R // 2], I32, name="raw_wt", offset=WINDOW_BYTES)
+        ws_c = keep.tile([P, PASSES, R], I32, name="ws_c", align_bytes=64)
+        wt_c = keep.tile([P, PASSES, R], U16, name="wt_c", align_bytes=64)
+        w_sc = keep.tile([P, PASSES, R], U8, name="w_sc", align_bytes=64)
+        dst_sc1 = keep.tile([P, J // 4], I32, name="dst_sc1", align_bytes=64)
+        y_first = keep.tile([P, 2, J], F32, name="y_first")
+        window0 = keep.tile([P, T], F32, name="window0")
+
+        nc.vector.memset(tab_sc[:], 0)
+        nc.vector.memset(window0[:], 0.0)
+        nc.vector.memset(dst_sc1[:], 0)
+
+        nc.sync.dma_start(dst_list[:], offs2)
+        nc.sync.dma_start(raw_wt[:], wt_words.rearrange("a p b -> p a b").bitcast(I32))
+        nc.sync.dma_start(raw_ws[:], ws_words.rearrange("a p r i -> p a (r i)").bitcast(I32))
+        nc.sync.dma_start(src_list[:], offs)
+        for q in range(QUADS):
+            nc.sync.dma_start(tab_sc[32 * q : 32 * q + 8, :], tab_scales[:, 4 * q : 4 * q + 4, :].bitcast(I32))
+        nc.sync.dma_start(tab_w[:], tab_words.rearrange("a p t i -> p a (t i)").bitcast(I32))
+
+        picked_sc = keep.tile([P, 2, J], U8, name="picked_sc", align_bytes=64)
+        picked_w = {}
+        products = {}
+
+        def gather_words(chunk, a, place):
+            entries = slice(chunk * CHUNK // 16, (chunk + 1) * CHUNK // 16)
+            picked = turns.tile([P, 2, CHUNK], U32, name="picked_w%d_%d" % (chunk, a), align_bytes=64, offset=place)
+            for side in (SRC, DST):
+                nc.vector.tensor_copy(picked[:, side, :], tab_w[:, a, :].bitcast(U32).indirect(lists[side][:, entries]))
+            picked_w[chunk, a] = picked
+
+        def hidden_layer(chunk, place):
+            grouped = turns.tile([P, CHUNK, PACK], BF16, name="grouped%d" % chunk, align_bytes=64, offset=place)
+            for u in range(CHUNK // UNIT):
+                cols = slice(u * UNIT, (u + 1) * UNIT)
+                first = chunk * CHUNK + u * UNIT
+                edges = slice(first, first + UNIT)
+                acc = psum.tile([P, PACK, UNIT], F32, name="acc", bufs=4)
+                for t in range(PACK):
+                    m = slice(t * P, (t + 1) * P)
+                    for a in range(PASSES):
+                        nc.tensor.matmul_mx(
+                            acc[:, t, :],
+                            lhsT=ws_c[:, a, m].bitcast(FP8X4),
+                            lhsT_scale=w_sc[ROWS:P, a, m],
+                            rhs=picked_w[chunk, a][:, SRC, cols].bitcast(FP8X4),
+                            rhs_scale=picked_sc[ROWS * a : P, SRC, edges],
+                            start=(a == 0),
+                            stop=False,
+                        )
+                        nc.tensor.matmul_mx(
+                            acc[:, t, :],
+                            lhsT=wt_c[:, a, m].bitcast(FP4X4),
+                            lhsT_scale=w_sc[:, a, m],
+                            rhs=picked_w[chunk, a][:, DST, cols].bitcast(FP8X4),
+                            rhs_scale=(picked_sc[:, DST, edges], dst_sc1[:].bitcast(U8)[:, edges])[a],
+                            start=False,
+                            stop=(a == PASSES - 1),
+                        )
+                act = work.tile([P, PACK, UNIT], F32, name="act")
+                nc.scalar.activation(act[:], acc[:], SILU)
+                hidden = turns.tile([P, PACK, UNIT], BF16, name="hidden%d_%d" % (chunk, u), offset=(24 + 5 * chunk + u) * KIB)
+                for t in range(PACK):
+                    nc.scalar.activation(hidden[:, t, :], act[:, t, :], COPY, scale=sm_sb[:, t : t + 1])
+                nc.scalar.copy(grouped[:, cols, :], hidden[:].rearrange("p t n -> p n t"))
+            h_c = work.tile([P, CHUNK], U32, name="h_c", align_bytes=64)
+            h_sc = work.tile([P, CHUNK], U8, name="h_sc", align_bytes=64)
+            nc.vector.quantize_mx(h_c[:].bitcast(FP8X4), h_sc[:], grouped[:].rearrange("p n t -> p (n t)"))
+            for pair in range(N_TILES // 2):
+                prod = psum.tile([P, 2, CHUNK], F32, name="prod", bufs=4)
+                for i in range(2):
+                    m = slice((2 * pair + i) * P, (2 * pair + i + 1) * P)
+                    nc.tensor.matmul_mx(
+                        prod[:, i, :],
+                        lhsT=wd_c[:, m].bitcast(FP8X4),
+                        lhsT_scale=wd_sc[:].bitcast(U8)[:, m],
+                        rhs=h_c[:].bitcast(FP8X4),
+                        rhs_scale=h_sc[:],
+                        start=True,
+                        stop=True,
+                    )
+                products[chunk, pair] = prod
+
+        def evacuate(chunk, pair):
+            target = messages(pair, chunk, chunk + 1)
+            nc.scalar.copy(target, products[chunk, pair][:])
+
+        def messages(pair, first, last):
+            if pair == 0:
+                return y_first[:, :, first * CHUNK : last * CHUNK]
+            base = min(first, 2)
+            if base not in y_second:
+                width = CHUNK * (2 if base == 2 else 1)
+                y_second[base] = turns.tile([P, 2, width], F32, name="y_second%d" % base, offset=(24 + 5 * (base + 1) + 1) * KIB)
+            return y_second[base][:, :, (first - base) * CHUNK : (last - base) * CHUNK]
+
+        def scatter(n_tile, first, last):
+            cols = slice(first * CHUNK, last * CHUNK)
+            entries = slice(first * CHUNK // 16, last * CHUNK // 16)
+            source = messages(n_tile // 2, first, last)[:, n_tile % 2, :]
+            nc.vector.tensor_tensor(windows[n_tile][:].indirect(dst_list[:, entries]), source, wgo_sb[:, cols], MULT)
+            if last == CHUNKS:
+                nc.sync.dma_start(out[n_tile * P : (n_tile + 1) * P, :], windows[n_tile][:])
+
+        y_second = {}
+        KIB = 1024
+        nc.vector.tensor_copy(
+            wt_c[:].rearrange("p a (t m) -> p a t m", t=PACK),
+            raw_wt[:].bitcast(U16).rearrange("p a (m t) -> p a t m", t=PACK),
+        )
+        raw_sc = shared.tile([P, 2 * T + 32], I32, name="raw_sc", offset=WINDOW_BYTES - 64)
+        used = PASSES * R // 4
+        nc.vector.memset(raw_sc[:, 0:used], 0)
+        for q in range(QUADS):
+            for first, scales in ((0, wt_scales), (ROWS, ws_scales)):
+                nc.scalar.dma_start(
+                    raw_sc[32 * q + first : 32 * q + first + ROWS, 0:used].rearrange("p (a w) -> p a w", a=PASSES),
+                    scales[:, 4 * q : 4 * q + 4, :].rearrange("a r n -> r a n").bitcast(I32),
+                )
+        nc.vector.tensor_copy(
+            ws_c[:].rearrange("p a (t m) -> p a m t", t=PACK),
+            raw_ws[:].rearrange("p a (m t) -> p a m t", t=PACK),
+        )
+        nc.vector.tensor_copy(picked_sc[:, DST, :], tab_sc[:].bitcast(U8).indirect(dst_list[:]))
+        nc.scalar.dma_start(dst_sc1[0:100, :], picked_sc[ROWS : ROWS + 100, DST, :].bitcast(I32))
+        nc.vector.tensor_copy(picked_sc[:, SRC, :], tab_sc[:].bitcast(U8).indirect(src_list[:]))
+        nc.vector.tensor_copy(
+            w_sc[:].rearrange("p a (t m) -> p a t m", t=PACK),
+            raw_sc[:, 0:used].bitcast(U8).rearrange("p (a m t) -> p a t m", a=PASSES, t=PACK),
+        )
+        late = 2 * WINDOW_BYTES
+        wgo_sb = shared.tile([P, J], F32, name="wgo_sb", offset=late)
+        wd_c = shared.tile([P, N], I32, name="wd_c", offset=late + 4 * J, align_bytes=64)
+        wd_sc = shared.tile([P, N // 4], I32, name="wd_sc", offset=late + 4 * J + 4 * N, align_bytes=64)
+        sm_sb = shared.tile([P, PACK], F32, name="sm_sb", offset=late + 4 * J + 5 * N)
+        nc.gpsimd.memset(wd_sc[:], 0)
+        nc.sync.dma_start(sm_sb[:], sm.rearrange("(p t) -> p t", t=PACK))
+        nc.sync.dma_start(wd_c[:], wd_words[0].rearrange("p n i -> p (n i)").bitcast(I32))
+        for q in range(QUADS):
+            nc.sync.dma_start(wd_sc[32 * q : 32 * q + ROWS, :], wd_scales[0, 4 * q : 4 * q + 4, :].bitcast(I32))
+        nc.sync.dma_start(wgo_sb[:], wgo)
+        windows = [window0]
+        for n_tile, place in ((1, 0), (2, WINDOW_BYTES), (3, 3 * WINDOW_BYTES - 64)):
+            window = shared.tile([P, T], F32, name="window%d" % n_tile, offset=place)
+            nc.gpsimd.memset(window[:], 0.0)
+            windows.append(window)
+
+        for step in range(CHUNKS * PASSES - 1):
+            gather_words(step // PASSES, step % PASSES, 2 * step * KIB)
+        hidden_layer(0, 14 * KIB)
+        gather_words(CHUNKS - 1, PASSES - 1, 14 * KIB)
+        evacuate(0, 0)
+        for chunk in range(1, CHUNKS):
+            hidden_layer(chunk, (14 + 2 * chunk) * KIB)
+            evacuate(chunk - 1, 1)
+            evacuate(chunk, 0)
+        evacuate(CHUNKS - 1, 1)
+        for chunk in range(2):
+            for n_tile in range(N_TILES):
+                scatter(n_tile, chunk, chunk + 1)
+        for chunk in range(2, CHUNKS):
+            for n_tile in range(N_TILES - 1):
+                scatter(n_tile, chunk, chunk + 1)
+        scatter(N_TILES - 1, 2, CHUNKS)

@@ -28,6 +28,7 @@ CHUNKS = J // CHUNK
 N_TILES = N // P
 WINDOW_BYTES = 4 * T
 SRC, DST = 0, 1
+KIB = 1024
 
 
 def tile_list_msg_silu_none_kernel(
@@ -45,9 +46,12 @@ def tile_list_msg_silu_none_kernel(
         dst_list = keep.tile([P, J // 16], U16, name="dst_list")
         lists = (src_list, dst_list)
         tab_sc = keep.tile([P, T // 4], I32, name="tab_sc", align_bytes=64)
-        tab_w = keep.tile([P, PASSES, T], I32, name="tab_w", align_bytes=64)
+        tab_w = [keep.tile([P, T], I32, name="tab_w%d" % a) for a in range(PASSES)]
         raw_ws = keep.tile([P, PASSES, R], I32, name="raw_ws")
-        raw_wt = shared.tile([P, PASSES, R // 2], I32, name="raw_wt", offset=WINDOW_BYTES)
+        raw_wt = shared.tile([P, T + 32], I32, name="raw_wt", offset=WINDOW_BYTES - 64)
+        raw_sc = turns.tile([P, 17 * KIB // 4], I32, name="raw_sc", offset=4 * KIB)
+        wt_used = PASSES * R // 2
+        sc_used = PASSES * R // 4
         ws_c = keep.tile([P, PASSES, R], I32, name="ws_c", align_bytes=64)
         wt_c = keep.tile([P, PASSES, R], U16, name="wt_c", align_bytes=64)
         w_sc = keep.tile([P, PASSES, R], U8, name="w_sc", align_bytes=64)
@@ -56,16 +60,29 @@ def tile_list_msg_silu_none_kernel(
         window0 = keep.tile([P, T], F32, name="window0")
 
         nc.vector.memset(tab_sc[:], 0)
+        nc.vector.memset(raw_sc[:, 0:sc_used], 0)
         nc.vector.memset(window0[:], 0.0)
         nc.vector.memset(dst_sc1[:], 0)
 
+        def load_weight_scales(piece, queue):
+            q, first, scales = piece // 2, ROWS * (piece % 2), (wt_scales, ws_scales)[piece % 2]
+            queue.dma_start(
+                raw_sc[32 * q + first : 32 * q + first + ROWS, 0:sc_used].rearrange("p (a w) -> p a w", a=PASSES),
+                scales[:, 4 * q : 4 * q + 4, :].rearrange("a r n -> r a n").bitcast(I32),
+            )
+
         nc.sync.dma_start(dst_list[:], offs2)
-        nc.sync.dma_start(raw_wt[:], wt_words.rearrange("a p b -> p a b").bitcast(I32))
-        nc.sync.dma_start(raw_ws[:], ws_words.rearrange("a p r i -> p a (r i)").bitcast(I32))
-        nc.sync.dma_start(src_list[:], offs)
+        nc.sync.dma_start(
+            raw_wt[:, 0:wt_used].rearrange("p (a w) -> p a w", a=PASSES), wt_words.rearrange("a p b -> p a b").bitcast(I32)
+        )
         for q in range(QUADS):
             nc.sync.dma_start(tab_sc[32 * q : 32 * q + 8, :], tab_scales[:, 4 * q : 4 * q + 4, :].bitcast(I32))
-        nc.sync.dma_start(tab_w[:], tab_words.rearrange("a p t i -> p a (t i)").bitcast(I32))
+        nc.sync.dma_start(src_list[:], offs)
+        nc.sync.dma_start(tab_w[0][:], tab_words[0].rearrange("p t i -> p (t i)").bitcast(I32))
+        nc.sync.dma_start(raw_ws[:], ws_words.rearrange("a p r i -> p a (r i)").bitcast(I32))
+        nc.sync.dma_start(tab_w[1][:], tab_words[1].rearrange("p t i -> p (t i)").bitcast(I32))
+        for piece in range(2 * QUADS):
+            load_weight_scales(piece, nc.sync if piece < 6 else nc.gpsimd)
 
         picked_sc = keep.tile([P, 2, J], U8, name="picked_sc", align_bytes=64)
         picked_w = {}
@@ -75,21 +92,21 @@ def tile_list_msg_silu_none_kernel(
             entries = slice(chunk * CHUNK // 16, (chunk + 1) * CHUNK // 16)
             picked = turns.tile([P, 2, CHUNK], U32, name="picked_w%d_%d" % (chunk, a), align_bytes=64, offset=place)
             for side in (SRC, DST):
-                nc.vector.tensor_copy(picked[:, side, :], tab_w[:, a, :].bitcast(U32).indirect(lists[side][:, entries]))
+                nc.vector.tensor_copy(picked[:, side, :], tab_w[a][:].bitcast(U32).indirect(lists[side][:, entries]))
             picked_w[chunk, a] = picked
 
         def hidden_layer(chunk, place):
             grouped = turns.tile([P, CHUNK, PACK], BF16, name="grouped%d" % chunk, align_bytes=64, offset=place)
-            for u in range(CHUNK // UNIT):
-                cols = slice(u * UNIT, (u + 1) * UNIT)
-                first = chunk * CHUNK + u * UNIT
-                edges = slice(first, first + UNIT)
-                acc = psum.tile([P, PACK, UNIT], F32, name="acc", bufs=4)
-                for t in range(PACK):
-                    m = slice(t * P, (t + 1) * P)
+            hidden = turns.tile([P, PACK, CHUNK], BF16, name="hidden%d" % chunk, offset=(32 + 4 * chunk) * KIB)
+            for t in range(PACK):
+                m = slice(t * P, (t + 1) * P)
+                acc = psum.tile([P, CHUNK], F32, name="acc", bufs=4)
+                for u in range(CHUNK // UNIT):
+                    cols = slice(u * UNIT, (u + 1) * UNIT)
+                    edges = slice(chunk * CHUNK + u * UNIT, chunk * CHUNK + (u + 1) * UNIT)
                     for a in range(PASSES):
                         nc.tensor.matmul_mx(
-                            acc[:, t, :],
+                            acc[:, cols],
                             lhsT=ws_c[:, a, m].bitcast(FP8X4),
                             lhsT_scale=w_sc[ROWS:P, a, m],
                             rhs=picked_w[chunk, a][:, SRC, cols].bitcast(FP8X4),
@@ -98,7 +115,7 @@ def tile_list_msg_silu_none_kernel(
                             stop=False,
                         )
                         nc.tensor.matmul_mx(
-                            acc[:, t, :],
+                            acc[:, cols],
                             lhsT=wt_c[:, a, m].bitcast(FP4X4),
                             lhsT_scale=w_sc[:, a, m],
                             rhs=picked_w[chunk, a][:, DST, cols].bitcast(FP8X4),
@@ -106,12 +123,10 @@ def tile_list_msg_silu_none_kernel(
                             start=False,
                             stop=(a == PASSES - 1),
                         )
-                act = work.tile([P, PACK, UNIT], F32, name="act")
+                act = work.tile([P, CHUNK], F32, name="act")
                 nc.scalar.activation(act[:], acc[:], SILU)
-                hidden = turns.tile([P, PACK, UNIT], BF16, name="hidden%d_%d" % (chunk, u), offset=(24 + 5 * chunk + u) * KIB)
-                for t in range(PACK):
-                    nc.scalar.activation(hidden[:, t, :], act[:, t, :], COPY, scale=sm_sb[:, t : t + 1])
-                nc.scalar.copy(grouped[:, cols, :], hidden[:].rearrange("p t n -> p n t"))
+                nc.scalar.activation(hidden[:, t, :], act[:], COPY, scale=sm_sb[:, t : t + 1])
+            nc.scalar.copy(grouped[:], hidden[:].rearrange("p t n -> p n t"))
             h_c = work.tile([P, CHUNK], U32, name="h_c", align_bytes=64)
             h_sc = work.tile([P, CHUNK], U8, name="h_sc", align_bytes=64)
             nc.vector.quantize_mx(h_c[:].bitcast(FP8X4), h_sc[:], grouped[:].rearrange("p n t -> p (n t)"))
@@ -140,7 +155,7 @@ def tile_list_msg_silu_none_kernel(
             base = min(first, 2)
             if base not in y_second:
                 width = CHUNK * (2 if base == 2 else 1)
-                y_second[base] = turns.tile([P, 2, width], F32, name="y_second%d" % base, offset=(24 + 5 * (base + 1) + 1) * KIB)
+                y_second[base] = turns.tile([P, 2, width], F32, name="y_second%d" % base, offset=(32 + 4 * (base + 1)) * KIB)
             return y_second[base][:, :, (first - base) * CHUNK : (last - base) * CHUNK]
 
         def scatter(n_tile, first, last):
@@ -152,55 +167,47 @@ def tile_list_msg_silu_none_kernel(
                 nc.sync.dma_start(out[n_tile * P : (n_tile + 1) * P, :], windows[n_tile][:])
 
         y_second = {}
-        KIB = 1024
         nc.vector.tensor_copy(
             wt_c[:].rearrange("p a (t m) -> p a t m", t=PACK),
-            raw_wt[:].bitcast(U16).rearrange("p a (m t) -> p a t m", t=PACK),
+            raw_wt[:, 0:wt_used].bitcast(U16).rearrange("p (a m t) -> p a t m", a=PASSES, t=PACK),
         )
-        raw_sc = shared.tile([P, 2 * T + 32], I32, name="raw_sc", offset=WINDOW_BYTES - 64)
-        used = PASSES * R // 4
-        nc.vector.memset(raw_sc[:, 0:used], 0)
-        for q in range(QUADS):
-            for first, scales in ((0, wt_scales), (ROWS, ws_scales)):
-                nc.scalar.dma_start(
-                    raw_sc[32 * q + first : 32 * q + first + ROWS, 0:used].rearrange("p (a w) -> p a w", a=PASSES),
-                    scales[:, 4 * q : 4 * q + 4, :].rearrange("a r n -> r a n").bitcast(I32),
-                )
+        windows = [window0]
+        for n_tile in range(1, N_TILES):
+            window = shared.tile([P, T], F32, name="window%d" % n_tile, offset=(n_tile - 1) * WINDOW_BYTES)
+            nc.gpsimd.memset(window[:], 0.0)
+            windows.append(window)
+        nc.vector.tensor_copy(picked_sc[:, DST, :], tab_sc[:].bitcast(U8).indirect(dst_list[:]))
+        nc.scalar.dma_start(dst_sc1[0:100, :], picked_sc[ROWS : ROWS + 100, DST, :].bitcast(I32))
+        nc.vector.tensor_copy(picked_sc[:, SRC, :], tab_sc[:].bitcast(U8).indirect(src_list[:]))
+        gather_words(0, 0, 0)
         nc.vector.tensor_copy(
             ws_c[:].rearrange("p a (t m) -> p a m t", t=PACK),
             raw_ws[:].rearrange("p a (m t) -> p a m t", t=PACK),
         )
-        nc.vector.tensor_copy(picked_sc[:, DST, :], tab_sc[:].bitcast(U8).indirect(dst_list[:]))
-        nc.scalar.dma_start(dst_sc1[0:100, :], picked_sc[ROWS : ROWS + 100, DST, :].bitcast(I32))
-        nc.vector.tensor_copy(picked_sc[:, SRC, :], tab_sc[:].bitcast(U8).indirect(src_list[:]))
+        gather_words(0, 1, 2 * KIB)
         nc.vector.tensor_copy(
             w_sc[:].rearrange("p a (t m) -> p a t m", t=PACK),
-            raw_sc[:, 0:used].bitcast(U8).rearrange("p (a m t) -> p a t m", a=PASSES, t=PACK),
+            raw_sc[:, 0:sc_used].bitcast(U8).rearrange("p (a m t) -> p a t m", a=PASSES, t=PACK),
         )
-        late = 2 * WINDOW_BYTES
-        wgo_sb = shared.tile([P, J], F32, name="wgo_sb", offset=late)
-        wd_c = shared.tile([P, N], I32, name="wd_c", offset=late + 4 * J, align_bytes=64)
-        wd_sc = shared.tile([P, N // 4], I32, name="wd_sc", offset=late + 4 * J + 4 * N, align_bytes=64)
-        sm_sb = shared.tile([P, PACK], F32, name="sm_sb", offset=late + 4 * J + 5 * N)
+        late = 14 * KIB
+        sm_sb = turns.tile([P, PACK], F32, name="sm_sb", offset=late)
+        wd_sc = turns.tile([P, N // 4], I32, name="wd_sc", offset=late + 64, align_bytes=64)
+        wd_c = turns.tile([P, N], I32, name="wd_c", offset=late + 64 + N, align_bytes=64)
+        wgo_sb = turns.tile([P, J], F32, name="wgo_sb", offset=late + 64 + 5 * N)
         nc.gpsimd.memset(wd_sc[:], 0)
         nc.sync.dma_start(sm_sb[:], sm.rearrange("(p t) -> p t", t=PACK))
         nc.sync.dma_start(wd_c[:], wd_words[0].rearrange("p n i -> p (n i)").bitcast(I32))
         for q in range(QUADS):
             nc.sync.dma_start(wd_sc[32 * q : 32 * q + ROWS, :], wd_scales[0, 4 * q : 4 * q + 4, :].bitcast(I32))
         nc.sync.dma_start(wgo_sb[:], wgo)
-        windows = [window0]
-        for n_tile, place in ((1, 0), (2, WINDOW_BYTES), (3, 3 * WINDOW_BYTES - 64)):
-            window = shared.tile([P, T], F32, name="window%d" % n_tile, offset=place)
-            nc.gpsimd.memset(window[:], 0.0)
-            windows.append(window)
 
-        for step in range(CHUNKS * PASSES - 1):
+        for step in range(PASSES, CHUNKS * PASSES - 1):
             gather_words(step // PASSES, step % PASSES, 2 * step * KIB)
-        hidden_layer(0, 14 * KIB)
-        gather_words(CHUNKS - 1, PASSES - 1, 14 * KIB)
+        hidden_layer(0, 22 * KIB)
+        gather_words(CHUNKS - 1, PASSES - 1, 22 * KIB)
         evacuate(0, 0)
         for chunk in range(1, CHUNKS):
-            hidden_layer(chunk, (14 + 2 * chunk) * KIB)
+            hidden_layer(chunk, (22 + 2 * chunk) * KIB)
             evacuate(chunk - 1, 1)
             evacuate(chunk, 0)
         evacuate(CHUNKS - 1, 1)

@@ -48,7 +48,7 @@ def tile_list_msg_silu_none_kernel(
         tab_sc = keep.tile([P, T // 4], I32, name="tab_sc", align_bytes=64)
         tab_w = [keep.tile([P, T], I32, name="tab_w%d" % a) for a in range(PASSES)]
         raw_ws = keep.tile([P, PASSES, R], I32, name="raw_ws")
-        raw_wt = shared.tile([P, T + 32], I32, name="raw_wt", offset=WINDOW_BYTES - 64)
+        raw_wt = shared.tile([P, PASSES * R // 2], I32, name="raw_wt", offset=WINDOW_BYTES - KIB)
         raw_sc = turns.tile([P, 17 * KIB // 4], I32, name="raw_sc", offset=4 * KIB)
         wt_used = PASSES * R // 2
         sc_used = PASSES * R // 4
@@ -97,7 +97,7 @@ def tile_list_msg_silu_none_kernel(
 
         def hidden_layer(chunk, place):
             grouped = turns.tile([P, CHUNK, PACK], BF16, name="grouped%d" % chunk, align_bytes=64, offset=place)
-            hidden = turns.tile([P, PACK, CHUNK], BF16, name="hidden%d" % chunk, offset=(32 + 4 * chunk) * KIB)
+            hidden = turns.tile([P, PACK, CHUNK], BF16, name="hidden%d" % chunk, offset=(40 + 4 * chunk) * KIB)
             for t in range(PACK):
                 m = slice(t * P, (t + 1) * P)
                 acc = psum.tile([P, CHUNK], F32, name="acc", bufs=4)
@@ -155,7 +155,7 @@ def tile_list_msg_silu_none_kernel(
             base = min(first, 2)
             if base not in y_second:
                 width = CHUNK * (2 if base == 2 else 1)
-                y_second[base] = turns.tile([P, 2, width], F32, name="y_second%d" % base, offset=(32 + 4 * (base + 1)) * KIB)
+                y_second[base] = turns.tile([P, 2, width], F32, name="y_second%d" % base, offset=(40 + 4 * (base + 1)) * KIB)
             return y_second[base][:, :, (first - base) * CHUNK : (last - base) * CHUNK]
 
         def scatter(n_tile, first, last):
@@ -172,7 +172,7 @@ def tile_list_msg_silu_none_kernel(
             raw_wt[:, 0:wt_used].bitcast(U16).rearrange("p (a m t) -> p a t m", a=PASSES, t=PACK),
         )
         windows = [window0]
-        for n_tile in range(1, N_TILES):
+        for n_tile in range(1, N_TILES - 1):
             window = shared.tile([P, T], F32, name="window%d" % n_tile, offset=(n_tile - 1) * WINDOW_BYTES)
             nc.gpsimd.memset(window[:], 0.0)
             windows.append(window)
@@ -195,6 +195,9 @@ def tile_list_msg_silu_none_kernel(
         wd_c = turns.tile([P, N], I32, name="wd_c", offset=late + 64 + N, align_bytes=64)
         wgo_sb = turns.tile([P, J], F32, name="wgo_sb", offset=late + 64 + 5 * N)
         nc.gpsimd.memset(wd_sc[:], 0)
+        window3 = turns.tile([P, T], F32, name="window3", offset=21 * KIB - 64)
+        nc.gpsimd.memset(window3[:], 0.0)
+        windows.append(window3)
         nc.sync.dma_start(sm_sb[:], sm.rearrange("(p t) -> p t", t=PACK))
         nc.sync.dma_start(wd_c[:], wd_words[0].rearrange("p n i -> p (n i)").bitcast(I32))
         for q in range(QUADS):
@@ -203,11 +206,11 @@ def tile_list_msg_silu_none_kernel(
 
         for step in range(PASSES, CHUNKS * PASSES - 1):
             gather_words(step // PASSES, step % PASSES, 2 * step * KIB)
-        hidden_layer(0, 22 * KIB)
-        gather_words(CHUNKS - 1, PASSES - 1, 22 * KIB)
+        hidden_layer(0, 30 * KIB)
+        gather_words(CHUNKS - 1, PASSES - 1, 30 * KIB)
         evacuate(0, 0)
         for chunk in range(1, CHUNKS):
-            hidden_layer(chunk, (22 + 2 * chunk) * KIB)
+            hidden_layer(chunk, (30 + 2 * chunk) * KIB)
             evacuate(chunk - 1, 1)
             evacuate(chunk, 0)
         evacuate(CHUNKS - 1, 1)

@@ -29,6 +29,9 @@ N_TILES = N // P
 WINDOW_BYTES = 4 * T
 SRC, DST = 0, 1
 KIB = 1024
+SCATTERS = ((0, 0, 1), (1, 0, 1), (2, 0, 1), (3, 0, 2), (0, 1, 2), (1, 1, 3), (2, 1, 3), (0, 2, 4), (1, 3, 4), (2, 3, 4), (3, 2, 4))
+EARLY = ((0, 1, 3), (3, 1), (1, 0, 3), (0, 1, 2, 3))
+HELD = {1: ((0, 2),), 2: ((1, 0),), 3: ((1, 2), (2, 2))}
 
 
 def tile_list_msg_silu_none_kernel(
@@ -56,7 +59,6 @@ def tile_list_msg_silu_none_kernel(
         wt_c = keep.tile([P, PASSES, R], U16, name="wt_c", align_bytes=64)
         w_sc = keep.tile([P, PASSES, R], U8, name="w_sc", align_bytes=64)
         dst_sc1 = keep.tile([P, J // 4], I32, name="dst_sc1", align_bytes=64)
-        y_first = keep.tile([P, 2, J], F32, name="y_first")
         window0 = keep.tile([P, T], F32, name="window0")
 
         nc.vector.memset(tab_sc[:], 0)
@@ -78,22 +80,26 @@ def tile_list_msg_silu_none_kernel(
         for q in range(QUADS):
             nc.sync.dma_start(tab_sc[32 * q : 32 * q + 8, :], tab_scales[:, 4 * q : 4 * q + 4, :].bitcast(I32))
         nc.sync.dma_start(src_list[:], offs)
+        for piece in range(0, 3):
+            load_weight_scales(piece, nc.sync)
         nc.sync.dma_start(tab_w[0][:], tab_words[0].rearrange("p t i -> p (t i)").bitcast(I32))
         nc.sync.dma_start(raw_ws[:], ws_words.rearrange("a p r i -> p a (r i)").bitcast(I32))
         nc.sync.dma_start(tab_w[1][:], tab_words[1].rearrange("p t i -> p (t i)").bitcast(I32))
-        for piece in range(2 * QUADS):
+        for piece in range(3, 2 * QUADS):
             load_weight_scales(piece, nc.sync if piece < 6 else nc.gpsimd)
 
         picked_sc = keep.tile([P, 2, J], U8, name="picked_sc", align_bytes=64)
         picked_w = {}
         products = {}
 
-        def gather_words(chunk, a, place):
-            entries = slice(chunk * CHUNK // 16, (chunk + 1) * CHUNK // 16)
-            picked = turns.tile([P, 2, CHUNK], U32, name="picked_w%d_%d" % (chunk, a), align_bytes=64, offset=place)
+        def gather_words(first, last, a, place):
+            width = (last - first) * CHUNK
+            entries = slice(first * CHUNK // 16, last * CHUNK // 16)
+            picked = turns.tile([P, 2, width], U32, name="picked_w%d_%d" % (first, a), align_bytes=64, offset=place)
             for side in (SRC, DST):
                 nc.vector.tensor_copy(picked[:, side, :], tab_w[a][:].bitcast(U32).indirect(lists[side][:, entries]))
-            picked_w[chunk, a] = picked
+            for chunk in range(first, last):
+                picked_w[chunk, a] = picked[:, :, (chunk - first) * CHUNK : (chunk - first + 1) * CHUNK]
 
         def hidden_layer(chunk, place):
             grouped = turns.tile([P, CHUNK, PACK], BF16, name="grouped%d" % chunk, align_bytes=64, offset=place)
@@ -145,28 +151,28 @@ def tile_list_msg_silu_none_kernel(
                     )
                 products[chunk, pair] = prod
 
-        def evacuate(chunk, pair):
-            target = messages(pair, chunk, chunk + 1)
-            nc.scalar.copy(target, products[chunk, pair][:])
-
-        def messages(pair, first, last):
-            if pair == 0:
-                return y_first[:, :, first * CHUNK : last * CHUNK]
-            base = min(first, 2)
-            if base not in y_second:
-                width = CHUNK * (2 if base == 2 else 1)
-                y_second[base] = turns.tile([P, 2, width], F32, name="y_second%d" % base, offset=(40 + 4 * (base + 1)) * KIB)
-            return y_second[base][:, :, (first - base) * CHUNK : (last - base) * CHUNK]
+        def evacuate(chunk, n_tile):
+            first, last = [(lo, hi) for n, lo, hi in SCATTERS if n == n_tile and lo <= chunk < hi][0]
+            if chunk == first:
+                behind = [later for later in HELD if (chunk, n_tile) in HELD[later]]
+                if behind:
+                    y = turns.tile([P, (last - first) * CHUNK], F32, name="y%d_%d" % (n_tile, first), offset=(40 + 4 * behind[0]) * KIB)
+                else:
+                    y = keep.tile([P, (last - first) * CHUNK], F32, name="y%d_%d" % (n_tile, first))
+                messages[n_tile, first] = y
+            cols = slice((chunk - first) * CHUNK, (chunk - first + 1) * CHUNK)
+            nc.scalar.copy(messages[n_tile, first][:, cols], products[chunk, n_tile // 2][:, n_tile % 2, :])
 
         def scatter(n_tile, first, last):
             cols = slice(first * CHUNK, last * CHUNK)
             entries = slice(first * CHUNK // 16, last * CHUNK // 16)
-            source = messages(n_tile // 2, first, last)[:, n_tile % 2, :]
-            nc.vector.tensor_tensor(windows[n_tile][:].indirect(dst_list[:, entries]), source, wgo_sb[:, cols], MULT)
+            nc.vector.tensor_tensor(
+                windows[n_tile][:].indirect(dst_list[:, entries]), messages[n_tile, first][:], wgo_sb[:, cols], MULT
+            )
             if last == CHUNKS:
                 nc.sync.dma_start(out[n_tile * P : (n_tile + 1) * P, :], windows[n_tile][:])
 
-        y_second = {}
+        messages = {}
         nc.vector.tensor_copy(
             wt_c[:].rearrange("p a (t m) -> p a t m", t=PACK),
             raw_wt[:, 0:wt_used].bitcast(U16).rearrange("p (a m t) -> p a t m", a=PASSES, t=PACK),
@@ -179,12 +185,12 @@ def tile_list_msg_silu_none_kernel(
         nc.vector.tensor_copy(picked_sc[:, DST, :], tab_sc[:].bitcast(U8).indirect(dst_list[:]))
         nc.scalar.dma_start(dst_sc1[0:100, :], picked_sc[ROWS : ROWS + 100, DST, :].bitcast(I32))
         nc.vector.tensor_copy(picked_sc[:, SRC, :], tab_sc[:].bitcast(U8).indirect(src_list[:]))
-        gather_words(0, 0, 0)
+        gather_words(0, 1, 0, 0)
         nc.vector.tensor_copy(
             ws_c[:].rearrange("p a (t m) -> p a m t", t=PACK),
             raw_ws[:].rearrange("p a (m t) -> p a m t", t=PACK),
         )
-        gather_words(0, 1, 2 * KIB)
+        gather_words(0, 1, 1, 2 * KIB)
         nc.vector.tensor_copy(
             w_sc[:].rearrange("p a (t m) -> p a t m", t=PACK),
             raw_sc[:, 0:sc_used].bitcast(U8).rearrange("p (a m t) -> p a t m", a=PASSES, t=PACK),
@@ -204,20 +210,21 @@ def tile_list_msg_silu_none_kernel(
             nc.sync.dma_start(wd_sc[32 * q : 32 * q + ROWS, :], wd_scales[0, 4 * q : 4 * q + 4, :].bitcast(I32))
         nc.sync.dma_start(wgo_sb[:], wgo)
 
-        for step in range(PASSES, CHUNKS * PASSES - 1):
-            gather_words(step // PASSES, step % PASSES, 2 * step * KIB)
+        gather_words(1, 2, 0, 4 * KIB)
+        gather_words(1, 2, 1, 6 * KIB)
+        gather_words(2, 4, 0, 8 * KIB)
+        gather_words(2, 3, 1, 12 * KIB)
         hidden_layer(0, 30 * KIB)
-        gather_words(CHUNKS - 1, PASSES - 1, 30 * KIB)
-        evacuate(0, 0)
-        for chunk in range(1, CHUNKS):
-            hidden_layer(chunk, (30 + 2 * chunk) * KIB)
-            evacuate(chunk - 1, 1)
-            evacuate(chunk, 0)
-        evacuate(CHUNKS - 1, 1)
-        for chunk in range(2):
-            for n_tile in range(N_TILES):
-                scatter(n_tile, chunk, chunk + 1)
-        for chunk in range(2, CHUNKS):
-            for n_tile in range(N_TILES - 1):
-                scatter(n_tile, chunk, chunk + 1)
-        scatter(N_TILES - 1, 2, CHUNKS)
+        gather_words(3, 4, 1, 30 * KIB)
+        for chunk in range(CHUNKS):
+            if chunk + 1 < CHUNKS:
+                for n_tile in EARLY[chunk]:
+                    evacuate(chunk, n_tile)
+                hidden_layer(chunk + 1, (32 + 2 * chunk) * KIB)
+                for held, n_tile in HELD[chunk + 1]:
+                    evacuate(held, n_tile)
+            else:
+                for n_tile in EARLY[chunk]:
+                    evacuate(chunk, n_tile)
+        for n_tile, first, last in SCATTERS:
+            scatter(n_tile, first, last)

@@ -1,6 +1,7 @@
 from contextlib import ExitStack
 
 import concourse.mybir as mybir
+from concourse.masks import make_identity
 
 K, R, N, T, J = 1024, 512, 512, 2048, 1024
 FLOPS = 2 * J * (2 * K * R + R * N)
@@ -24,14 +25,11 @@ QUADS = 4
 ROWS = 4
 UNIT = 128
 CHUNK = 256
+UNITS = CHUNK // UNIT
 CHUNKS = J // CHUNK
 N_TILES = N // P
-WINDOW_BYTES = 4 * T
 SRC, DST = 0, 1
-KIB = 1024
-SCATTERS = ((0, 0, 1), (1, 0, 1), (2, 0, 1), (3, 0, 2), (0, 1, 2), (1, 1, 3), (2, 1, 3), (0, 2, 4), (1, 3, 4), (2, 3, 4), (3, 2, 4))
-EARLY = ((0, 1, 3), (3, 1), (1, 0, 3), (0, 1, 2, 3))
-HELD = {1: ((0, 2),), 2: ((1, 0),), 3: ((1, 2), (2, 2))}
+AHEAD = (3, 2, 1)
 
 
 def tile_list_msg_silu_none_kernel(
@@ -40,191 +38,175 @@ def tile_list_msg_silu_none_kernel(
     nc = tc.nc
     with ExitStack() as ctx:
         keep = ctx.enter_context(tc.tile_pool(name="keep", bufs=1))
-        shared = ctx.enter_context(tc.tile_pool(name="shared", bufs=1))
-        turns = ctx.enter_context(tc.tile_pool(name="turns", bufs=1))
+        late = ctx.enter_context(tc.tile_pool(name="late", bufs=1))
         work = ctx.enter_context(tc.tile_pool(name="work", bufs=2))
         psum = ctx.enter_context(tc.psum_pool(name="psum", bufs=1))
 
         src_list = keep.tile([P, J // 16], U16, name="src_list")
         dst_list = keep.tile([P, J // 16], U16, name="dst_list")
         lists = (src_list, dst_list)
-        tab_sc = keep.tile([P, T // 4], I32, name="tab_sc", align_bytes=64)
-        tab_w = [keep.tile([P, T], I32, name="tab_w%d" % a) for a in range(PASSES)]
-        raw_ws = keep.tile([P, PASSES, R], I32, name="raw_ws")
-        raw_wt = shared.tile([P, PASSES * R // 2], I32, name="raw_wt", offset=WINDOW_BYTES - KIB)
-        raw_sc = turns.tile([P, 17 * KIB // 4], I32, name="raw_sc", offset=4 * KIB)
-        wt_used = PASSES * R // 2
-        sc_used = PASSES * R // 4
-        ws_c = keep.tile([P, PASSES, R], I32, name="ws_c", align_bytes=64)
-        wt_c = keep.tile([P, PASSES, R], U16, name="wt_c", align_bytes=64)
-        w_sc = keep.tile([P, PASSES, R], U8, name="w_sc", align_bytes=64)
+        tab_sc = late.tile([P, T // 4], I32, name="tab_sc", align_bytes=64, offset=4 * J - 64)
+        tab_w = keep.tile([P, PASSES, T], I32, name="tab_w")
+        ws_w = keep.tile([P, PASSES, R], I32, name="ws_w", align_bytes=64)
+        wt_w = keep.tile([P, PASSES, R // 2], I32, name="wt_w", align_bytes=64)
+        w_sc = keep.tile([P, PASSES, R // 4], I32, name="w_sc", align_bytes=64)
         dst_sc1 = keep.tile([P, J // 4], I32, name="dst_sc1", align_bytes=64)
-        window0 = keep.tile([P, T], F32, name="window0")
+        ident = keep.tile([P, P], F32, name="ident")
+        warm = keep.tile([P, 1], F32, name="warm")
+        windows = [keep.tile([P, T], F32, name="window%d" % n) for n in range(N_TILES)]
 
-        nc.vector.memset(tab_sc[:], 0)
-        nc.vector.memset(raw_sc[:, 0:sc_used], 0)
-        nc.vector.memset(window0[:], 0.0)
-        nc.vector.memset(dst_sc1[:], 0)
+        def load_weight_scales(scales, first, queue):
+            for q in range(QUADS):
+                queue.dma_start(
+                    w_sc[32 * q + first : 32 * q + first + ROWS, :, :],
+                    scales[:, 4 * q : 4 * q + 4, :].rearrange("a r n -> r a n").bitcast(I32),
+                )
 
-        def load_weight_scales(piece, queue):
-            q, first, scales = piece // 2, ROWS * (piece % 2), (wt_scales, ws_scales)[piece % 2]
-            queue.dma_start(
-                raw_sc[32 * q + first : 32 * q + first + ROWS, 0:sc_used].rearrange("p (a w) -> p a w", a=PASSES),
-                scales[:, 4 * q : 4 * q + 4, :].rearrange("a r n -> r a n").bitcast(I32),
-            )
+        nc.gpsimd.memset(tab_sc[:], 0)
+        nc.gpsimd.memset(w_sc[:], 0)
+        load_weight_scales(wt_scales, 0, nc.gpsimd)
+        make_identity(nc, ident[:])
+        nc.gpsimd.memset(dst_sc1[:], 0)
+        for n_tile in range(N_TILES):
+            (nc.vector if n_tile < 2 else nc.gpsimd).memset(windows[n_tile][:], 0.0)
+        nc.scalar.activation(warm[:], ident[:, 0:1], SILU)
 
         nc.sync.dma_start(dst_list[:], offs2)
-        nc.sync.dma_start(
-            raw_wt[:, 0:wt_used].rearrange("p (a w) -> p a w", a=PASSES), wt_words.rearrange("a p b -> p a b").bitcast(I32)
-        )
-        for q in range(QUADS):
-            nc.sync.dma_start(tab_sc[32 * q : 32 * q + 8, :], tab_scales[:, 4 * q : 4 * q + 4, :].bitcast(I32))
         nc.sync.dma_start(src_list[:], offs)
-        for piece in range(0, 3):
-            load_weight_scales(piece, nc.sync)
-        nc.sync.dma_start(tab_w[0][:], tab_words[0].rearrange("p t i -> p (t i)").bitcast(I32))
-        nc.sync.dma_start(raw_ws[:], ws_words.rearrange("a p r i -> p a (r i)").bitcast(I32))
-        nc.sync.dma_start(tab_w[1][:], tab_words[1].rearrange("p t i -> p (t i)").bitcast(I32))
-        for piece in range(3, 2 * QUADS):
-            load_weight_scales(piece, nc.sync if piece < 6 else nc.gpsimd)
+        for q in range(QUADS):
+            nc.sync.dma_start(tab_sc[32 * q : 32 * q + PASSES * ROWS, :], tab_scales[:, 4 * q : 4 * q + 4, :].bitcast(I32))
+        nc.sync.dma_start(tab_w[:], tab_words.rearrange("a p t i -> p a (t i)").bitcast(I32))
+        nc.sync.dma_start(ws_w[:], ws_words.rearrange("a p r i -> p a (r i)").bitcast(I32))
+        load_weight_scales(ws_scales, ROWS, nc.sync)
+        nc.sync.dma_start(wt_w[:], wt_words.rearrange("a p b -> p a b").bitcast(I32))
 
         picked_sc = keep.tile([P, 2, J], U8, name="picked_sc", align_bytes=64)
+        nc.vector.tensor_copy(picked_sc[:, DST, :], tab_sc[:].bitcast(U8).indirect(dst_list[:]))
+        nc.scalar.dma_start(dst_sc1[0:100, :], picked_sc[ROWS : ROWS + 100, DST, :].bitcast(I32))
+        nc.vector.tensor_copy(picked_sc[:, SRC, :], tab_sc[:].bitcast(U8).indirect(src_list[:]))
+
+        wgo_sb = late.tile([P, J], F32, name="wgo_sb", offset=0)
+        sm_sb = late.tile([P, PACK], F32, name="sm_sb", offset=4 * J)
+        wd_sc = late.tile([P, N // 4], I32, name="wd_sc", offset=4 * J + 64, align_bytes=64)
+        wd_w = late.tile([P, N], I32, name="wd_w", offset=4 * J + 64 + N, align_bytes=64)
+        nc.vector.memset(wd_sc[:], 0)
+        nc.sync.dma_start(sm_sb[:], sm.rearrange("(p t) -> p t", t=PACK))
+        nc.sync.dma_start(wd_w[:], wd_words[0].rearrange("p n i -> p (n i)").bitcast(I32))
+        for q in range(QUADS):
+            nc.sync.dma_start(wd_sc[32 * q : 32 * q + ROWS, :], wd_scales[0, 4 * q : 4 * q + 4, :].bitcast(I32))
+        nc.sync.dma_start(wgo_sb[:], wgo)
+
         picked_w = {}
         products = {}
+        messages = {}
 
-        def gather_words(first, last, a, place):
+        def gather_words(first, last, a, tag):
             width = (last - first) * CHUNK
             entries = slice(first * CHUNK // 16, last * CHUNK // 16)
-            picked = turns.tile([P, 2, width], U32, name="picked_w%d_%d" % (first, a), align_bytes=64, offset=place)
+            picked = keep.tile([P, 2, width], U32, name="picked_w%d_%d" % (first, a), tag=tag, align_bytes=64)
             for side in (SRC, DST):
-                nc.vector.tensor_copy(picked[:, side, :], tab_w[a][:].bitcast(U32).indirect(lists[side][:, entries]))
+                nc.vector.tensor_copy(picked[:, side, :], tab_w[:, a, :].bitcast(U32).indirect(lists[side][:, entries]))
             for chunk in range(first, last):
                 picked_w[chunk, a] = picked[:, :, (chunk - first) * CHUNK : (chunk - first + 1) * CHUNK]
 
-        def hidden_layer(chunk, place):
-            grouped = turns.tile([P, CHUNK, PACK], BF16, name="grouped%d" % chunk, align_bytes=64, offset=place)
-            hidden = turns.tile([P, PACK, CHUNK], BF16, name="hidden%d" % chunk, offset=(40 + 4 * chunk) * KIB)
-            for t in range(PACK):
-                m = slice(t * P, (t + 1) * P)
-                acc = psum.tile([P, CHUNK], F32, name="acc", bufs=4)
-                for u in range(CHUNK // UNIT):
-                    cols = slice(u * UNIT, (u + 1) * UNIT)
-                    edges = slice(chunk * CHUNK + u * UNIT, chunk * CHUNK + (u + 1) * UNIT)
-                    for a in range(PASSES):
-                        nc.tensor.matmul_mx(
-                            acc[:, cols],
-                            lhsT=ws_c[:, a, m].bitcast(FP8X4),
-                            lhsT_scale=w_sc[ROWS:P, a, m],
-                            rhs=picked_w[chunk, a][:, SRC, cols].bitcast(FP8X4),
-                            rhs_scale=picked_sc[ROWS * a : P, SRC, edges],
-                            start=(a == 0),
-                            stop=False,
-                        )
-                        nc.tensor.matmul_mx(
-                            acc[:, cols],
-                            lhsT=wt_c[:, a, m].bitcast(FP4X4),
-                            lhsT_scale=w_sc[:, a, m],
-                            rhs=picked_w[chunk, a][:, DST, cols].bitcast(FP8X4),
-                            rhs_scale=(picked_sc[:, DST, edges], dst_sc1[:].bitcast(U8)[:, edges])[a],
-                            start=False,
-                            stop=(a == PASSES - 1),
-                        )
-                act = work.tile([P, CHUNK], F32, name="act")
-                nc.scalar.activation(act[:], acc[:], SILU)
-                nc.scalar.activation(hidden[:, t, :], act[:], COPY, scale=sm_sb[:, t : t + 1])
-            nc.scalar.copy(grouped[:], hidden[:].rearrange("p t n -> p n t"))
-            h_c = work.tile([P, CHUNK], U32, name="h_c", align_bytes=64)
+        def first_layer(chunk):
+            act = work.tile([P, UNITS, PACK, P], F32, name="act")
+            accs = [psum.tile([P, R], F32, name="acc", tag="bank%d" % ((2 * chunk + u) % 4)) for u in range(UNITS)]
+            steps = [(u, a, side) for u in range(UNITS) for a in range(PASSES) for side in (SRC, DST)]
+            if chunk == 0:
+                steps = sorted(steps, key=lambda step: step[1:])
+            for u, a, side in steps:
+                cols = slice(u * UNIT, (u + 1) * UNIT)
+                edges = slice(chunk * CHUNK + u * UNIT, chunk * CHUNK + (u + 1) * UNIT)
+                if side == SRC:
+                    edge_sc = picked_sc[ROWS * a : P, SRC, edges]
+                    weight, weight_sc = ws_w[:, a, :].bitcast(FP8X4), w_sc[ROWS:P, a, :]
+                else:
+                    edge_sc = (picked_sc[:, DST, edges], dst_sc1[:].bitcast(U8)[:, edges])[a]
+                    weight, weight_sc = wt_w[:, a, :].bitcast(FP4X4), w_sc[:, a, :]
+                nc.tensor.matmul_mx(
+                    accs[u][:],
+                    lhsT=picked_w[chunk, a][:, side, cols].bitcast(FP8X4),
+                    lhsT_scale=edge_sc,
+                    rhs=weight,
+                    rhs_scale=weight_sc.bitcast(U8),
+                    start=(a, side) == (0, SRC),
+                    stop=(a, side) == (PASSES - 1, DST),
+                )
+            for u in range(UNITS):
+                nc.scalar.activation(act[:, u, :, :], accs[u][:].rearrange("e (m t) -> e t m", t=PACK), SILU)
+            return act
+
+        def second_layer(chunk, act):
+            hidden = keep.tile([P, PACK, CHUNK], BF16, name="hidden", tag="hidden%d" % chunk)
+            for half in range(2):
+                turned = psum.tile([P, 2, CHUNK], F32, name="turned", tag="bank%d" % ((2 * chunk + 2 + half) % 4))
+                for u in range(UNITS):
+                    for i in range(2):
+                        nc.tensor.transpose(turned[:, i, u * UNIT : (u + 1) * UNIT], act[:, u, 2 * half + i, :], ident[:])
+                for i in range(2):
+                    t = 2 * half + i
+                    nc.scalar.activation(hidden[:, t, :], turned[:, i, :], COPY, scale=sm_sb[:, t : t + 1])
+            grouped = keep.tile([P, CHUNK, PACK], BF16, name="grouped", tag="grouped%d" % chunk, align_bytes=64)
+            nc.scalar.copy(
+                grouped[:].rearrange("p (c i) t -> p c t i", i=4), hidden[:].rearrange("p t (c i) -> p c t i", i=4)
+            )
+            h_w = work.tile([P, CHUNK], U32, name="h_w", align_bytes=64)
             h_sc = work.tile([P, CHUNK], U8, name="h_sc", align_bytes=64)
-            nc.vector.quantize_mx(h_c[:].bitcast(FP8X4), h_sc[:], grouped[:].rearrange("p n t -> p (n t)"))
+            nc.vector.quantize_mx(h_w[:].bitcast(FP8X4), h_sc[:], grouped[:].rearrange("p n t -> p (n t)"))
             for pair in range(N_TILES // 2):
-                prod = psum.tile([P, 2, CHUNK], F32, name="prod", bufs=4)
+                prod = psum.tile([P, 2, CHUNK], F32, name="prod", tag="prod%d" % ((2 * chunk + pair) % 4))
                 for i in range(2):
                     m = slice((2 * pair + i) * P, (2 * pair + i + 1) * P)
                     nc.tensor.matmul_mx(
                         prod[:, i, :],
-                        lhsT=wd_c[:, m].bitcast(FP8X4),
+                        lhsT=wd_w[:, m].bitcast(FP8X4),
                         lhsT_scale=wd_sc[:].bitcast(U8)[:, m],
-                        rhs=h_c[:].bitcast(FP8X4),
+                        rhs=h_w[:].bitcast(FP8X4),
                         rhs_scale=h_sc[:],
                         start=True,
                         stop=True,
                     )
                 products[chunk, pair] = prod
 
-        def evacuate(chunk, n_tile):
-            first, last = [(lo, hi) for n, lo, hi in SCATTERS if n == n_tile and lo <= chunk < hi][0]
+        def span(chunk, n_tile):
+            joined = n_tile >= N_TILES // 2 and chunk >= CHUNKS - 2
+            return (CHUNKS - 2, CHUNKS) if joined else (chunk, chunk + 1)
+
+        def evacuate(chunk, n_tile, held=None):
+            first, last = span(chunk, n_tile)
             if chunk == first:
-                behind = [later for later in HELD if (chunk, n_tile) in HELD[later]]
-                if behind:
-                    y = turns.tile([P, (last - first) * CHUNK], F32, name="y%d_%d" % (n_tile, first), offset=(40 + 4 * behind[0]) * KIB)
-                else:
-                    y = keep.tile([P, (last - first) * CHUNK], F32, name="y%d_%d" % (n_tile, first))
-                messages[n_tile, first] = y
+                if held is None:
+                    held = keep.tile([P, (last - first) * CHUNK], F32, name="y%d_%d" % (n_tile, first))[:]
+                messages[n_tile, first] = held
             cols = slice((chunk - first) * CHUNK, (chunk - first + 1) * CHUNK)
             nc.scalar.copy(messages[n_tile, first][:, cols], products[chunk, n_tile // 2][:, n_tile % 2, :])
+            if chunk == last - 1:
+                entries = slice(first * CHUNK // 16, last * CHUNK // 16)
+                nc.vector.tensor_tensor(
+                    windows[n_tile][:].indirect(dst_list[:, entries]),
+                    messages[n_tile, first],
+                    wgo_sb[:, first * CHUNK : last * CHUNK],
+                    MULT,
+                )
+                if last == CHUNKS:
+                    nc.sync.dma_start(out[n_tile * P : (n_tile + 1) * P, :], windows[n_tile][:])
 
-        def scatter(n_tile, first, last):
-            cols = slice(first * CHUNK, last * CHUNK)
-            entries = slice(first * CHUNK // 16, last * CHUNK // 16)
-            nc.vector.tensor_tensor(
-                windows[n_tile][:].indirect(dst_list[:, entries]), messages[n_tile, first][:], wgo_sb[:, cols], MULT
-            )
-            if last == CHUNKS:
-                nc.sync.dma_start(out[n_tile * P : (n_tile + 1) * P, :], windows[n_tile][:])
-
-        messages = {}
-        nc.vector.tensor_copy(
-            wt_c[:].rearrange("p a (t m) -> p a t m", t=PACK),
-            raw_wt[:, 0:wt_used].bitcast(U16).rearrange("p (a m t) -> p a t m", a=PASSES, t=PACK),
-        )
-        windows = [window0]
-        for n_tile in range(1, N_TILES - 1):
-            window = shared.tile([P, T], F32, name="window%d" % n_tile, offset=(n_tile - 1) * WINDOW_BYTES)
-            nc.gpsimd.memset(window[:], 0.0)
-            windows.append(window)
-        nc.vector.tensor_copy(picked_sc[:, DST, :], tab_sc[:].bitcast(U8).indirect(dst_list[:]))
-        nc.scalar.dma_start(dst_sc1[0:100, :], picked_sc[ROWS : ROWS + 100, DST, :].bitcast(I32))
-        nc.vector.tensor_copy(picked_sc[:, SRC, :], tab_sc[:].bitcast(U8).indirect(src_list[:]))
-        gather_words(0, 1, 0, 0)
-        nc.vector.tensor_copy(
-            ws_c[:].rearrange("p a (t m) -> p a m t", t=PACK),
-            raw_ws[:].rearrange("p a (m t) -> p a m t", t=PACK),
-        )
-        gather_words(0, 1, 1, 2 * KIB)
-        nc.vector.tensor_copy(
-            w_sc[:].rearrange("p a (t m) -> p a t m", t=PACK),
-            raw_sc[:, 0:sc_used].bitcast(U8).rearrange("p (a m t) -> p a t m", a=PASSES, t=PACK),
-        )
-        late = 14 * KIB
-        sm_sb = turns.tile([P, PACK], F32, name="sm_sb", offset=late)
-        wd_sc = turns.tile([P, N // 4], I32, name="wd_sc", offset=late + 64, align_bytes=64)
-        wd_c = turns.tile([P, N], I32, name="wd_c", offset=late + 64 + N, align_bytes=64)
-        wgo_sb = turns.tile([P, J], F32, name="wgo_sb", offset=late + 64 + 5 * N)
-        nc.gpsimd.memset(wd_sc[:], 0)
-        window3 = turns.tile([P, T], F32, name="window3", offset=21 * KIB - 64)
-        nc.gpsimd.memset(window3[:], 0.0)
-        windows.append(window3)
-        nc.sync.dma_start(sm_sb[:], sm.rearrange("(p t) -> p t", t=PACK))
-        nc.sync.dma_start(wd_c[:], wd_words[0].rearrange("p n i -> p (n i)").bitcast(I32))
-        for q in range(QUADS):
-            nc.sync.dma_start(wd_sc[32 * q : 32 * q + ROWS, :], wd_scales[0, 4 * q : 4 * q + 4, :].bitcast(I32))
-        nc.sync.dma_start(wgo_sb[:], wgo)
-
-        gather_words(1, 2, 0, 4 * KIB)
-        gather_words(1, 2, 1, 6 * KIB)
-        gather_words(2, 4, 0, 8 * KIB)
-        gather_words(2, 3, 1, 12 * KIB)
-        hidden_layer(0, 30 * KIB)
-        gather_words(3, 4, 1, 30 * KIB)
-        for chunk in range(CHUNKS):
-            if chunk + 1 < CHUNKS:
-                for n_tile in EARLY[chunk]:
-                    evacuate(chunk, n_tile)
-                hidden_layer(chunk + 1, (32 + 2 * chunk) * KIB)
-                for held, n_tile in HELD[chunk + 1]:
-                    evacuate(held, n_tile)
-            else:
-                for n_tile in EARLY[chunk]:
-                    evacuate(chunk, n_tile)
-        for n_tile, first, last in SCATTERS:
-            scatter(n_tile, first, last)
+        for chunk in range(2):
+            for a in range(PASSES):
+                gather_words(chunk, chunk + 1, a, "words%d_%d" % (chunk, a))
+        gather_words(2, 4, 0, "words2_0")
+        gather_words(2, 3, 1, "words2_1")
+        second_layer(0, first_layer(0))
+        gather_words(3, 4, 1, "grouped0")
+        for chunk in range(1, CHUNKS):
+            act = first_layer(chunk)
+            for n_tile in range(AHEAD[chunk - 1]):
+                evacuate(chunk - 1, n_tile)
+            second_layer(chunk, act)
+            held = keep.tile([P, 2, CHUNK], F32, name="held", tag="hidden%d" % chunk)
+            for i, n_tile in enumerate(range(AHEAD[chunk - 1], N_TILES)):
+                single = span(chunk - 1, n_tile) == (chunk - 1, chunk)
+                evacuate(chunk - 1, n_tile, held[:, i, :] if single else None)
+        for n_tile in range(N_TILES):
+            evacuate(CHUNKS - 1, n_tile)

@@ -39,6 +39,7 @@ def tile_list_msg_silu_none_kernel(
     with ExitStack() as ctx:
         keep = ctx.enter_context(tc.tile_pool(name="keep", bufs=1))
         late = ctx.enter_context(tc.tile_pool(name="late", bufs=1))
+        reuse = ctx.enter_context(tc.tile_pool(name="reuse", bufs=1))
         work = ctx.enter_context(tc.tile_pool(name="work", bufs=2))
         psum = ctx.enter_context(tc.psum_pool(name="psum", bufs=1))
 
@@ -46,44 +47,71 @@ def tile_list_msg_silu_none_kernel(
         dst_list = keep.tile([P, J // 16], U16, name="dst_list")
         lists = (src_list, dst_list)
         tab_sc = late.tile([P, T // 4], I32, name="tab_sc", align_bytes=64, offset=4 * J - 64)
-        tab_w = keep.tile([P, PASSES, T], I32, name="tab_w")
+        tab_w = reuse.tile([P, PASSES * T], I32, name="tab_w", offset=0)
         ws_w = keep.tile([P, PASSES, R], I32, name="ws_w", align_bytes=64)
         wt_w = keep.tile([P, PASSES, R // 2], I32, name="wt_w", align_bytes=64)
-        w_sc = keep.tile([P, PASSES, R // 4], I32, name="w_sc", align_bytes=64)
+        ws_sc = keep.tile([P, PASSES, R // 4], I32, name="ws_sc", align_bytes=64)
+        wt_sc = keep.tile([P, PASSES, R // 4], I32, name="wt_sc", align_bytes=64)
         dst_sc1 = keep.tile([P, J // 4], I32, name="dst_sc1", align_bytes=64)
         ident = keep.tile([P, P], F32, name="ident")
         warm = keep.tile([P, 1], F32, name="warm")
-        windows = [keep.tile([P, T], F32, name="window%d" % n) for n in range(N_TILES)]
+        windows = [keep.tile([P, T], F32, name="window%d" % n) for n in range(2)]
 
-        def load_weight_scales(scales, first, queue):
-            for q in range(QUADS):
+        def load_weight_scales(tile, scales, queue, quads=range(QUADS)):
+            for q in quads:
                 queue.dma_start(
-                    w_sc[32 * q + first : 32 * q + first + ROWS, :, :],
+                    tile[32 * q : 32 * q + ROWS, :, :],
                     scales[:, 4 * q : 4 * q + 4, :].rearrange("a r n -> r a n").bitcast(I32),
                 )
 
         nc.gpsimd.memset(tab_sc[:], 0)
-        nc.gpsimd.memset(w_sc[:], 0)
-        load_weight_scales(wt_scales, 0, nc.gpsimd)
+        nc.vector.memset(wt_sc[:], 0)
+        nc.gpsimd.memset(ws_sc[:], 0)
+        load_weight_scales(ws_sc, ws_scales, nc.gpsimd)
         make_identity(nc, ident[:])
         nc.gpsimd.memset(dst_sc1[:], 0)
-        for n_tile in range(N_TILES):
+        for n_tile in range(2):
             (nc.vector if n_tile < 2 else nc.gpsimd).memset(windows[n_tile][:], 0.0)
         nc.scalar.activation(warm[:], ident[:, 0:1], SILU)
 
+        def load_table(a):
+            nc.sync.dma_start(tab_w[:, a * T : (a + 1) * T], tab_words[a].rearrange("p t i -> p (t i)").bitcast(I32))
+
         nc.sync.dma_start(dst_list[:], offs2)
-        nc.sync.dma_start(src_list[:], offs)
         for q in range(QUADS):
             nc.sync.dma_start(tab_sc[32 * q : 32 * q + PASSES * ROWS, :], tab_scales[:, 4 * q : 4 * q + 4, :].bitcast(I32))
-        nc.sync.dma_start(tab_w[:], tab_words.rearrange("a p t i -> p a (t i)").bitcast(I32))
-        nc.sync.dma_start(ws_w[:], ws_words.rearrange("a p r i -> p a (r i)").bitcast(I32))
-        load_weight_scales(ws_scales, ROWS, nc.sync)
+        load_weight_scales(wt_sc, wt_scales, nc.sync, range(1))
+        load_table(0)
+        nc.sync.dma_start(src_list[:], offs)
         nc.sync.dma_start(wt_w[:], wt_words.rearrange("a p b -> p a b").bitcast(I32))
+        nc.sync.dma_start(ws_w[:], ws_words.rearrange("a p r i -> p a (r i)").bitcast(I32))
+        load_weight_scales(wt_sc, wt_scales, nc.sync, range(1, QUADS))
+        load_table(1)
 
         picked_sc = keep.tile([P, 2, J], U8, name="picked_sc", align_bytes=64)
-        nc.vector.tensor_copy(picked_sc[:, DST, :], tab_sc[:].bitcast(U8).indirect(dst_list[:]))
+        picked_w = {}
+
+        def gather_scales(side, first, last):
+            nc.vector.tensor_copy(
+                picked_sc[:, side, first:last], tab_sc[:].bitcast(U8).indirect(lists[side][:, first // 16 : last // 16])
+            )
+
+        def gather_words(first, last, a, sides, spare=0, tag=""):
+            picked = keep.tile(
+                [P, len(sides), last - first], U32, name="picked_w%d_%d_%d" % (first, a, sides[0]), tag=tag, align_bytes=64
+            )
+            window = tab_w[:, a * T : (a + 1) * T + spare].bitcast(U32)
+            for i, side in enumerate(sides):
+                nc.vector.tensor_copy(picked[:, i, :], window.indirect(lists[side][:, first // 16 : last // 16]))
+                for unit in range(first // UNIT, last // UNIT):
+                    picked_w[unit, a, side] = picked[:, i, unit * UNIT - first : (unit + 1) * UNIT - first]
+
+        gather_scales(DST, 0, J)
         nc.scalar.dma_start(dst_sc1[0:100, :], picked_sc[ROWS : ROWS + 100, DST, :].bitcast(I32))
-        nc.vector.tensor_copy(picked_sc[:, SRC, :], tab_sc[:].bitcast(U8).indirect(src_list[:]))
+        gather_words(0, CHUNK, 0, (DST,))
+        gather_scales(SRC, 0, CHUNK)
+        gather_words(0, CHUNK, 0, (SRC,))
+        gather_scales(SRC, CHUNK, J)
 
         wgo_sb = late.tile([P, J], F32, name="wgo_sb", offset=0)
         sm_sb = late.tile([P, PACK], F32, name="sm_sb", offset=4 * J)
@@ -96,42 +124,31 @@ def tile_list_msg_silu_none_kernel(
             nc.sync.dma_start(wd_sc[32 * q : 32 * q + ROWS, :], wd_scales[0, 4 * q : 4 * q + 4, :].bitcast(I32))
         nc.sync.dma_start(wgo_sb[:], wgo)
 
-        picked_w = {}
         products = {}
         messages = {}
 
-        def gather_words(first, last, a, tag):
-            width = (last - first) * CHUNK
-            entries = slice(first * CHUNK // 16, last * CHUNK // 16)
-            picked = keep.tile([P, 2, width], U32, name="picked_w%d_%d" % (first, a), tag=tag, align_bytes=64)
-            for side in (SRC, DST):
-                nc.vector.tensor_copy(picked[:, side, :], tab_w[:, a, :].bitcast(U32).indirect(lists[side][:, entries]))
-            for chunk in range(first, last):
-                picked_w[chunk, a] = picked[:, :, (chunk - first) * CHUNK : (chunk - first + 1) * CHUNK]
-
         def first_layer(chunk):
             act = work.tile([P, UNITS, PACK, P], F32, name="act")
-            accs = [psum.tile([P, R], F32, name="acc", tag="bank%d" % ((2 * chunk + u) % 4)) for u in range(UNITS)]
-            steps = [(u, a, side) for u in range(UNITS) for a in range(PASSES) for side in (SRC, DST)]
+            accs = [psum.tile([P, R], F32, name="acc", tag="acc%d" % u) for u in range(UNITS)]
+            steps = [(u, a, side) for u in range(UNITS) for a in range(PASSES) for side in (DST, SRC)]
             if chunk == 0:
-                steps = sorted(steps, key=lambda step: step[1:])
+                steps = sorted(steps, key=lambda step: (step[1], -step[2]))
             for u, a, side in steps:
-                cols = slice(u * UNIT, (u + 1) * UNIT)
                 edges = slice(chunk * CHUNK + u * UNIT, chunk * CHUNK + (u + 1) * UNIT)
                 if side == SRC:
                     edge_sc = picked_sc[ROWS * a : P, SRC, edges]
-                    weight, weight_sc = ws_w[:, a, :].bitcast(FP8X4), w_sc[ROWS:P, a, :]
+                    weight, weight_sc = ws_w[:, a, :].bitcast(FP8X4), ws_sc[:, a, :]
                 else:
                     edge_sc = (picked_sc[:, DST, edges], dst_sc1[:].bitcast(U8)[:, edges])[a]
-                    weight, weight_sc = wt_w[:, a, :].bitcast(FP4X4), w_sc[:, a, :]
+                    weight, weight_sc = wt_w[:, a, :].bitcast(FP4X4), wt_sc[:, a, :]
                 nc.tensor.matmul_mx(
                     accs[u][:],
-                    lhsT=picked_w[chunk, a][:, side, cols].bitcast(FP8X4),
+                    lhsT=picked_w[chunk * UNITS + u, a, side].bitcast(FP8X4),
                     lhsT_scale=edge_sc,
                     rhs=weight,
                     rhs_scale=weight_sc.bitcast(U8),
-                    start=(a, side) == (0, SRC),
-                    stop=(a, side) == (PASSES - 1, DST),
+                    start=(a, side) == (0, DST),
+                    stop=(a, side) == (PASSES - 1, SRC),
                 )
             for u in range(UNITS):
                 nc.scalar.activation(act[:, u, :, :], accs[u][:].rearrange("e (m t) -> e t m", t=PACK), SILU)
@@ -140,7 +157,7 @@ def tile_list_msg_silu_none_kernel(
         def second_layer(chunk, act):
             hidden = keep.tile([P, PACK, CHUNK], BF16, name="hidden", tag="hidden%d" % chunk)
             for half in range(2):
-                turned = psum.tile([P, 2, CHUNK], F32, name="turned", tag="bank%d" % ((2 * chunk + 2 + half) % 4))
+                turned = psum.tile([P, 2, CHUNK], F32, name="turned", tag="turned%d" % half)
                 for u in range(UNITS):
                     for i in range(2):
                         nc.tensor.transpose(turned[:, i, u * UNIT : (u + 1) * UNIT], act[:, u, 2 * half + i, :], ident[:])
@@ -192,13 +209,18 @@ def tile_list_msg_silu_none_kernel(
                 if last == CHUNKS:
                     nc.sync.dma_start(out[n_tile * P : (n_tile + 1) * P, :], windows[n_tile][:])
 
-        for chunk in range(2):
-            for a in range(PASSES):
-                gather_words(chunk, chunk + 1, a, "words%d_%d" % (chunk, a))
-        gather_words(2, 4, 0, "words2_0")
-        gather_words(2, 3, 1, "words2_1")
+        both = (DST, SRC)
+        gather_words(0, CHUNK, 1, both)
+        gather_words(CHUNK, 5 * UNIT, 0, both, spare=8)
+        gather_words(CHUNK, 2 * CHUNK, 1, both)
+        gather_words(5 * UNIT, J, 0, both, spare=8)
+        gather_words(2 * CHUNK, 3 * CHUNK, 1, both)
         second_layer(0, first_layer(0))
-        gather_words(3, 4, 1, "grouped0")
+        gather_words(3 * CHUNK, J, 1, both, tag="grouped0")
+        for i in range(2):
+            window = reuse.tile([P, T], F32, name="window%d" % (2 + i), offset=4 * T * i)
+            nc.gpsimd.memset(window[:], 0.0)
+            windows.append(window)
         for chunk in range(1, CHUNKS):
             act = first_layer(chunk)
             for n_tile in range(AHEAD[chunk - 1]):

@@ -29,7 +29,12 @@ UNITS = CHUNK // UNIT
 CHUNKS = J // CHUNK
 N_TILES = N // P
 SRC, DST = 0, 1
-AHEAD = (3, 2, 1)
+ACC_BANKS = "aaaa"
+TURN_BANKS = "dddd"
+PROD_BANKS = "cbcb"
+STARTS = ((0, 1, 2, 3), (0, 1, 2, 3), (0, 1, 3), (0, 1, 2))
+AHEAD = ((0, 1, 2), (0, 1, 2), (2, 0, 3), (0, 1, 2, 3))
+HELD = (((0, 3),), ((1, 3),), ((2, 1),))
 
 
 def tile_list_msg_silu_none_kernel(
@@ -54,7 +59,6 @@ def tile_list_msg_silu_none_kernel(
         wt_sc = keep.tile([P, PASSES, R // 4], I32, name="wt_sc", align_bytes=64)
         dst_sc1 = keep.tile([P, J // 4], I32, name="dst_sc1", align_bytes=64)
         ident = keep.tile([P, P], F32, name="ident")
-        warm = keep.tile([P, 1], F32, name="warm")
         windows = [keep.tile([P, T], F32, name="window%d" % n) for n in range(2)]
 
         def load_weight_scales(tile, scales, queue, quads=range(QUADS)):
@@ -69,24 +73,29 @@ def tile_list_msg_silu_none_kernel(
         nc.gpsimd.memset(ws_sc[:], 0)
         load_weight_scales(ws_sc, ws_scales, nc.gpsimd)
         make_identity(nc, ident[:])
-        nc.gpsimd.memset(dst_sc1[:], 0)
+        nc.vector.memset(dst_sc1[:], 0)
         for n_tile in range(2):
-            (nc.vector if n_tile < 2 else nc.gpsimd).memset(windows[n_tile][:], 0.0)
-        nc.scalar.activation(warm[:], ident[:, 0:1], SILU)
+            (nc.vector if n_tile < 0 else nc.gpsimd).memset(windows[n_tile][:], 0.0)
+
+        def load_ws(a):
+            nc.sync.dma_start(ws_w[:, a, :], ws_words[a].rearrange("p r i -> p (r i)").bitcast(I32))
 
         def load_table(a):
             nc.sync.dma_start(tab_w[:, a * T : (a + 1) * T], tab_words[a].rearrange("p t i -> p (t i)").bitcast(I32))
 
+        sm_sb = keep.tile([P, PACK], F32, name="sm_sb")
         nc.sync.dma_start(dst_list[:], offs2)
+        nc.sync.dma_start(sm_sb[:], sm.rearrange("(p t) -> p t", t=PACK))
         for q in range(QUADS):
             nc.sync.dma_start(tab_sc[32 * q : 32 * q + PASSES * ROWS, :], tab_scales[:, 4 * q : 4 * q + 4, :].bitcast(I32))
         load_weight_scales(wt_sc, wt_scales, nc.sync, range(1))
         load_table(0)
         nc.sync.dma_start(src_list[:], offs)
         nc.sync.dma_start(wt_w[:], wt_words.rearrange("a p b -> p a b").bitcast(I32))
-        nc.sync.dma_start(ws_w[:], ws_words.rearrange("a p r i -> p a (r i)").bitcast(I32))
         load_weight_scales(wt_sc, wt_scales, nc.sync, range(1, QUADS))
+        load_ws(0)
         load_table(1)
+        load_ws(1)
 
         picked_sc = keep.tile([P, 2, J], U8, name="picked_sc", align_bytes=64)
         picked_w = {}
@@ -114,11 +123,9 @@ def tile_list_msg_silu_none_kernel(
         gather_scales(SRC, CHUNK, J)
 
         wgo_sb = late.tile([P, J], F32, name="wgo_sb", offset=0)
-        sm_sb = late.tile([P, PACK], F32, name="sm_sb", offset=4 * J)
         wd_sc = late.tile([P, N // 4], I32, name="wd_sc", offset=4 * J + 64, align_bytes=64)
         wd_w = late.tile([P, N], I32, name="wd_w", offset=4 * J + 64 + N, align_bytes=64)
-        nc.vector.memset(wd_sc[:], 0)
-        nc.sync.dma_start(sm_sb[:], sm.rearrange("(p t) -> p t", t=PACK))
+        nc.gpsimd.memset(wd_sc[:], 0)
         nc.sync.dma_start(wd_w[:], wd_words[0].rearrange("p n i -> p (n i)").bitcast(I32))
         for q in range(QUADS):
             nc.sync.dma_start(wd_sc[32 * q : 32 * q + ROWS, :], wd_scales[0, 4 * q : 4 * q + 4, :].bitcast(I32))
@@ -129,7 +136,7 @@ def tile_list_msg_silu_none_kernel(
 
         def first_layer(chunk):
             act = work.tile([P, UNITS, PACK, P], F32, name="act")
-            accs = [psum.tile([P, R], F32, name="acc", tag="acc%d" % u) for u in range(UNITS)]
+            accs = [psum.tile([P, R], F32, name="acc", tag="bank_%s%d" % (ACC_BANKS[chunk], u)) for u in range(UNITS)]
             steps = [(u, a, side) for u in range(UNITS) for a in range(PASSES) for side in (DST, SRC)]
             if chunk == 0:
                 steps = sorted(steps, key=lambda step: (step[1], -step[2]))
@@ -157,7 +164,7 @@ def tile_list_msg_silu_none_kernel(
         def second_layer(chunk, act):
             hidden = keep.tile([P, PACK, CHUNK], BF16, name="hidden", tag="hidden%d" % chunk)
             for half in range(2):
-                turned = psum.tile([P, 2, CHUNK], F32, name="turned", tag="turned%d" % half)
+                turned = psum.tile([P, 2, CHUNK], F32, name="turned", tag="bank_%s%d" % (TURN_BANKS[chunk], half))
                 for u in range(UNITS):
                     for i in range(2):
                         nc.tensor.transpose(turned[:, i, u * UNIT : (u + 1) * UNIT], act[:, u, 2 * half + i, :], ident[:])
@@ -171,8 +178,8 @@ def tile_list_msg_silu_none_kernel(
             h_w = work.tile([P, CHUNK], U32, name="h_w", align_bytes=64)
             h_sc = work.tile([P, CHUNK], U8, name="h_sc", align_bytes=64)
             nc.vector.quantize_mx(h_w[:].bitcast(FP8X4), h_sc[:], grouped[:].rearrange("p n t -> p (n t)"))
-            for pair in range(N_TILES // 2):
-                prod = psum.tile([P, 2, CHUNK], F32, name="prod", tag="prod%d" % ((2 * chunk + pair) % 4))
+            for pair in sorted(range(N_TILES // 2), key=lambda pair: pair != AHEAD[chunk][0] // 2):
+                prod = psum.tile([P, 2, CHUNK], F32, name="prod", tag="bank_%s%d" % (PROD_BANKS[chunk], pair))
                 for i in range(2):
                     m = slice((2 * pair + i) * P, (2 * pair + i + 1) * P)
                     nc.tensor.matmul_mx(
@@ -187,22 +194,20 @@ def tile_list_msg_silu_none_kernel(
                 products[chunk, pair] = prod
 
         def span(chunk, n_tile):
-            joined = n_tile >= N_TILES // 2 and chunk >= CHUNKS - 2
-            return (CHUNKS - 2, CHUNKS) if joined else (chunk, chunk + 1)
+            bounds = STARTS[n_tile] + (CHUNKS,)
+            return max(b for b in bounds if b <= chunk), min(b for b in bounds if b > chunk)
 
-        def evacuate(chunk, n_tile, held=None):
+        def evacuate(chunk, n_tile, tag=""):
             first, last = span(chunk, n_tile)
             if chunk == first:
-                if held is None:
-                    held = keep.tile([P, (last - first) * CHUNK], F32, name="y%d_%d" % (n_tile, first))[:]
-                messages[n_tile, first] = held
+                messages[n_tile, first] = keep.tile([P, (last - first) * CHUNK], F32, name="y%d_%d" % (n_tile, first), tag=tag)
             cols = slice((chunk - first) * CHUNK, (chunk - first + 1) * CHUNK)
             nc.scalar.copy(messages[n_tile, first][:, cols], products[chunk, n_tile // 2][:, n_tile % 2, :])
             if chunk == last - 1:
                 entries = slice(first * CHUNK // 16, last * CHUNK // 16)
                 nc.vector.tensor_tensor(
                     windows[n_tile][:].indirect(dst_list[:, entries]),
-                    messages[n_tile, first],
+                    messages[n_tile, first][:],
                     wgo_sb[:, first * CHUNK : last * CHUNK],
                     MULT,
                 )
@@ -223,12 +228,10 @@ def tile_list_msg_silu_none_kernel(
             windows.append(window)
         for chunk in range(1, CHUNKS):
             act = first_layer(chunk)
-            for n_tile in range(AHEAD[chunk - 1]):
+            for n_tile in AHEAD[chunk - 1]:
                 evacuate(chunk - 1, n_tile)
             second_layer(chunk, act)
-            held = keep.tile([P, 2, CHUNK], F32, name="held", tag="hidden%d" % chunk)
-            for i, n_tile in enumerate(range(AHEAD[chunk - 1], N_TILES)):
-                single = span(chunk - 1, n_tile) == (chunk - 1, chunk)
-                evacuate(chunk - 1, n_tile, held[:, i, :] if single else None)
-        for n_tile in range(N_TILES):
+            for held in HELD[chunk - 1]:
+                evacuate(*held, tag="hidden%d" % chunk)
+        for n_tile in AHEAD[CHUNKS - 1]:
             evacuate(CHUNKS - 1, n_tile)

@@ -29,12 +29,7 @@ UNITS = CHUNK // UNIT
 CHUNKS = J // CHUNK
 N_TILES = N // P
 SRC, DST = 0, 1
-ACC_BANKS = "aaaa"
-TURN_BANKS = "dddd"
-PROD_BANKS = "cbcb"
-STARTS = ((0, 1, 2, 3), (0, 1, 2, 3), (0, 1, 3), (0, 1, 2))
-AHEAD = ((0, 1, 2), (0, 1, 2), (2, 0, 3), (0, 1, 2, 3))
-HELD = (((0, 3),), ((1, 3),), ((2, 1),))
+TURN_BANKS = "dede"
 
 
 def tile_list_msg_silu_none_kernel(
@@ -59,7 +54,7 @@ def tile_list_msg_silu_none_kernel(
         wt_sc = keep.tile([P, PASSES, R // 4], I32, name="wt_sc", align_bytes=64)
         dst_sc1 = keep.tile([P, J // 4], I32, name="dst_sc1", align_bytes=64)
         ident = keep.tile([P, P], F32, name="ident")
-        windows = [keep.tile([P, T], F32, name="window%d" % n) for n in range(2)]
+        windows = [keep.tile([P, T], F32, name="window%d" % n) for n in range(N_TILES)]
 
         def load_weight_scales(tile, scales, queue, quads=range(QUADS)):
             for q in quads:
@@ -72,10 +67,14 @@ def tile_list_msg_silu_none_kernel(
         nc.vector.memset(wt_sc[:], 0)
         nc.gpsimd.memset(ws_sc[:], 0)
         load_weight_scales(ws_sc, ws_scales, nc.gpsimd)
+        sm_sb = keep.tile([P, PACK], F32, name="sm_sb")
+        nc.gpsimd.dma_start(sm_sb[:], sm.rearrange("(p t) -> p t", t=PACK))
         make_identity(nc, ident[:])
         nc.vector.memset(dst_sc1[:], 0)
-        for n_tile in range(2):
-            (nc.vector if n_tile < 0 else nc.gpsimd).memset(windows[n_tile][:], 0.0)
+        wd_sc = keep.tile([P, N // 4], I32, name="wd_sc", align_bytes=64)
+        nc.vector.memset(wd_sc[:], 0)
+        for window in windows:
+            nc.gpsimd.memset(window[:], 0.0)
 
         def load_ws(a):
             nc.sync.dma_start(ws_w[:, a, :], ws_words[a].rearrange("p r i -> p (r i)").bitcast(I32))
@@ -83,14 +82,12 @@ def tile_list_msg_silu_none_kernel(
         def load_table(a):
             nc.sync.dma_start(tab_w[:, a * T : (a + 1) * T], tab_words[a].rearrange("p t i -> p (t i)").bitcast(I32))
 
-        sm_sb = keep.tile([P, PACK], F32, name="sm_sb")
         nc.sync.dma_start(dst_list[:], offs2)
-        nc.sync.dma_start(sm_sb[:], sm.rearrange("(p t) -> p t", t=PACK))
+        nc.sync.dma_start(src_list[:], offs)
         for q in range(QUADS):
             nc.sync.dma_start(tab_sc[32 * q : 32 * q + PASSES * ROWS, :], tab_scales[:, 4 * q : 4 * q + 4, :].bitcast(I32))
         load_weight_scales(wt_sc, wt_scales, nc.sync, range(1))
         load_table(0)
-        nc.sync.dma_start(src_list[:], offs)
         nc.sync.dma_start(wt_w[:], wt_words.rearrange("a p b -> p a b").bitcast(I32))
         load_weight_scales(wt_sc, wt_scales, nc.sync, range(1, QUADS))
         load_ws(0)
@@ -117,26 +114,22 @@ def tile_list_msg_silu_none_kernel(
 
         gather_scales(DST, 0, J)
         nc.scalar.dma_start(dst_sc1[0:100, :], picked_sc[ROWS : ROWS + 100, DST, :].bitcast(I32))
-        gather_words(0, CHUNK, 0, (DST,))
-        gather_scales(SRC, 0, CHUNK)
-        gather_words(0, CHUNK, 0, (SRC,))
-        gather_scales(SRC, CHUNK, J)
+        gather_scales(SRC, 0, J)
+        gather_words(0, CHUNK, 0, (DST, SRC))
 
         wgo_sb = late.tile([P, J], F32, name="wgo_sb", offset=0)
-        wd_sc = late.tile([P, N // 4], I32, name="wd_sc", offset=4 * J + 64, align_bytes=64)
-        wd_w = late.tile([P, N], I32, name="wd_w", offset=4 * J + 64 + N, align_bytes=64)
-        nc.gpsimd.memset(wd_sc[:], 0)
+        wd_w = late.tile([P, N], I32, name="wd_w", offset=4 * J + 64, align_bytes=64)
         nc.sync.dma_start(wd_w[:], wd_words[0].rearrange("p n i -> p (n i)").bitcast(I32))
         for q in range(QUADS):
             nc.sync.dma_start(wd_sc[32 * q : 32 * q + ROWS, :], wd_scales[0, 4 * q : 4 * q + 4, :].bitcast(I32))
         nc.sync.dma_start(wgo_sb[:], wgo)
 
-        products = {}
-        messages = {}
+        h_w = keep.tile([P, J], U32, name="h_w", align_bytes=64)
+        h_sc = keep.tile([P, J], U8, name="h_sc", align_bytes=64)
 
         def first_layer(chunk):
             act = work.tile([P, UNITS, PACK, P], F32, name="act")
-            accs = [psum.tile([P, R], F32, name="acc", tag="bank_%s%d" % (ACC_BANKS[chunk], u)) for u in range(UNITS)]
+            acc = psum.tile([P, UNITS, R], F32, name="acc")
             steps = [(u, a, side) for u in range(UNITS) for a in range(PASSES) for side in (DST, SRC)]
             if chunk == 0:
                 steps = sorted(steps, key=lambda step: (step[1], -step[2]))
@@ -149,7 +142,7 @@ def tile_list_msg_silu_none_kernel(
                     edge_sc = (picked_sc[:, DST, edges], dst_sc1[:].bitcast(U8)[:, edges])[a]
                     weight, weight_sc = wt_w[:, a, :].bitcast(FP4X4), wt_sc[:, a, :]
                 nc.tensor.matmul_mx(
-                    accs[u][:],
+                    acc[:, u, :],
                     lhsT=picked_w[chunk * UNITS + u, a, side].bitcast(FP8X4),
                     lhsT_scale=edge_sc,
                     rhs=weight,
@@ -158,11 +151,11 @@ def tile_list_msg_silu_none_kernel(
                     stop=(a, side) == (PASSES - 1, SRC),
                 )
             for u in range(UNITS):
-                nc.scalar.activation(act[:, u, :, :], accs[u][:].rearrange("e (m t) -> e t m", t=PACK), SILU)
+                nc.scalar.activation(act[:, u, :, :], acc[:, u, :].rearrange("e (m t) -> e t m", t=PACK), SILU)
             return act
 
-        def second_layer(chunk, act):
-            hidden = keep.tile([P, PACK, CHUNK], BF16, name="hidden", tag="hidden%d" % chunk)
+        def scale_hidden(chunk, act):
+            hidden = keep.tile([P, PACK, CHUNK], BF16, name="hidden", tag="hidden%d" % chunk, align_bytes=64)
             for half in range(2):
                 turned = psum.tile([P, 2, CHUNK], F32, name="turned", tag="bank_%s%d" % (TURN_BANKS[chunk], half))
                 for u in range(UNITS):
@@ -171,47 +164,40 @@ def tile_list_msg_silu_none_kernel(
                 for i in range(2):
                     t = 2 * half + i
                     nc.scalar.activation(hidden[:, t, :], turned[:, i, :], COPY, scale=sm_sb[:, t : t + 1])
+            return hidden
+
+        def quantize_hidden(chunk, hidden):
             grouped = keep.tile([P, CHUNK, PACK], BF16, name="grouped", tag="grouped%d" % chunk, align_bytes=64)
             nc.scalar.copy(
                 grouped[:].rearrange("p (c i) t -> p c t i", i=4), hidden[:].rearrange("p t (c i) -> p c t i", i=4)
             )
-            h_w = work.tile([P, CHUNK], U32, name="h_w", align_bytes=64)
-            h_sc = work.tile([P, CHUNK], U8, name="h_sc", align_bytes=64)
-            nc.vector.quantize_mx(h_w[:].bitcast(FP8X4), h_sc[:], grouped[:].rearrange("p n t -> p (n t)"))
-            for pair in sorted(range(N_TILES // 2), key=lambda pair: pair != AHEAD[chunk][0] // 2):
-                prod = psum.tile([P, 2, CHUNK], F32, name="prod", tag="bank_%s%d" % (PROD_BANKS[chunk], pair))
-                for i in range(2):
-                    m = slice((2 * pair + i) * P, (2 * pair + i + 1) * P)
-                    nc.tensor.matmul_mx(
-                        prod[:, i, :],
-                        lhsT=wd_w[:, m].bitcast(FP8X4),
-                        lhsT_scale=wd_sc[:].bitcast(U8)[:, m],
-                        rhs=h_w[:].bitcast(FP8X4),
-                        rhs_scale=h_sc[:],
-                        start=True,
-                        stop=True,
-                    )
-                products[chunk, pair] = prod
+            edges = slice(chunk * CHUNK, (chunk + 1) * CHUNK)
+            nc.vector.quantize_mx(h_w[:, edges].bitcast(FP8X4), h_sc[:, edges], grouped[:].rearrange("p n t -> p (n t)"))
 
-        def span(chunk, n_tile):
-            bounds = STARTS[n_tile] + (CHUNKS,)
-            return max(b for b in bounds if b <= chunk), min(b for b in bounds if b > chunk)
-
-        def evacuate(chunk, n_tile, tag=""):
-            first, last = span(chunk, n_tile)
-            if chunk == first:
-                messages[n_tile, first] = keep.tile([P, (last - first) * CHUNK], F32, name="y%d_%d" % (n_tile, first), tag=tag)
-            cols = slice((chunk - first) * CHUNK, (chunk - first + 1) * CHUNK)
-            nc.scalar.copy(messages[n_tile, first][:, cols], products[chunk, n_tile // 2][:, n_tile % 2, :])
-            if chunk == last - 1:
-                entries = slice(first * CHUNK // 16, last * CHUNK // 16)
+        def second_layer(n_tiles, first, last, bank, tag):
+            width = last - first
+            prod = psum.tile([P, len(n_tiles), width], F32, name="prod", tag="bank_" + bank)
+            for i, n_tile in enumerate(n_tiles):
+                m = slice(n_tile * P, (n_tile + 1) * P)
+                nc.tensor.matmul_mx(
+                    prod[:, i, :],
+                    lhsT=wd_w[:, m].bitcast(FP8X4),
+                    lhsT_scale=wd_sc[:].bitcast(U8)[:, m],
+                    rhs=h_w[:, first:last].bitcast(FP8X4),
+                    rhs_scale=h_sc[:, first:last],
+                    start=True,
+                    stop=True,
+                )
+            message = keep.tile([P, len(n_tiles), width], F32, name="y%d_%d" % (n_tiles[0], first), tag=tag, align_bytes=64)
+            for i, n_tile in enumerate(n_tiles):
+                nc.scalar.copy(message[:, i, :], prod[:, i, :])
                 nc.vector.tensor_tensor(
-                    windows[n_tile][:].indirect(dst_list[:, entries]),
-                    messages[n_tile, first][:],
-                    wgo_sb[:, first * CHUNK : last * CHUNK],
+                    windows[n_tile][:].indirect(dst_list[:, first // 16 : last // 16]),
+                    message[:, i, :],
+                    wgo_sb[:, first:last],
                     MULT,
                 )
-                if last == CHUNKS:
+                if last == J:
                     nc.sync.dma_start(out[n_tile * P : (n_tile + 1) * P, :], windows[n_tile][:])
 
         both = (DST, SRC)
@@ -220,18 +206,22 @@ def tile_list_msg_silu_none_kernel(
         gather_words(CHUNK, 2 * CHUNK, 1, both)
         gather_words(5 * UNIT, J, 0, both, spare=8)
         gather_words(2 * CHUNK, 3 * CHUNK, 1, both)
-        second_layer(0, first_layer(0))
-        gather_words(3 * CHUNK, J, 1, both, tag="grouped0")
-        for i in range(2):
-            window = reuse.tile([P, T], F32, name="window%d" % (2 + i), offset=4 * T * i)
-            nc.gpsimd.memset(window[:], 0.0)
-            windows.append(window)
-        for chunk in range(1, CHUNKS):
-            act = first_layer(chunk)
-            for n_tile in AHEAD[chunk - 1]:
-                evacuate(chunk - 1, n_tile)
-            second_layer(chunk, act)
-            for held in HELD[chunk - 1]:
-                evacuate(*held, tag="hidden%d" % chunk)
-        for n_tile in AHEAD[CHUNKS - 1]:
-            evacuate(CHUNKS - 1, n_tile)
+        def scatter(n_tiles, first, last, bank, tag=""):
+            second_layer(n_tiles, first * CHUNK, last * CHUNK, bank, tag)
+
+        quantize_hidden(0, scale_hidden(0, first_layer(0)))
+        gather_words(3 * CHUNK, J, 1, both, tag="hidden0")
+        act = first_layer(1)
+        scatter((0, 1), 0, 1, "f0")
+        quantize_hidden(1, scale_hidden(1, act))
+        scatter((2, 3), 0, 1, "e1", "hidden1")
+        hidden = scale_hidden(2, first_layer(2))
+        scatter((0, 1), 1, 2, "d0")
+        quantize_hidden(2, hidden)
+        scatter((2, 3), 1, 2, "d1", "hidden2")
+        quantize_hidden(3, scale_hidden(3, first_layer(3)))
+        scatter((0,), 2, 3, "e1", "hidden3")
+        scatter((1,), 2, 4, "f0")
+        scatter((0,), 3, 4, "f1")
+        scatter((2,), 2, 4, "e0")
+        scatter((3,), 2, 4, "d0")

@@ -28,7 +28,9 @@ CHUNK = 256
 UNITS = CHUNK // UNIT
 CHUNKS = J // CHUNK
 N_TILES = N // P
+HALF = J // 2
 SRC, DST = 0, 1
+ORDER = ((0, DST), (0, SRC), (1, SRC), (1, DST))
 TURN_BANKS = "dede"
 
 
@@ -38,7 +40,6 @@ def tile_list_msg_silu_none_kernel(
     nc = tc.nc
     with ExitStack() as ctx:
         keep = ctx.enter_context(tc.tile_pool(name="keep", bufs=1))
-        late = ctx.enter_context(tc.tile_pool(name="late", bufs=1))
         reuse = ctx.enter_context(tc.tile_pool(name="reuse", bufs=1))
         work = ctx.enter_context(tc.tile_pool(name="work", bufs=2))
         psum = ctx.enter_context(tc.psum_pool(name="psum", bufs=1))
@@ -46,13 +47,13 @@ def tile_list_msg_silu_none_kernel(
         src_list = keep.tile([P, J // 16], U16, name="src_list")
         dst_list = keep.tile([P, J // 16], U16, name="dst_list")
         lists = (src_list, dst_list)
-        tab_sc = late.tile([P, T // 4], I32, name="tab_sc", align_bytes=64, offset=4 * J - 64)
+        tab_sc = keep.tile([P, T // 4], I32, name="tab_sc", align_bytes=64)
         tab_w = reuse.tile([P, PASSES * T], I32, name="tab_w", offset=0)
         ws_w = keep.tile([P, PASSES, R], I32, name="ws_w", align_bytes=64)
         wt_w = keep.tile([P, PASSES, R // 2], I32, name="wt_w", align_bytes=64)
         ws_sc = keep.tile([P, PASSES, R // 4], I32, name="ws_sc", align_bytes=64)
         wt_sc = keep.tile([P, PASSES, R // 4], I32, name="wt_sc", align_bytes=64)
-        dst_sc1 = keep.tile([P, J // 4], I32, name="dst_sc1", align_bytes=64)
+        dst_sc1 = keep.tile([P, 2, HALF // 4], I32, name="dst_sc1", align_bytes=64)
         ident = keep.tile([P, P], F32, name="ident")
         windows = [keep.tile([P, T], F32, name="window%d" % n) for n in range(N_TILES)]
 
@@ -64,9 +65,9 @@ def tile_list_msg_silu_none_kernel(
                 )
 
         nc.gpsimd.memset(tab_sc[:], 0)
-        nc.vector.memset(wt_sc[:], 0)
-        nc.gpsimd.memset(ws_sc[:], 0)
-        load_weight_scales(ws_sc, ws_scales, nc.gpsimd)
+        nc.vector.memset(ws_sc[:], 0)
+        nc.gpsimd.memset(wt_sc[:], 0)
+        load_weight_scales(wt_sc, wt_scales, nc.gpsimd)
         sm_sb = keep.tile([P, PACK], F32, name="sm_sb")
         nc.gpsimd.dma_start(sm_sb[:], sm.rearrange("(p t) -> p t", t=PACK))
         make_identity(nc, ident[:])
@@ -83,24 +84,26 @@ def tile_list_msg_silu_none_kernel(
             nc.sync.dma_start(tab_w[:, a * T : (a + 1) * T], tab_words[a].rearrange("p t i -> p (t i)").bitcast(I32))
 
         nc.sync.dma_start(dst_list[:], offs2)
+        load_table(0)
         nc.sync.dma_start(src_list[:], offs)
         for q in range(QUADS):
             nc.sync.dma_start(tab_sc[32 * q : 32 * q + PASSES * ROWS, :], tab_scales[:, 4 * q : 4 * q + 4, :].bitcast(I32))
-        load_weight_scales(wt_sc, wt_scales, nc.sync, range(1))
-        load_table(0)
         nc.sync.dma_start(wt_w[:], wt_words.rearrange("a p b -> p a b").bitcast(I32))
-        load_weight_scales(wt_sc, wt_scales, nc.sync, range(1, QUADS))
         load_ws(0)
         load_table(1)
         load_ws(1)
+        load_weight_scales(ws_sc, ws_scales, nc.sync)
 
-        picked_sc = keep.tile([P, 2, J], U8, name="picked_sc", align_bytes=64)
+        picked_sc = {}
         picked_w = {}
 
-        def gather_scales(side, first, last):
-            nc.vector.tensor_copy(
-                picked_sc[:, side, first:last], tab_sc[:].bitcast(U8).indirect(lists[side][:, first // 16 : last // 16])
-            )
+        def gather_scales(half, tag=""):
+            picked = keep.tile([P, 2, HALF], U8, name="picked_sc%d" % half, tag=tag, align_bytes=64)
+            entries = slice(half * HALF // 16, (half + 1) * HALF // 16)
+            nc.vector.tensor_copy(picked[:, DST, :], tab_sc[:].bitcast(U8).indirect(dst_list[:, entries]))
+            (nc.scalar, nc.sync)[half].dma_start(dst_sc1[0:100, half, :], picked[ROWS : ROWS + 100, DST, :].bitcast(I32))
+            nc.vector.tensor_copy(picked[:, SRC, :], tab_sc[:].bitcast(U8).indirect(src_list[:, entries]))
+            picked_sc[half] = picked
 
         def gather_words(first, last, a, sides, spare=0, tag=""):
             picked = keep.tile(
@@ -112,13 +115,11 @@ def tile_list_msg_silu_none_kernel(
                 for unit in range(first // UNIT, last // UNIT):
                     picked_w[unit, a, side] = picked[:, i, unit * UNIT - first : (unit + 1) * UNIT - first]
 
-        gather_scales(DST, 0, J)
-        nc.scalar.dma_start(dst_sc1[0:100, :], picked_sc[ROWS : ROWS + 100, DST, :].bitcast(I32))
-        gather_scales(SRC, 0, J)
-        gather_words(0, CHUNK, 0, (DST, SRC))
+        gather_words(0, 2 * CHUNK, 0, (DST, SRC))
+        gather_scales(0)
 
-        wgo_sb = late.tile([P, J], F32, name="wgo_sb", offset=0)
-        wd_w = late.tile([P, N], I32, name="wd_w", offset=4 * J + 64, align_bytes=64)
+        wgo_sb = keep.tile([P, J], F32, name="wgo_sb")
+        wd_w = keep.tile([P, N], I32, name="wd_w", align_bytes=64)
         nc.sync.dma_start(wd_w[:], wd_words[0].rearrange("p n i -> p (n i)").bitcast(I32))
         for q in range(QUADS):
             nc.sync.dma_start(wd_sc[32 * q : 32 * q + ROWS, :], wd_scales[0, 4 * q : 4 * q + 4, :].bitcast(I32))
@@ -130,16 +131,17 @@ def tile_list_msg_silu_none_kernel(
         def first_layer(chunk):
             act = work.tile([P, UNITS, PACK, P], F32, name="act")
             acc = psum.tile([P, UNITS, R], F32, name="acc")
-            steps = [(u, a, side) for u in range(UNITS) for a in range(PASSES) for side in (DST, SRC)]
+            steps = [(u, a, side) for u in range(UNITS) for a, side in ORDER]
             if chunk == 0:
-                steps = sorted(steps, key=lambda step: (step[1], -step[2]))
+                steps = sorted(steps, key=lambda step: ORDER.index(step[1:]))
             for u, a, side in steps:
-                edges = slice(chunk * CHUNK + u * UNIT, chunk * CHUNK + (u + 1) * UNIT)
+                half, start = divmod(chunk * CHUNK + u * UNIT, HALF)
+                edges = slice(start, start + UNIT)
                 if side == SRC:
-                    edge_sc = picked_sc[ROWS * a : P, SRC, edges]
+                    edge_sc = picked_sc[half][ROWS * a : P, SRC, edges]
                     weight, weight_sc = ws_w[:, a, :].bitcast(FP8X4), ws_sc[:, a, :]
                 else:
-                    edge_sc = (picked_sc[:, DST, edges], dst_sc1[:].bitcast(U8)[:, edges])[a]
+                    edge_sc = (picked_sc[half][:, DST, edges], dst_sc1[:, half, :].bitcast(U8)[:, edges])[a]
                     weight, weight_sc = wt_w[:, a, :].bitcast(FP4X4), wt_sc[:, a, :]
                 nc.tensor.matmul_mx(
                     acc[:, u, :],
@@ -147,8 +149,8 @@ def tile_list_msg_silu_none_kernel(
                     lhsT_scale=edge_sc,
                     rhs=weight,
                     rhs_scale=weight_sc.bitcast(U8),
-                    start=(a, side) == (0, DST),
-                    stop=(a, side) == (PASSES - 1, SRC),
+                    start=(a, side) == ORDER[0],
+                    stop=(a, side) == ORDER[-1],
                 )
             for u in range(UNITS):
                 nc.scalar.activation(act[:, u, :, :], acc[:, u, :].rearrange("e (m t) -> e t m", t=PACK), SILU)
@@ -156,14 +158,14 @@ def tile_list_msg_silu_none_kernel(
 
         def scale_hidden(chunk, act):
             hidden = keep.tile([P, PACK, CHUNK], BF16, name="hidden", tag="hidden%d" % chunk, align_bytes=64)
-            for half in range(2):
-                turned = psum.tile([P, 2, CHUNK], F32, name="turned", tag="bank_%s%d" % (TURN_BANKS[chunk], half))
-                for u in range(UNITS):
-                    for i in range(2):
-                        nc.tensor.transpose(turned[:, i, u * UNIT : (u + 1) * UNIT], act[:, u, 2 * half + i, :], ident[:])
-                for i in range(2):
-                    t = 2 * half + i
-                    nc.scalar.activation(hidden[:, t, :], turned[:, i, :], COPY, scale=sm_sb[:, t : t + 1])
+            for u in range(UNITS):
+                turned = psum.tile([P, PACK, UNIT], F32, name="turned", tag="bank_%s%d" % (TURN_BANKS[chunk], u))
+                for t in range(PACK):
+                    nc.tensor.transpose(turned[:, t, :], act[:, u, t, :], ident[:])
+                for t in range(PACK):
+                    nc.scalar.activation(
+                        hidden[:, t, u * UNIT : (u + 1) * UNIT], turned[:, t, :], COPY, scale=sm_sb[:, t : t + 1]
+                    )
             return hidden
 
         def quantize_hidden(chunk, hidden):
@@ -201,15 +203,16 @@ def tile_list_msg_silu_none_kernel(
                     nc.sync.dma_start(out[n_tile * P : (n_tile + 1) * P, :], windows[n_tile][:])
 
         both = (DST, SRC)
-        gather_words(0, CHUNK, 1, both)
-        gather_words(CHUNK, 5 * UNIT, 0, both, spare=8)
+        gather_words(0, CHUNK, 1, (SRC, DST), tag="first_words")
         gather_words(CHUNK, 2 * CHUNK, 1, both)
-        gather_words(5 * UNIT, J, 0, both, spare=8)
+        gather_words(2 * CHUNK, J, 0, both, spare=8)
         gather_words(2 * CHUNK, 3 * CHUNK, 1, both)
         def scatter(n_tiles, first, last, bank, tag=""):
             second_layer(n_tiles, first * CHUNK, last * CHUNK, bank, tag)
 
-        quantize_hidden(0, scale_hidden(0, first_layer(0)))
+        act = first_layer(0)
+        gather_scales(1, tag="first_words")
+        quantize_hidden(0, scale_hidden(0, act))
         gather_words(3 * CHUNK, J, 1, both, tag="hidden0")
         act = first_layer(1)
         scatter((0, 1), 0, 1, "f0")

@@ -89,10 +89,10 @@ def tile_list_msg_silu_none_kernel(
         for q in range(QUADS):
             nc.sync.dma_start(tab_sc[32 * q : 32 * q + PASSES * ROWS, :], tab_scales[:, 4 * q : 4 * q + 4, :].bitcast(I32))
         nc.sync.dma_start(wt_w[:], wt_words.rearrange("a p b -> p a b").bitcast(I32))
-        load_ws(0)
         load_table(1)
-        load_ws(1)
         load_weight_scales(ws_sc, ws_scales, nc.sync)
+        load_ws(0)
+        load_ws(1)
 
         picked_sc = {}
         picked_w = {}
@@ -105,17 +105,17 @@ def tile_list_msg_silu_none_kernel(
             nc.vector.tensor_copy(picked[:, SRC, :], tab_sc[:].bitcast(U8).indirect(src_list[:, entries]))
             picked_sc[half] = picked
 
-        def gather_words(first, last, a, sides, spare=0, tag=""):
+        def gather_words(a, width, parts, spare=0, tag=""):
             picked = keep.tile(
-                [P, len(sides), last - first], U32, name="picked_w%d_%d_%d" % (first, a, sides[0]), tag=tag, align_bytes=64
+                [P, len(parts), width], U32, name="picked_w%d_%d_%d" % ((a,) + parts[0]), tag=tag, align_bytes=64
             )
             window = tab_w[:, a * T : (a + 1) * T + spare].bitcast(U32)
-            for i, side in enumerate(sides):
-                nc.vector.tensor_copy(picked[:, i, :], window.indirect(lists[side][:, first // 16 : last // 16]))
-                for unit in range(first // UNIT, last // UNIT):
-                    picked_w[unit, a, side] = picked[:, i, unit * UNIT - first : (unit + 1) * UNIT - first]
+            for i, (first, side) in enumerate(parts):
+                nc.vector.tensor_copy(picked[:, i, :], window.indirect(lists[side][:, first // 16 : (first + width) // 16]))
+                for j in range(width // UNIT):
+                    picked_w[first // UNIT + j, a, side] = picked[:, i, j * UNIT : (j + 1) * UNIT]
 
-        gather_words(0, 2 * CHUNK, 0, (DST, SRC))
+        gather_words(0, HALF, ((0, DST), (0, SRC)))
         gather_scales(0)
 
         wgo_sb = keep.tile([P, J], F32, name="wgo_sb")
@@ -202,20 +202,21 @@ def tile_list_msg_silu_none_kernel(
                 if last == J:
                     nc.sync.dma_start(out[n_tile * P : (n_tile + 1) * P, :], windows[n_tile][:])
 
-        both = (DST, SRC)
-        gather_words(0, CHUNK, 1, (SRC, DST), tag="first_words")
-        gather_words(CHUNK, 2 * CHUNK, 1, both)
-        gather_words(2 * CHUNK, J, 0, both, spare=8)
-        gather_words(2 * CHUNK, 3 * CHUNK, 1, both)
+        gather_words(1, CHUNK, ((0, SRC), (0, DST)), tag="first_words")
+        gather_words(1, CHUNK, ((CHUNK, SRC), (CHUNK, DST)))
+        gather_words(0, HALF, ((HALF, DST), (HALF, SRC)), spare=8)
+        gather_words(1, CHUNK, ((2 * CHUNK, SRC),))
+
         def scatter(n_tiles, first, last, bank, tag=""):
             second_layer(n_tiles, first * CHUNK, last * CHUNK, bank, tag)
 
         act = first_layer(0)
         gather_scales(1, tag="first_words")
         quantize_hidden(0, scale_hidden(0, act))
-        gather_words(3 * CHUNK, J, 1, both, tag="hidden0")
+        gather_words(1, CHUNK, ((2 * CHUNK, DST), (3 * CHUNK, SRC), (3 * CHUNK, DST)), tag="hidden0")
         act = first_layer(1)
-        scatter((0, 1), 0, 1, "f0")
+        scatter((0,), 0, 1, "f0")
+        scatter((1,), 0, 1, "f1")
         quantize_hidden(1, scale_hidden(1, act))
         scatter((2, 3), 0, 1, "e1", "hidden1")
         hidden = scale_hidden(2, first_layer(2))
@@ -223,8 +224,7 @@ def tile_list_msg_silu_none_kernel(
         quantize_hidden(2, hidden)
         scatter((2, 3), 1, 2, "d1", "hidden2")
         quantize_hidden(3, scale_hidden(3, first_layer(3)))
-        scatter((0,), 2, 3, "e1", "hidden3")
-        scatter((1,), 2, 4, "f0")
-        scatter((0,), 3, 4, "f1")
-        scatter((2,), 2, 4, "e0")
+        scatter((0, 1), 2, 3, "e1", "hidden3")
+        scatter((2,), 2, 4, "f0")
+        scatter((0, 1), 3, 4, "f1")
         scatter((3,), 2, 4, "d0")

@@ -65,9 +65,9 @@ def tile_list_msg_silu_none_kernel(
                 )
 
         nc.gpsimd.memset(tab_sc[:], 0)
+        nc.vector.memset(wt_sc[:], 0)
+        load_weight_scales(wt_sc, wt_scales, nc.scalar)
         nc.vector.memset(ws_sc[:], 0)
-        nc.gpsimd.memset(wt_sc[:], 0)
-        load_weight_scales(wt_sc, wt_scales, nc.gpsimd)
         sm_sb = keep.tile([P, PACK], F32, name="sm_sb")
         nc.gpsimd.dma_start(sm_sb[:], sm.rearrange("(p t) -> p t", t=PACK))
         make_identity(nc, ident[:])

@@ -69,7 +69,6 @@ def tile_list_msg_silu_none_kernel(
         load_weight_scales(wt_sc, wt_scales, nc.scalar)
         nc.vector.memset(ws_sc[:], 0)
         sm_sb = keep.tile([P, PACK], F32, name="sm_sb")
-        nc.gpsimd.dma_start(sm_sb[:], sm.rearrange("(p t) -> p t", t=PACK))
         make_identity(nc, ident[:])
         nc.vector.memset(dst_sc1[:], 0)
         wd_sc = keep.tile([P, N // 4], I32, name="wd_sc", align_bytes=64)
@@ -83,8 +82,8 @@ def tile_list_msg_silu_none_kernel(
         def load_table(a):
             nc.sync.dma_start(tab_w[:, a * T : (a + 1) * T], tab_words[a].rearrange("p t i -> p (t i)").bitcast(I32))
 
-        nc.sync.dma_start(dst_list[:], offs2)
         load_table(0)
+        nc.sync.dma_start(dst_list[:], offs2)
         nc.sync.dma_start(src_list[:], offs)
         for q in range(QUADS):
             nc.sync.dma_start(tab_sc[32 * q : 32 * q + PASSES * ROWS, :], tab_scales[:, 4 * q : 4 * q + 4, :].bitcast(I32))
@@ -93,6 +92,7 @@ def tile_list_msg_silu_none_kernel(
         load_weight_scales(ws_sc, ws_scales, nc.sync)
         load_ws(0)
         load_ws(1)
+        nc.sync.dma_start(sm_sb[:], sm.rearrange("(p t) -> p t", t=PACK))
 
         picked_sc = {}
         picked_w = {}
@@ -202,18 +202,15 @@ def tile_list_msg_silu_none_kernel(
                 if last == J:
                     nc.sync.dma_start(out[n_tile * P : (n_tile + 1) * P, :], windows[n_tile][:])
 
-        gather_words(1, CHUNK, ((0, SRC), (0, DST)), tag="first_words")
-        gather_words(1, CHUNK, ((CHUNK, SRC), (CHUNK, DST)))
+        gather_words(1, CHUNK, ((0, SRC), (0, DST)))
+        gather_words(1, J - CHUNK, ((CHUNK, SRC), (CHUNK, DST)))
         gather_words(0, HALF, ((HALF, DST), (HALF, SRC)), spare=8)
-        gather_words(1, CHUNK, ((2 * CHUNK, SRC),))
 
         def scatter(n_tiles, first, last, bank, tag=""):
             second_layer(n_tiles, first * CHUNK, last * CHUNK, bank, tag)
 
-        act = first_layer(0)
-        gather_scales(1, tag="first_words")
-        quantize_hidden(0, scale_hidden(0, act))
-        gather_words(1, CHUNK, ((2 * CHUNK, DST), (3 * CHUNK, SRC), (3 * CHUNK, DST)), tag="hidden0")
+        quantize_hidden(0, scale_hidden(0, first_layer(0)))
+        gather_scales(1, tag="hidden0")
         act = first_layer(1)
         scatter((0,), 0, 1, "f0")
         scatter((1,), 0, 1, "f1")

@@ -30,8 +30,11 @@ CHUNKS = J // CHUNK
 N_TILES = N // P
 HALF = J // 2
 SRC, DST = 0, 1
-ORDER = ((0, DST), (0, SRC), (1, SRC), (1, DST))
+ORDER = ((0, DST), (1, DST), (0, SRC), (1, SRC))
 TURN_BANKS = "dede"
+SHIFT = 16
+LIVE = 100
+SPLIT = 640
 
 
 def tile_list_msg_silu_none_kernel(
@@ -53,7 +56,7 @@ def tile_list_msg_silu_none_kernel(
         wt_w = keep.tile([P, PASSES, R // 2], I32, name="wt_w", align_bytes=64)
         ws_sc = keep.tile([P, PASSES, R // 4], I32, name="ws_sc", align_bytes=64)
         wt_sc = keep.tile([P, PASSES, R // 4], I32, name="wt_sc", align_bytes=64)
-        dst_sc1 = keep.tile([P, 2, HALF // 4], I32, name="dst_sc1", align_bytes=64)
+        pass1_sc = keep.tile([P, 2, 2 * HALF // 4], I32, name="pass1_sc", align_bytes=64)
         ident = keep.tile([P, P], F32, name="ident")
         windows = [keep.tile([P, T], F32, name="window%d" % n) for n in range(N_TILES)]
 
@@ -66,11 +69,11 @@ def tile_list_msg_silu_none_kernel(
 
         nc.gpsimd.memset(tab_sc[:], 0)
         nc.vector.memset(wt_sc[:], 0)
-        load_weight_scales(wt_sc, wt_scales, nc.scalar)
         nc.vector.memset(ws_sc[:], 0)
         sm_sb = keep.tile([P, PACK], F32, name="sm_sb")
         make_identity(nc, ident[:])
-        nc.vector.memset(dst_sc1[:], 0)
+        load_weight_scales(ws_sc, ws_scales, nc.gpsimd)
+        nc.vector.memset(pass1_sc[:], 0)
         wd_sc = keep.tile([P, N // 4], I32, name="wd_sc", align_bytes=64)
         nc.vector.memset(wd_sc[:], 0)
         for window in windows:
@@ -82,14 +85,14 @@ def tile_list_msg_silu_none_kernel(
         def load_table(a):
             nc.sync.dma_start(tab_w[:, a * T : (a + 1) * T], tab_words[a].rearrange("p t i -> p (t i)").bitcast(I32))
 
-        load_table(0)
         nc.sync.dma_start(dst_list[:], offs2)
         nc.sync.dma_start(src_list[:], offs)
-        for q in range(QUADS):
-            nc.sync.dma_start(tab_sc[32 * q : 32 * q + PASSES * ROWS, :], tab_scales[:, 4 * q : 4 * q + 4, :].bitcast(I32))
+        for r in range(ROWS):
+            nc.sync.dma_start(tab_sc[r:P:SHIFT, :], tab_scales.rearrange("a (q r) t -> r q a t", r=ROWS)[r].bitcast(I32))
+        load_table(0)
+        load_weight_scales(wt_sc, wt_scales, nc.sync)
         nc.sync.dma_start(wt_w[:], wt_words.rearrange("a p b -> p a b").bitcast(I32))
         load_table(1)
-        load_weight_scales(ws_sc, ws_scales, nc.sync)
         load_ws(0)
         load_ws(1)
         nc.sync.dma_start(sm_sb[:], sm.rearrange("(p t) -> p t", t=PACK))
@@ -101,8 +104,10 @@ def tile_list_msg_silu_none_kernel(
             picked = keep.tile([P, 2, HALF], U8, name="picked_sc%d" % half, tag=tag, align_bytes=64)
             entries = slice(half * HALF // 16, (half + 1) * HALF // 16)
             nc.vector.tensor_copy(picked[:, DST, :], tab_sc[:].bitcast(U8).indirect(dst_list[:, entries]))
-            (nc.scalar, nc.sync)[half].dma_start(dst_sc1[0:100, half, :], picked[ROWS : ROWS + 100, DST, :].bitcast(I32))
             nc.vector.tensor_copy(picked[:, SRC, :], tab_sc[:].bitcast(U8).indirect(src_list[:, entries]))
+            (nc.scalar, nc.sync)[half].dma_start(
+                pass1_sc[0:LIVE, half, :], picked[SHIFT : SHIFT + LIVE, :, :].rearrange("p s e -> p (s e)").bitcast(I32)
+            )
             picked_sc[half] = picked
 
         def gather_words(a, width, parts, spare=0, tag=""):
@@ -115,8 +120,8 @@ def tile_list_msg_silu_none_kernel(
                 for j in range(width // UNIT):
                     picked_w[first // UNIT + j, a, side] = picked[:, i, j * UNIT : (j + 1) * UNIT]
 
-        gather_words(0, HALF, ((0, DST), (0, SRC)))
         gather_scales(0)
+        gather_words(0, SPLIT, ((0, DST), (0, SRC)))
 
         wgo_sb = keep.tile([P, J], F32, name="wgo_sb")
         wd_w = keep.tile([P, N], I32, name="wd_w", align_bytes=64)
@@ -133,15 +138,17 @@ def tile_list_msg_silu_none_kernel(
             acc = psum.tile([P, UNITS, R], F32, name="acc")
             steps = [(u, a, side) for u in range(UNITS) for a, side in ORDER]
             if chunk == 0:
-                steps = sorted(steps, key=lambda step: ORDER.index(step[1:]))
+                steps = sorted(steps, key=lambda step: step[1:] != ORDER[0])
             for u, a, side in steps:
                 half, start = divmod(chunk * CHUNK + u * UNIT, HALF)
                 edges = slice(start, start + UNIT)
+                if a == 0:
+                    edge_sc = picked_sc[half][:, side, edges]
+                else:
+                    edge_sc = pass1_sc[:, half, :].bitcast(U8)[:, side * HALF + start : side * HALF + start + UNIT]
                 if side == SRC:
-                    edge_sc = picked_sc[half][ROWS * a : P, SRC, edges]
                     weight, weight_sc = ws_w[:, a, :].bitcast(FP8X4), ws_sc[:, a, :]
                 else:
-                    edge_sc = (picked_sc[half][:, DST, edges], dst_sc1[:, half, :].bitcast(U8)[:, edges])[a]
                     weight, weight_sc = wt_w[:, a, :].bitcast(FP4X4), wt_sc[:, a, :]
                 nc.tensor.matmul_mx(
                     acc[:, u, :],
@@ -202,15 +209,16 @@ def tile_list_msg_silu_none_kernel(
                 if last == J:
                     nc.sync.dma_start(out[n_tile * P : (n_tile + 1) * P, :], windows[n_tile][:])
 
-        gather_words(1, CHUNK, ((0, SRC), (0, DST)))
-        gather_words(1, J - CHUNK, ((CHUNK, SRC), (CHUNK, DST)))
-        gather_words(0, HALF, ((HALF, DST), (HALF, SRC)), spare=8)
+        gather_words(1, CHUNK, ((0, DST), (0, SRC)), tag="first_words")
+        gather_words(1, J - CHUNK, ((CHUNK, DST), (CHUNK, SRC)))
 
         def scatter(n_tiles, first, last, bank, tag=""):
             second_layer(n_tiles, first * CHUNK, last * CHUNK, bank, tag)
 
-        quantize_hidden(0, scale_hidden(0, first_layer(0)))
-        gather_scales(1, tag="hidden0")
+        act = first_layer(0)
+        gather_scales(1, tag="first_words")
+        quantize_hidden(0, scale_hidden(0, act))
+        gather_words(0, J - SPLIT, ((SPLIT, DST), (SPLIT, SRC)), tag="hidden0")
         act = first_layer(1)
         scatter((0,), 0, 1, "f0")
         scatter((1,), 0, 1, "f1")

@@ -34,7 +34,9 @@ ORDER = ((0, DST), (1, DST), (0, SRC), (1, SRC))
 TURN_BANKS = "dede"
 SHIFT = 16
 LIVE = 100
-SPLIT = 640
+SPARE = 8
+BANK_BYTES = 2048
+LAST = J - CHUNK
 
 
 def tile_list_msg_silu_none_kernel(
@@ -46,6 +48,7 @@ def tile_list_msg_silu_none_kernel(
         reuse = ctx.enter_context(tc.tile_pool(name="reuse", bufs=1))
         work = ctx.enter_context(tc.tile_pool(name="work", bufs=2))
         psum = ctx.enter_context(tc.psum_pool(name="psum", bufs=1))
+        sums = ctx.enter_context(tc.psum_pool(name="sums", bufs=1))
 
         src_list = keep.tile([P, J // 16], U16, name="src_list")
         dst_list = keep.tile([P, J // 16], U16, name="dst_list")
@@ -56,9 +59,9 @@ def tile_list_msg_silu_none_kernel(
         wt_w = keep.tile([P, PASSES, R // 2], I32, name="wt_w", align_bytes=64)
         ws_sc = keep.tile([P, PASSES, R // 4], I32, name="ws_sc", align_bytes=64)
         wt_sc = keep.tile([P, PASSES, R // 4], I32, name="wt_sc", align_bytes=64)
-        pass1_sc = keep.tile([P, 2, 2 * HALF // 4], I32, name="pass1_sc", align_bytes=64)
+        pass1_sc = keep.tile([P, 2, 2, HALF // 4], I32, name="pass1_sc", align_bytes=64)
         ident = keep.tile([P, P], F32, name="ident")
-        windows = [keep.tile([P, T], F32, name="window%d" % n) for n in range(N_TILES)]
+        windows = [keep.tile([P, T], F32, name="window%d" % n) for n in range(N_TILES - 1)]
 
         def load_weight_scales(tile, scales, queue, quads=range(QUADS)):
             for q in quads:
@@ -68,14 +71,14 @@ def tile_list_msg_silu_none_kernel(
                 )
 
         nc.gpsimd.memset(tab_sc[:], 0)
+        nc.gpsimd.memset(ws_sc[:], 0)
+        load_weight_scales(ws_sc, ws_scales, nc.gpsimd)
         nc.vector.memset(wt_sc[:], 0)
-        nc.vector.memset(ws_sc[:], 0)
         sm_sb = keep.tile([P, PACK], F32, name="sm_sb")
         make_identity(nc, ident[:])
-        load_weight_scales(ws_sc, ws_scales, nc.gpsimd)
         nc.vector.memset(pass1_sc[:], 0)
         wd_sc = keep.tile([P, N // 4], I32, name="wd_sc", align_bytes=64)
-        nc.vector.memset(wd_sc[:], 0)
+        nc.gpsimd.memset(wd_sc[:], 0)
         for window in windows:
             nc.gpsimd.memset(window[:], 0.0)
 
@@ -87,11 +90,11 @@ def tile_list_msg_silu_none_kernel(
 
         nc.sync.dma_start(dst_list[:], offs2)
         nc.sync.dma_start(src_list[:], offs)
+        nc.sync.dma_start(wt_w[:], wt_words.rearrange("a p b -> p a b").bitcast(I32))
         for r in range(ROWS):
             nc.sync.dma_start(tab_sc[r:P:SHIFT, :], tab_scales.rearrange("a (q r) t -> r q a t", r=ROWS)[r].bitcast(I32))
         load_table(0)
         load_weight_scales(wt_sc, wt_scales, nc.sync)
-        nc.sync.dma_start(wt_w[:], wt_words.rearrange("a p b -> p a b").bitcast(I32))
         load_table(1)
         load_ws(0)
         load_ws(1)
@@ -103,25 +106,26 @@ def tile_list_msg_silu_none_kernel(
         def gather_scales(half, tag=""):
             picked = keep.tile([P, 2, HALF], U8, name="picked_sc%d" % half, tag=tag, align_bytes=64)
             entries = slice(half * HALF // 16, (half + 1) * HALF // 16)
-            nc.vector.tensor_copy(picked[:, DST, :], tab_sc[:].bitcast(U8).indirect(dst_list[:, entries]))
-            nc.vector.tensor_copy(picked[:, SRC, :], tab_sc[:].bitcast(U8).indirect(src_list[:, entries]))
-            (nc.scalar, nc.sync)[half].dma_start(
-                pass1_sc[0:LIVE, half, :], picked[SHIFT : SHIFT + LIVE, :, :].rearrange("p s e -> p (s e)").bitcast(I32)
-            )
+            for side in (DST, SRC):
+                nc.vector.tensor_copy(picked[:, side, :], tab_sc[:].bitcast(U8).indirect(lists[side][:, entries]))
+                (nc.scalar, nc.sync)[half].dma_start(
+                    pass1_sc[0:LIVE, half, side, :], picked[SHIFT : SHIFT + LIVE, side, :].bitcast(I32)
+                )
             picked_sc[half] = picked
 
-        def gather_words(a, width, parts, spare=0, tag=""):
-            picked = keep.tile(
-                [P, len(parts), width], U32, name="picked_w%d_%d_%d" % ((a,) + parts[0]), tag=tag, align_bytes=64
-            )
-            window = tab_w[:, a * T : (a + 1) * T + spare].bitcast(U32)
-            for i, (first, side) in enumerate(parts):
-                nc.vector.tensor_copy(picked[:, i, :], window.indirect(lists[side][:, first // 16 : (first + width) // 16]))
-                for j in range(width // UNIT):
-                    picked_w[first // UNIT + j, a, side] = picked[:, i, j * UNIT : (j + 1) * UNIT]
+        def gather_words(parts, spare=0, tag=""):
+            total = sum(last - first for a, side, first, last in parts)
+            picked = keep.tile([P, total], U32, name="picked_w%d_%d_%d_%d" % parts[0], tag=tag, align_bytes=64)
+            at = 0
+            for a, side, first, last in parts:
+                window = tab_w[:, a * T : (a + 1) * T + spare].bitcast(U32)
+                nc.vector.tensor_copy(picked[:, at : at + last - first], window.indirect(lists[side][:, first // 16 : last // 16]))
+                for edge in range(first, last, UNIT):
+                    picked_w[edge // UNIT, a, side] = picked[:, at + edge - first : at + edge - first + UNIT]
+                at = at + last - first
 
         gather_scales(0)
-        gather_words(0, SPLIT, ((0, DST), (0, SRC)))
+        gather_words(((0, DST, 0, HALF), (0, SRC, 0, HALF)))
 
         wgo_sb = keep.tile([P, J], F32, name="wgo_sb")
         wd_w = keep.tile([P, N], I32, name="wd_w", align_bytes=64)
@@ -135,7 +139,11 @@ def tile_list_msg_silu_none_kernel(
 
         def first_layer(chunk):
             act = work.tile([P, UNITS, PACK, P], F32, name="act")
-            acc = psum.tile([P, UNITS, R], F32, name="acc")
+            if chunk == 0:
+                acc = [sums.tile([P, R], F32, name="acc_unit%d" % u, offset=u * BANK_BYTES)[:] for u in range(UNITS)]
+            else:
+                both = sums.tile([P, UNITS, R], F32, name="acc", offset=0)
+                acc = [both[:, u, :] for u in range(UNITS)]
             steps = [(u, a, side) for u in range(UNITS) for a, side in ORDER]
             if chunk == 0:
                 steps = sorted(steps, key=lambda step: step[1:] != ORDER[0])
@@ -145,13 +153,13 @@ def tile_list_msg_silu_none_kernel(
                 if a == 0:
                     edge_sc = picked_sc[half][:, side, edges]
                 else:
-                    edge_sc = pass1_sc[:, half, :].bitcast(U8)[:, side * HALF + start : side * HALF + start + UNIT]
+                    edge_sc = pass1_sc[:, half, side, :].bitcast(U8)[:, edges]
                 if side == SRC:
                     weight, weight_sc = ws_w[:, a, :].bitcast(FP8X4), ws_sc[:, a, :]
                 else:
                     weight, weight_sc = wt_w[:, a, :].bitcast(FP4X4), wt_sc[:, a, :]
                 nc.tensor.matmul_mx(
-                    acc[:, u, :],
+                    acc[u],
                     lhsT=picked_w[chunk * UNITS + u, a, side].bitcast(FP8X4),
                     lhsT_scale=edge_sc,
                     rhs=weight,
@@ -160,7 +168,7 @@ def tile_list_msg_silu_none_kernel(
                     stop=(a, side) == ORDER[-1],
                 )
             for u in range(UNITS):
-                nc.scalar.activation(act[:, u, :, :], acc[:, u, :].rearrange("e (m t) -> e t m", t=PACK), SILU)
+                nc.scalar.activation(act[:, u, :, :], acc[u].rearrange("e (m t) -> e t m", t=PACK), SILU)
             return act
 
         def scale_hidden(chunk, act):
@@ -209,8 +217,9 @@ def tile_list_msg_silu_none_kernel(
                 if last == J:
                     nc.sync.dma_start(out[n_tile * P : (n_tile + 1) * P, :], windows[n_tile][:])
 
-        gather_words(1, CHUNK, ((0, DST), (0, SRC)), tag="first_words")
-        gather_words(1, J - CHUNK, ((CHUNK, DST), (CHUNK, SRC)))
+        gather_words(((1, DST, 0, CHUNK), (1, SRC, 0, CHUNK)), tag="first_words")
+        gather_words(((1, DST, CHUNK, J), (1, SRC, CHUNK, LAST)))
+        gather_words(((0, DST, HALF, J),), spare=SPARE)
 
         def scatter(n_tiles, first, last, bank, tag=""):
             second_layer(n_tiles, first * CHUNK, last * CHUNK, bank, tag)
@@ -218,7 +227,9 @@ def tile_list_msg_silu_none_kernel(
         act = first_layer(0)
         gather_scales(1, tag="first_words")
         quantize_hidden(0, scale_hidden(0, act))
-        gather_words(0, J - SPLIT, ((SPLIT, DST), (SPLIT, SRC)), tag="hidden0")
+        gather_words(((0, SRC, HALF, J), (1, SRC, LAST, J)), tag="hidden0")
+        windows.append(keep.tile([P, T], F32, name="window_last", tag="grouped0", align_bytes=64))
+        nc.gpsimd.memset(windows[-1][:], 0.0)
         act = first_layer(1)
         scatter((0,), 0, 1, "f0")
         scatter((1,), 0, 1, "f1")

@@ -35,6 +35,10 @@ TURN_BANKS = "dede"
 SHIFT = 16
 LIVE = 100
 SPARE = 8
+EARLY_WINDOWS = 2
+TABLE_BYTES = PASSES * T * 4
+WINDOW_BYTES = T * 4
+GROUPED_BYTES = CHUNK * PACK * 2
 BANK_BYTES = 2048
 LAST = J - CHUNK
 
@@ -61,7 +65,7 @@ def tile_list_msg_silu_none_kernel(
         wt_sc = keep.tile([P, PASSES, R // 4], I32, name="wt_sc", align_bytes=64)
         pass1_sc = keep.tile([P, 2, 2, HALF // 4], I32, name="pass1_sc", align_bytes=64)
         ident = keep.tile([P, P], F32, name="ident")
-        windows = [keep.tile([P, T], F32, name="window%d" % n) for n in range(N_TILES - 1)]
+        windows = [keep.tile([P, T], F32, name="window%d" % n) for n in range(EARLY_WINDOWS)]
 
         def load_weight_scales(tile, scales, queue, quads=range(QUADS)):
             for q in quads:
@@ -173,20 +177,37 @@ def tile_list_msg_silu_none_kernel(
 
         def scale_hidden(chunk, act):
             hidden = keep.tile([P, PACK, CHUNK], BF16, name="hidden", tag="hidden%d" % chunk, align_bytes=64)
+            if chunk == 0:
+                offset = TABLE_BYTES + WINDOW_BYTES - GROUPED_BYTES // 2
+                grouped = reuse.tile([P, CHUNK, PACK], BF16, name="grouped_first", offset=offset, align_bytes=64)
+            else:
+                grouped = keep.tile([P, CHUNK, PACK], BF16, name="grouped", tag="grouped%d" % chunk, align_bytes=64)
             for u in range(UNITS):
                 turned = psum.tile([P, PACK, UNIT], F32, name="turned", tag="bank_%s%d" % (TURN_BANKS[chunk], u))
                 for t in range(PACK):
                     nc.tensor.transpose(turned[:, t, :], act[:, u, t, :], ident[:])
+                if chunk == 0 and u == 0:
+                    staged = keep.tile([P, PACK, UNIT], F32, name="staged")
+                    nc.scalar.copy(staged[:], turned[:])
+                    nc.gpsimd.tensor_tensor(
+                        grouped[:, :UNIT, :],
+                        staged[:].rearrange("p t e -> p e t"),
+                        sm_sb[:].unsqueeze(1).to_broadcast([P, UNIT, PACK]),
+                        MULT,
+                    )
+                    continue
                 for t in range(PACK):
                     nc.scalar.activation(
                         hidden[:, t, u * UNIT : (u + 1) * UNIT], turned[:, t, :], COPY, scale=sm_sb[:, t : t + 1]
                     )
-            return hidden
+            return hidden, grouped
 
-        def quantize_hidden(chunk, hidden):
-            grouped = keep.tile([P, CHUNK, PACK], BF16, name="grouped", tag="grouped%d" % chunk, align_bytes=64)
+        def quantize_hidden(chunk, tiles):
+            hidden, grouped = tiles
+            first = UNIT if chunk == 0 else 0
             nc.scalar.copy(
-                grouped[:].rearrange("p (c i) t -> p c t i", i=4), hidden[:].rearrange("p t (c i) -> p c t i", i=4)
+                grouped[:, first:, :].rearrange("p (c i) t -> p c t i", i=4),
+                hidden[:, :, first:].rearrange("p t (c i) -> p c t i", i=4),
             )
             edges = slice(chunk * CHUNK, (chunk + 1) * CHUNK)
             nc.vector.quantize_mx(h_w[:, edges].bitcast(FP8X4), h_sc[:, edges], grouped[:].rearrange("p n t -> p (n t)"))
@@ -228,8 +249,10 @@ def tile_list_msg_silu_none_kernel(
         gather_scales(1, tag="first_words")
         quantize_hidden(0, scale_hidden(0, act))
         gather_words(((0, SRC, HALF, J), (1, SRC, LAST, J)), tag="hidden0")
-        windows.append(keep.tile([P, T], F32, name="window_last", tag="grouped0", align_bytes=64))
-        nc.gpsimd.memset(windows[-1][:], 0.0)
+        for n in range(EARLY_WINDOWS, N_TILES):
+            offset = TABLE_BYTES + (n - EARLY_WINDOWS) * WINDOW_BYTES
+            windows.append(reuse.tile([P, T], F32, name="window%d" % n, offset=offset))
+            nc.gpsimd.memset(windows[n][:], 0.0)
         act = first_layer(1)
         scatter((0,), 0, 1, "f0")
         scatter((1,), 0, 1, "f1")

@@ -26,21 +26,14 @@ ROWS = 4
 UNIT = 128
 CHUNK = 256
 UNITS = CHUNK // UNIT
-CHUNKS = J // CHUNK
-N_TILES = N // P
 HALF = J // 2
-SRC, DST = 0, 1
-ORDER = ((0, DST), (1, DST), (0, SRC), (1, SRC))
-TURN_BANKS = "dede"
-SHIFT = 16
-LIVE = 100
-SPARE = 8
-EARLY_WINDOWS = 2
-TABLE_BYTES = PASSES * T * 4
+DST, SRC = 0, 1
+SCALE_ROWS = PASSES * QUADS * ROWS
+FIRST_ROW = P - SCALE_ROWS
 WINDOW_BYTES = T * 4
 GROUPED_BYTES = CHUNK * PACK * 2
 BANK_BYTES = 2048
-LAST = J - CHUNK
+EARLY_DST = 3 * CHUNK
 
 
 def tile_list_msg_silu_none_kernel(
@@ -54,92 +47,77 @@ def tile_list_msg_silu_none_kernel(
         psum = ctx.enter_context(tc.psum_pool(name="psum", bufs=1))
         sums = ctx.enter_context(tc.psum_pool(name="sums", bufs=1))
 
-        src_list = keep.tile([P, J // 16], U16, name="src_list")
         dst_list = keep.tile([P, J // 16], U16, name="dst_list")
-        lists = (src_list, dst_list)
+        src_list = keep.tile([P, J // 16], U16, name="src_list")
+        lists = (dst_list, src_list)
         tab_sc = keep.tile([P, T // 4], I32, name="tab_sc", align_bytes=64)
-        tab_w = reuse.tile([P, PASSES * T], I32, name="tab_w", offset=0)
-        ws_w = keep.tile([P, PASSES, R], I32, name="ws_w", align_bytes=64)
+        tab_w = [keep.tile([P, T], I32, name="tab_w%d" % a, align_bytes=64) for a in range(PASSES)]
+        ws_w = [keep.tile([P, R], I32, name="ws_w%d" % a, align_bytes=64) for a in range(PASSES)]
         wt_w = keep.tile([P, PASSES, R // 2], I32, name="wt_w", align_bytes=64)
         ws_sc = keep.tile([P, PASSES, R // 4], I32, name="ws_sc", align_bytes=64)
         wt_sc = keep.tile([P, PASSES, R // 4], I32, name="wt_sc", align_bytes=64)
-        pass1_sc = keep.tile([P, 2, 2, HALF // 4], I32, name="pass1_sc", align_bytes=64)
+        wd_sc = keep.tile([P, N // 4], I32, name="wd_sc", align_bytes=64)
+        planes = [keep.tile([P, PASSES, 2 * HALF // 4], I32, name="planes%d" % h, align_bytes=64) for h in range(2)]
         ident = keep.tile([P, P], F32, name="ident")
-        windows = [keep.tile([P, T], F32, name="window%d" % n) for n in range(EARLY_WINDOWS)]
+        sm_sb = keep.tile([P, PACK], F32, name="sm_sb")
+        wgo_sb = keep.tile([P, J], F32, name="wgo_sb")
+        wd_w = keep.tile([P, N], I32, name="wd_w", align_bytes=64)
+        h_w = keep.tile([P, J], U32, name="h_w", align_bytes=64)
+        h_sc = keep.tile([P, J], U8, name="h_sc", align_bytes=64)
+        windows = [keep.tile([P, T], F32, name="window%d" % n) for n in range(2)]
 
-        def load_weight_scales(tile, scales, queue, quads=range(QUADS)):
-            for q in quads:
+        def load_weight_scales(tile, scales, queue):
+            for q in range(QUADS):
                 queue.dma_start(
                     tile[32 * q : 32 * q + ROWS, :, :],
                     scales[:, 4 * q : 4 * q + 4, :].rearrange("a r n -> r a n").bitcast(I32),
                 )
 
-        nc.gpsimd.memset(tab_sc[:], 0)
+        nc.gpsimd.memset(wt_sc[:], 0)
+        load_weight_scales(wt_sc, wt_scales, nc.scalar)
         nc.gpsimd.memset(ws_sc[:], 0)
         load_weight_scales(ws_sc, ws_scales, nc.gpsimd)
-        nc.vector.memset(wt_sc[:], 0)
-        sm_sb = keep.tile([P, PACK], F32, name="sm_sb")
+        nc.vector.memset(tab_sc[0:FIRST_ROW, :], 0)
+        nc.vector.memset(planes[0][:], 0)
         make_identity(nc, ident[:])
-        nc.vector.memset(pass1_sc[:], 0)
-        wd_sc = keep.tile([P, N // 4], I32, name="wd_sc", align_bytes=64)
         nc.gpsimd.memset(wd_sc[:], 0)
+        nc.gpsimd.memset(planes[1][:], 0)
         for window in windows:
             nc.gpsimd.memset(window[:], 0.0)
 
-        def load_ws(a):
-            nc.sync.dma_start(ws_w[:, a, :], ws_words[a].rearrange("p r i -> p (r i)").bitcast(I32))
-
-        def load_table(a):
-            nc.sync.dma_start(tab_w[:, a * T : (a + 1) * T], tab_words[a].rearrange("p t i -> p (t i)").bitcast(I32))
-
         nc.sync.dma_start(dst_list[:], offs2)
+        nc.sync.dma_start(tab_sc[FIRST_ROW:P, :], tab_scales.rearrange("a q t -> q a t").bitcast(I32))
         nc.sync.dma_start(src_list[:], offs)
+        nc.sync.dma_start(tab_w[0][:], tab_words[0].rearrange("p t i -> p (t i)").bitcast(I32))
         nc.sync.dma_start(wt_w[:], wt_words.rearrange("a p b -> p a b").bitcast(I32))
-        for r in range(ROWS):
-            nc.sync.dma_start(tab_sc[r:P:SHIFT, :], tab_scales.rearrange("a (q r) t -> r q a t", r=ROWS)[r].bitcast(I32))
-        load_table(0)
-        load_weight_scales(wt_sc, wt_scales, nc.sync)
-        load_table(1)
-        load_ws(0)
-        load_ws(1)
-        nc.sync.dma_start(sm_sb[:], sm.rearrange("(p t) -> p t", t=PACK))
+        nc.sync.dma_start(tab_w[1][:], tab_words[1].rearrange("p t i -> p (t i)").bitcast(I32))
+        for a in range(PASSES):
+            nc.sync.dma_start(ws_w[a][:], ws_words[a].rearrange("p r i -> p (r i)").bitcast(I32))
 
-        picked_sc = {}
         picked_w = {}
 
-        def gather_scales(half, tag=""):
+        def gather_scales(half, queue, tag=""):
             picked = keep.tile([P, 2, HALF], U8, name="picked_sc%d" % half, tag=tag, align_bytes=64)
             entries = slice(half * HALF // 16, (half + 1) * HALF // 16)
             for side in (DST, SRC):
                 nc.vector.tensor_copy(picked[:, side, :], tab_sc[:].bitcast(U8).indirect(lists[side][:, entries]))
-                (nc.scalar, nc.sync)[half].dma_start(
-                    pass1_sc[0:LIVE, half, side, :], picked[SHIFT : SHIFT + LIVE, side, :].bitcast(I32)
+            for q in range(QUADS):
+                rows = slice(FIRST_ROW + 8 * q, FIRST_ROW + 8 * q + 8)
+                queue.dma_start(
+                    planes[half][32 * q : 32 * q + ROWS, :, :],
+                    picked[rows, :, :].rearrange("p s e -> p (s e)").bitcast(I32),
                 )
-            picked_sc[half] = picked
 
-        def gather_words(parts, spare=0, tag=""):
+        def gather_words(parts, tag=""):
             total = sum(last - first for a, side, first, last in parts)
             picked = keep.tile([P, total], U32, name="picked_w%d_%d_%d_%d" % parts[0], tag=tag, align_bytes=64)
             at = 0
             for a, side, first, last in parts:
-                window = tab_w[:, a * T : (a + 1) * T + spare].bitcast(U32)
+                window = tab_w[a][:].bitcast(U32)
                 nc.vector.tensor_copy(picked[:, at : at + last - first], window.indirect(lists[side][:, first // 16 : last // 16]))
                 for edge in range(first, last, UNIT):
                     picked_w[edge // UNIT, a, side] = picked[:, at + edge - first : at + edge - first + UNIT]
                 at = at + last - first
-
-        gather_scales(0)
-        gather_words(((0, DST, 0, HALF), (0, SRC, 0, HALF)))
-
-        wgo_sb = keep.tile([P, J], F32, name="wgo_sb")
-        wd_w = keep.tile([P, N], I32, name="wd_w", align_bytes=64)
-        nc.sync.dma_start(wd_w[:], wd_words[0].rearrange("p n i -> p (n i)").bitcast(I32))
-        for q in range(QUADS):
-            nc.sync.dma_start(wd_sc[32 * q : 32 * q + ROWS, :], wd_scales[0, 4 * q : 4 * q + 4, :].bitcast(I32))
-        nc.sync.dma_start(wgo_sb[:], wgo)
-
-        h_w = keep.tile([P, J], U32, name="h_w", align_bytes=64)
-        h_sc = keep.tile([P, J], U8, name="h_sc", align_bytes=64)
 
         def first_layer(chunk):
             act = work.tile([P, UNITS, PACK, P], F32, name="act")
@@ -148,18 +126,15 @@ def tile_list_msg_silu_none_kernel(
             else:
                 both = sums.tile([P, UNITS, R], F32, name="acc", offset=0)
                 acc = [both[:, u, :] for u in range(UNITS)]
-            steps = [(u, a, side) for u in range(UNITS) for a, side in ORDER]
+            order = ((0, DST), (0, SRC), (1, DST), (1, SRC))
+            steps = [(u, a, side) for u in range(UNITS) for a, side in order]
             if chunk == 0:
-                steps = sorted(steps, key=lambda step: step[1:] != ORDER[0])
+                steps = sorted(steps, key=lambda step: step[1:] != order[0])
             for u, a, side in steps:
                 half, start = divmod(chunk * CHUNK + u * UNIT, HALF)
-                edges = slice(start, start + UNIT)
-                if a == 0:
-                    edge_sc = picked_sc[half][:, side, edges]
-                else:
-                    edge_sc = pass1_sc[:, half, side, :].bitcast(U8)[:, edges]
+                edge_sc = planes[half][:, a, :].bitcast(U8)[:, side * HALF + start : side * HALF + start + UNIT]
                 if side == SRC:
-                    weight, weight_sc = ws_w[:, a, :].bitcast(FP8X4), ws_sc[:, a, :]
+                    weight, weight_sc = ws_w[a][:].bitcast(FP8X4), ws_sc[:, a, :]
                 else:
                     weight, weight_sc = wt_w[:, a, :].bitcast(FP4X4), wt_sc[:, a, :]
                 nc.tensor.matmul_mx(
@@ -168,8 +143,8 @@ def tile_list_msg_silu_none_kernel(
                     lhsT_scale=edge_sc,
                     rhs=weight,
                     rhs_scale=weight_sc.bitcast(U8),
-                    start=(a, side) == ORDER[0],
-                    stop=(a, side) == ORDER[-1],
+                    start=(a, side) == order[0],
+                    stop=(a, side) == order[-1],
                 )
             for u in range(UNITS):
                 nc.scalar.activation(act[:, u, :, :], acc[u].rearrange("e (m t) -> e t m", t=PACK), SILU)
@@ -178,12 +153,12 @@ def tile_list_msg_silu_none_kernel(
         def scale_hidden(chunk, act):
             hidden = keep.tile([P, PACK, CHUNK], BF16, name="hidden", tag="hidden%d" % chunk, align_bytes=64)
             if chunk == 0:
-                offset = TABLE_BYTES + WINDOW_BYTES - GROUPED_BYTES // 2
+                offset = WINDOW_BYTES - GROUPED_BYTES // 2
                 grouped = reuse.tile([P, CHUNK, PACK], BF16, name="grouped_first", offset=offset, align_bytes=64)
             else:
                 grouped = keep.tile([P, CHUNK, PACK], BF16, name="grouped", tag="grouped%d" % chunk, align_bytes=64)
             for u in range(UNITS):
-                turned = psum.tile([P, PACK, UNIT], F32, name="turned", tag="bank_%s%d" % (TURN_BANKS[chunk], u))
+                turned = psum.tile([P, PACK, UNIT], F32, name="turned", tag="dede"[chunk] + str(u))
                 for t in range(PACK):
                     nc.tensor.transpose(turned[:, t, :], act[:, u, t, :], ident[:])
                 if chunk == 0 and u == 0:
@@ -212,9 +187,10 @@ def tile_list_msg_silu_none_kernel(
             edges = slice(chunk * CHUNK, (chunk + 1) * CHUNK)
             nc.vector.quantize_mx(h_w[:, edges].bitcast(FP8X4), h_sc[:, edges], grouped[:].rearrange("p n t -> p (n t)"))
 
-        def second_layer(n_tiles, first, last, bank, tag):
+        def scatter(n_tiles, first_chunk, last_chunk, bank, tag=""):
+            first, last = first_chunk * CHUNK, last_chunk * CHUNK
             width = last - first
-            prod = psum.tile([P, len(n_tiles), width], F32, name="prod", tag="bank_" + bank)
+            prod = psum.tile([P, len(n_tiles), width], F32, name="prod", tag=bank)
             for i, n_tile in enumerate(n_tiles):
                 m = slice(n_tile * P, (n_tile + 1) * P)
                 nc.tensor.matmul_mx(
@@ -238,21 +214,24 @@ def tile_list_msg_silu_none_kernel(
                 if last == J:
                     nc.sync.dma_start(out[n_tile * P : (n_tile + 1) * P, :], windows[n_tile][:])
 
-        gather_words(((1, DST, 0, CHUNK), (1, SRC, 0, CHUNK)), tag="first_words")
-        gather_words(((1, DST, CHUNK, J), (1, SRC, CHUNK, LAST)))
-        gather_words(((0, DST, HALF, J),), spare=SPARE)
+        gather_scales(0, nc.scalar)
+        nc.sync.dma_start(sm_sb[:], sm.rearrange("(p t) -> p t", t=PACK))
+        nc.sync.dma_start(wd_w[:], wd_words[0].rearrange("p n i -> p (n i)").bitcast(I32))
+        for q in range(QUADS):
+            nc.sync.dma_start(wd_sc[32 * q : 32 * q + ROWS, :], wd_scales[0, 4 * q : 4 * q + 4, :].bitcast(I32))
+        nc.sync.dma_start(wgo_sb[:], wgo)
 
-        def scatter(n_tiles, first, last, bank, tag=""):
-            second_layer(n_tiles, first * CHUNK, last * CHUNK, bank, tag)
+        gather_words(((0, DST, 0, EARLY_DST), (0, SRC, 0, HALF)))
+        gather_words(((1, DST, 0, CHUNK), (1, SRC, 0, CHUNK)), tag="first_words")
+        gather_words(((1, DST, CHUNK, J), (1, SRC, CHUNK, J)))
 
         act = first_layer(0)
-        gather_scales(1, tag="first_words")
+        gather_scales(1, nc.sync, tag="first_words")
         quantize_hidden(0, scale_hidden(0, act))
-        gather_words(((0, SRC, HALF, J), (1, SRC, LAST, J)), tag="hidden0")
-        for n in range(EARLY_WINDOWS, N_TILES):
-            offset = TABLE_BYTES + (n - EARLY_WINDOWS) * WINDOW_BYTES
-            windows.append(reuse.tile([P, T], F32, name="window%d" % n, offset=offset))
-            nc.gpsimd.memset(windows[n][:], 0.0)
+        gather_words(((0, SRC, HALF, J), (0, DST, EARLY_DST, J)), tag="hidden0")
+        for n in range(2):
+            windows.append(reuse.tile([P, T], F32, name="window%d" % (n + 2), offset=n * WINDOW_BYTES))
+            nc.gpsimd.memset(windows[n + 2][:], 0.0)
         act = first_layer(1)
         scatter((0,), 0, 1, "f0")
         scatter((1,), 0, 1, "f1")

@@ -74,7 +74,6 @@ def tile_list_msg_silu_none_kernel(
                 )
 
         nc.gpsimd.memset(wt_sc[:], 0)
-        load_weight_scales(wt_sc, wt_scales, nc.scalar)
         nc.gpsimd.memset(ws_sc[:], 0)
         load_weight_scales(ws_sc, ws_scales, nc.gpsimd)
         nc.vector.memset(tab_sc[0:FIRST_ROW, :], 0)
@@ -88,11 +87,10 @@ def tile_list_msg_silu_none_kernel(
         nc.sync.dma_start(dst_list[:], offs2)
         nc.sync.dma_start(tab_sc[FIRST_ROW:P, :], tab_scales.rearrange("a q t -> q a t").bitcast(I32))
         nc.sync.dma_start(src_list[:], offs)
+        load_weight_scales(wt_sc, wt_scales, nc.sync)
         nc.sync.dma_start(tab_w[0][:], tab_words[0].rearrange("p t i -> p (t i)").bitcast(I32))
         nc.sync.dma_start(wt_w[:], wt_words.rearrange("a p b -> p a b").bitcast(I32))
         nc.sync.dma_start(tab_w[1][:], tab_words[1].rearrange("p t i -> p (t i)").bitcast(I32))
-        for a in range(PASSES):
-            nc.sync.dma_start(ws_w[a][:], ws_words[a].rearrange("p r i -> p (r i)").bitcast(I32))
 
         picked_w = {}
 
@@ -126,11 +124,8 @@ def tile_list_msg_silu_none_kernel(
             else:
                 both = sums.tile([P, UNITS, R], F32, name="acc", offset=0)
                 acc = [both[:, u, :] for u in range(UNITS)]
-            order = ((0, DST), (0, SRC), (1, DST), (1, SRC))
-            steps = [(u, a, side) for u in range(UNITS) for a, side in order]
-            if chunk == 0:
-                steps = sorted(steps, key=lambda step: step[1:] != order[0])
-            for u, a, side in steps:
+            order = ((0, DST), (1, DST), (0, SRC), (1, SRC))
+            for u, a, side in [(u, a, side) for u in range(UNITS) for a, side in order]:
                 half, start = divmod(chunk * CHUNK + u * UNIT, HALF)
                 edge_sc = planes[half][:, a, :].bitcast(U8)[:, side * HALF + start : side * HALF + start + UNIT]
                 if side == SRC:
@@ -214,7 +209,9 @@ def tile_list_msg_silu_none_kernel(
                 if last == J:
                     nc.sync.dma_start(out[n_tile * P : (n_tile + 1) * P, :], windows[n_tile][:])
 
-        gather_scales(0, nc.scalar)
+        gather_scales(0, nc.sync)
+        for a in range(PASSES):
+            nc.sync.dma_start(ws_w[a][:], ws_words[a].rearrange("p r i -> p (r i)").bitcast(I32))
         nc.sync.dma_start(sm_sb[:], sm.rearrange("(p t) -> p t", t=PACK))
         nc.sync.dma_start(wd_w[:], wd_words[0].rearrange("p n i -> p (n i)").bitcast(I32))
         for q in range(QUADS):

@@ -33,7 +33,7 @@ FIRST_ROW = P - SCALE_ROWS
 WINDOW_BYTES = T * 4
 GROUPED_BYTES = CHUNK * PACK * 2
 BANK_BYTES = 2048
-EARLY_DST = 3 * CHUNK
+LAST = J - CHUNK
 
 
 def tile_list_msg_silu_none_kernel(
@@ -84,11 +84,11 @@ def tile_list_msg_silu_none_kernel(
         for window in windows:
             nc.gpsimd.memset(window[:], 0.0)
 
-        nc.sync.dma_start(dst_list[:], offs2)
         nc.sync.dma_start(tab_sc[FIRST_ROW:P, :], tab_scales.rearrange("a q t -> q a t").bitcast(I32))
+        nc.sync.dma_start(dst_list[:], offs2)
         nc.sync.dma_start(src_list[:], offs)
-        load_weight_scales(wt_sc, wt_scales, nc.sync)
         nc.sync.dma_start(tab_w[0][:], tab_words[0].rearrange("p t i -> p (t i)").bitcast(I32))
+        load_weight_scales(wt_sc, wt_scales, nc.sync)
         nc.sync.dma_start(wt_w[:], wt_words.rearrange("a p b -> p a b").bitcast(I32))
         nc.sync.dma_start(tab_w[1][:], tab_words[1].rearrange("p t i -> p (t i)").bitcast(I32))
 
@@ -218,14 +218,14 @@ def tile_list_msg_silu_none_kernel(
             nc.sync.dma_start(wd_sc[32 * q : 32 * q + ROWS, :], wd_scales[0, 4 * q : 4 * q + 4, :].bitcast(I32))
         nc.sync.dma_start(wgo_sb[:], wgo)
 
-        gather_words(((0, DST, 0, EARLY_DST), (0, SRC, 0, HALF)))
+        gather_words(((0, DST, 0, HALF), (0, SRC, 0, LAST)))
         gather_words(((1, DST, 0, CHUNK), (1, SRC, 0, CHUNK)), tag="first_words")
         gather_words(((1, DST, CHUNK, J), (1, SRC, CHUNK, J)))
 
         act = first_layer(0)
         gather_scales(1, nc.sync, tag="first_words")
         quantize_hidden(0, scale_hidden(0, act))
-        gather_words(((0, SRC, HALF, J), (0, DST, EARLY_DST, J)), tag="hidden0")
+        gather_words(((0, DST, HALF, J), (0, SRC, LAST, J)), tag="hidden0")
         for n in range(2):
             windows.append(reuse.tile([P, T], F32, name="window%d" % (n + 2), offset=n * WINDOW_BYTES))
             nc.gpsimd.memset(windows[n + 2][:], 0.0)

@@ -34,6 +34,7 @@ WINDOW_BYTES = T * 4
 GROUPED_BYTES = CHUNK * PACK * 2
 BANK_BYTES = 2048
 LAST = J - CHUNK
+WARM_UPS = 3
 
 
 def tile_list_msg_silu_none_kernel(
@@ -43,6 +44,9 @@ def tile_list_msg_silu_none_kernel(
     with ExitStack() as ctx:
         keep = ctx.enter_context(tc.tile_pool(name="keep", bufs=1))
         reuse = ctx.enter_context(tc.tile_pool(name="reuse", bufs=1))
+        late = ctx.enter_context(tc.tile_pool(name="late", bufs=1))
+        middle = ctx.enter_context(tc.tile_pool(name="middle", bufs=1))
+        early = ctx.enter_context(tc.tile_pool(name="early", bufs=1))
         work = ctx.enter_context(tc.tile_pool(name="work", bufs=2))
         psum = ctx.enter_context(tc.psum_pool(name="psum", bufs=1))
         sums = ctx.enter_context(tc.psum_pool(name="sums", bufs=1))
@@ -94,8 +98,11 @@ def tile_list_msg_silu_none_kernel(
 
         picked_w = {}
 
-        def gather_scales(half, queue, tag=""):
-            picked = keep.tile([P, 2, HALF], U8, name="picked_sc%d" % half, tag=tag, align_bytes=64)
+        def gather_scales(half, queue):
+            if half == 0:
+                picked = keep.tile([P, 2, HALF], U8, name="picked_sc0", align_bytes=64)
+            else:
+                picked = early.tile([P, 2, HALF], U8, name="picked_sc1", offset=0, align_bytes=64)
             entries = slice(half * HALF // 16, (half + 1) * HALF // 16)
             for side in (DST, SRC):
                 nc.vector.tensor_copy(picked[:, side, :], tab_sc[:].bitcast(U8).indirect(lists[side][:, entries]))
@@ -106,9 +113,12 @@ def tile_list_msg_silu_none_kernel(
                     picked[rows, :, :].rearrange("p s e -> p (s e)").bitcast(I32),
                 )
 
-        def gather_words(parts, tag=""):
+        def gather_words(parts, tag="", offset=None):
             total = sum(last - first for a, side, first, last in parts)
-            picked = keep.tile([P, total], U32, name="picked_w%d_%d_%d_%d" % parts[0], tag=tag, align_bytes=64)
+            if offset is None:
+                picked = keep.tile([P, total], U32, name="picked_w%d_%d_%d_%d" % parts[0], tag=tag, align_bytes=64)
+            else:
+                picked = early.tile([P, total], U32, name="picked_w%d_%d_%d_%d" % parts[0], offset=offset, align_bytes=64)
             at = 0
             for a, side, first, last in parts:
                 window = tab_w[a][:].bitcast(U32)
@@ -118,14 +128,22 @@ def tile_list_msg_silu_none_kernel(
                 at = at + last - first
 
         def first_layer(chunk):
-            act = work.tile([P, UNITS, PACK, P], F32, name="act")
-            if chunk == 0:
-                acc = [sums.tile([P, R], F32, name="acc_unit%d" % u, offset=u * BANK_BYTES)[:] for u in range(UNITS)]
+            if chunk == 2:
+                act = middle.tile([P, UNITS, PACK, P], F32, name="act_held", offset=512)
+            else:
+                act = work.tile([P, UNITS, PACK, P], F32, name="act")
+            if chunk in (0, 2):
+                acc = [sums.tile([P, R], F32, name="acc%d_%d" % (chunk, u), offset=u * BANK_BYTES)[:] for u in range(UNITS)]
+            elif chunk == 3:
+                acc = [psum.tile([P, R], F32, name="acc_last", tag="f%d" % u)[:] for u in range(UNITS)]
             else:
                 both = sums.tile([P, UNITS, R], F32, name="acc", offset=0)
                 acc = [both[:, u, :] for u in range(UNITS)]
-            order = ((0, DST), (1, DST), (0, SRC), (1, SRC))
-            for u, a, side in [(u, a, side) for u in range(UNITS) for a, side in order]:
+            order = ((0, DST), (1, DST), (0, SRC), (1, SRC)) if chunk < 2 else ((1, DST), (1, SRC), (0, SRC), (0, DST))
+            steps = [(u, a, side) for u in range(UNITS) for a, side in order]
+            if chunk == 0:
+                steps.insert(1, steps.pop(len(order)))
+            for u, a, side in steps:
                 half, start = divmod(chunk * CHUNK + u * UNIT, HALF)
                 edge_sc = planes[half][:, a, :].bitcast(U8)[:, side * HALF + start : side * HALF + start + UNIT]
                 if side == SRC:
@@ -146,7 +164,12 @@ def tile_list_msg_silu_none_kernel(
             return act
 
         def scale_hidden(chunk, act):
-            hidden = keep.tile([P, PACK, CHUNK], BF16, name="hidden", tag="hidden%d" % chunk, align_bytes=64)
+            if chunk == 1:
+                hidden = middle.tile([P, PACK, CHUNK], BF16, name="hidden_middle", offset=4096, align_bytes=64)
+            elif chunk == 3:
+                hidden = late.tile([P, PACK, CHUNK], BF16, name="hidden_last", offset=0, align_bytes=64)
+            else:
+                hidden = keep.tile([P, PACK, CHUNK], BF16, name="hidden", tag="hidden%d" % chunk, align_bytes=64)
             if chunk == 0:
                 offset = WINDOW_BYTES - GROUPED_BYTES // 2
                 grouped = reuse.tile([P, CHUNK, PACK], BF16, name="grouped_first", offset=offset, align_bytes=64)
@@ -182,32 +205,35 @@ def tile_list_msg_silu_none_kernel(
             edges = slice(chunk * CHUNK, (chunk + 1) * CHUNK)
             nc.vector.quantize_mx(h_w[:, edges].bitcast(FP8X4), h_sc[:, edges], grouped[:].rearrange("p n t -> p (n t)"))
 
+        def second_layer(prod, n_tile, first, last):
+            m = slice(n_tile * P, (n_tile + 1) * P)
+            nc.tensor.matmul_mx(
+                prod,
+                lhsT=wd_w[:, m].bitcast(FP8X4),
+                lhsT_scale=wd_sc[:].bitcast(U8)[:, m],
+                rhs=h_w[:, first:last].bitcast(FP8X4),
+                rhs_scale=h_sc[:, first:last],
+                start=True,
+                stop=True,
+            )
+
+        def place(n_tile, first, last, message):
+            nc.vector.tensor_tensor(
+                windows[n_tile][:].indirect(dst_list[:, first // 16 : last // 16]), message, wgo_sb[:, first:last], MULT
+            )
+            if last == J:
+                nc.sync.dma_start(out[n_tile * P : (n_tile + 1) * P, :], windows[n_tile][:])
+
         def scatter(n_tiles, first_chunk, last_chunk, bank, tag=""):
             first, last = first_chunk * CHUNK, last_chunk * CHUNK
             width = last - first
             prod = psum.tile([P, len(n_tiles), width], F32, name="prod", tag=bank)
             for i, n_tile in enumerate(n_tiles):
-                m = slice(n_tile * P, (n_tile + 1) * P)
-                nc.tensor.matmul_mx(
-                    prod[:, i, :],
-                    lhsT=wd_w[:, m].bitcast(FP8X4),
-                    lhsT_scale=wd_sc[:].bitcast(U8)[:, m],
-                    rhs=h_w[:, first:last].bitcast(FP8X4),
-                    rhs_scale=h_sc[:, first:last],
-                    start=True,
-                    stop=True,
-                )
+                second_layer(prod[:, i, :], n_tile, first, last)
             message = keep.tile([P, len(n_tiles), width], F32, name="y%d_%d" % (n_tiles[0], first), tag=tag, align_bytes=64)
             for i, n_tile in enumerate(n_tiles):
                 nc.scalar.copy(message[:, i, :], prod[:, i, :])
-                nc.vector.tensor_tensor(
-                    windows[n_tile][:].indirect(dst_list[:, first // 16 : last // 16]),
-                    message[:, i, :],
-                    wgo_sb[:, first:last],
-                    MULT,
-                )
-                if last == J:
-                    nc.sync.dma_start(out[n_tile * P : (n_tile + 1) * P, :], windows[n_tile][:])
+                place(n_tile, first, last, message[:, i, :])
 
         gather_scales(0, nc.sync)
         for a in range(PASSES):
@@ -218,12 +244,24 @@ def tile_list_msg_silu_none_kernel(
             nc.sync.dma_start(wd_sc[32 * q : 32 * q + ROWS, :], wd_scales[0, 4 * q : 4 * q + 4, :].bitcast(I32))
         nc.sync.dma_start(wgo_sb[:], wgo)
 
+        idle = psum.tile([P, R], F32, name="idle", tag="f1")
+        for u in range(WARM_UPS):
+            nc.tensor.matmul_mx(
+                idle[:],
+                lhsT=tab_w[0][:, u * UNIT : (u + 1) * UNIT].bitcast(FP8X4),
+                lhsT_scale=tab_sc[:].bitcast(U8)[:, u * UNIT : (u + 1) * UNIT],
+                rhs=wt_w[:, 0, :].bitcast(FP4X4),
+                rhs_scale=wt_sc[:, 0, :].bitcast(U8),
+                start=True,
+                stop=True,
+            )
         gather_words(((0, DST, 0, HALF), (0, SRC, 0, LAST)))
-        gather_words(((1, DST, 0, CHUNK), (1, SRC, 0, CHUNK)), tag="first_words")
-        gather_words(((1, DST, CHUNK, J), (1, SRC, CHUNK, J)))
+        gather_words(((1, DST, 0, CHUNK), (1, SRC, 0, CHUNK)), offset=0)
+        gather_words(((1, DST, CHUNK, J), (1, SRC, CHUNK, HALF)))
 
         act = first_layer(0)
-        gather_scales(1, nc.sync, tag="first_words")
+        gather_scales(1, nc.sync)
+        gather_words(((1, SRC, HALF, J),), offset=2 * HALF)
         quantize_hidden(0, scale_hidden(0, act))
         gather_words(((0, DST, HALF, J), (0, SRC, LAST, J)), tag="hidden0")
         for n in range(2):
@@ -233,13 +271,37 @@ def tile_list_msg_silu_none_kernel(
         scatter((0,), 0, 1, "f0")
         scatter((1,), 0, 1, "f1")
         quantize_hidden(1, scale_hidden(1, act))
-        scatter((2, 3), 0, 1, "e1", "hidden1")
-        hidden = scale_hidden(2, first_layer(2))
-        scatter((0, 1), 1, 2, "d0")
+        prod = psum.tile([P, CHUNK], F32, name="prod_first_cover", tag="e1")
+        second_layer(prod[:], 2, 0, CHUNK)
+        message = middle.tile([P, CHUNK], F32, name="y_first_cover", offset=4608, align_bytes=64)
+        nc.scalar.copy(message[:], prod[:])
+        place(2, 0, CHUNK, message[:])
+        wide = middle.tile([P, HALF], F32, name="y_wide", offset=5632, align_bytes=64)
+        prod = psum.tile([P, CHUNK], F32, name="prod_wide", tag="e0")
+        second_layer(prod[:], 3, 0, CHUNK)
+        nc.scalar.copy(wide[:, :CHUNK], prod[:])
+        act = first_layer(2)
+        prod = sums.tile([P, CHUNK], F32, name="prod_wide_rest", offset=0)
+        second_layer(prod[:], 3, CHUNK, HALF)
+        nc.scalar.copy(wide[:, CHUNK:], prod[:])
+        place(3, 0, HALF, wide[:])
+        hidden = scale_hidden(2, act)
+        scatter((0,), 1, 2, "d0")
+        act = first_layer(3)
         quantize_hidden(2, hidden)
-        scatter((2, 3), 1, 2, "d1", "hidden2")
-        quantize_hidden(3, scale_hidden(3, first_layer(3)))
-        scatter((0, 1), 2, 3, "e1", "hidden3")
-        scatter((2,), 2, 4, "f0")
-        scatter((0, 1), 3, 4, "f1")
-        scatter((3,), 2, 4, "d0")
+        scatter((1,), 1, 2, "d1", "hidden2")
+        quantize_hidden(3, scale_hidden(3, act))
+        prod = psum.tile([P, CHUNK], F32, name="prod_cover", tag="d0")
+        second_layer(prod[:], 2, CHUNK, HALF)
+        message = late.tile([P, CHUNK], F32, name="y_cover", offset=0, align_bytes=64)
+        nc.scalar.copy(message[:], prod[:])
+        place(2, CHUNK, HALF, message[:])
+        message = late.tile([P, HALF], F32, name="y_halves", offset=CHUNK * 4, align_bytes=64)
+        for first, bank in ((HALF, "e1"), (LAST, "e0")):
+            prod = psum.tile([P, CHUNK], F32, name="prod_half", tag=bank)
+            second_layer(prod[:], 0, first, first + CHUNK)
+            nc.scalar.copy(message[:, first - HALF : first - HALF + CHUNK], prod[:])
+        place(0, HALF, J, message[:])
+        scatter((1,), 2, 4, "f0")
+        scatter((2,), 2, 4, "f1")
+        scatter((3,), 2, 4, "d1")

@@ -34,7 +34,9 @@ WINDOW_BYTES = T * 4
 GROUPED_BYTES = CHUNK * PACK * 2
 BANK_BYTES = 2048
 LAST = J - CHUNK
-WARM_UPS = 3
+WARM_UPS = 2
+SUM_BANKS = (("a0", "a1"), ("a1", "d0"), ("a1", "d0"), ("e0", "e1"))
+TURN_BANKS = (("d0", "d1"), ("e0", "e1"), ("a0", "d1"), ("f0", "f1"))
 
 
 def tile_list_msg_silu_none_kernel(
@@ -127,18 +129,17 @@ def tile_list_msg_silu_none_kernel(
                     picked_w[edge // UNIT, a, side] = picked[:, at + edge - first : at + edge - first + UNIT]
                 at = at + last - first
 
+        def bank(name, shape, where):
+            if where[0] == "a":
+                return sums.tile(shape, F32, name=name, offset=int(where[1]) * BANK_BYTES)
+            return psum.tile(shape, F32, name=name, tag=where)
+
         def first_layer(chunk):
             if chunk == 2:
                 act = middle.tile([P, UNITS, PACK, P], F32, name="act_held", offset=512)
             else:
                 act = work.tile([P, UNITS, PACK, P], F32, name="act")
-            if chunk in (0, 2):
-                acc = [sums.tile([P, R], F32, name="acc%d_%d" % (chunk, u), offset=u * BANK_BYTES)[:] for u in range(UNITS)]
-            elif chunk == 3:
-                acc = [psum.tile([P, R], F32, name="acc_last", tag="f%d" % u)[:] for u in range(UNITS)]
-            else:
-                both = sums.tile([P, UNITS, R], F32, name="acc", offset=0)
-                acc = [both[:, u, :] for u in range(UNITS)]
+            acc = [bank("acc%d_%d" % (chunk, u), [P, R], SUM_BANKS[chunk][u])[:] for u in range(UNITS)]
             order = ((0, DST), (1, DST), (0, SRC), (1, SRC)) if chunk < 2 else ((1, DST), (1, SRC), (0, SRC), (0, DST))
             steps = [(u, a, side) for u in range(UNITS) for a, side in order]
             if chunk == 0:
@@ -163,7 +164,7 @@ def tile_list_msg_silu_none_kernel(
                 nc.scalar.activation(act[:, u, :, :], acc[u].rearrange("e (m t) -> e t m", t=PACK), SILU)
             return act
 
-        def scale_hidden(chunk, act):
+        def scale_hidden(chunk, act, between):
             if chunk == 1:
                 hidden = middle.tile([P, PACK, CHUNK], BF16, name="hidden_middle", offset=4096, align_bytes=64)
             elif chunk == 3:
@@ -176,7 +177,7 @@ def tile_list_msg_silu_none_kernel(
             else:
                 grouped = keep.tile([P, CHUNK, PACK], BF16, name="grouped", tag="grouped%d" % chunk, align_bytes=64)
             for u in range(UNITS):
-                turned = psum.tile([P, PACK, UNIT], F32, name="turned", tag="dede"[chunk] + str(u))
+                turned = bank("turned%d_%d" % (chunk, u), [P, PACK, UNIT], TURN_BANKS[chunk][u])
                 for t in range(PACK):
                     nc.tensor.transpose(turned[:, t, :], act[:, u, t, :], ident[:])
                 if chunk == 0 and u == 0:
@@ -193,6 +194,8 @@ def tile_list_msg_silu_none_kernel(
                     nc.scalar.activation(
                         hidden[:, t, u * UNIT : (u + 1) * UNIT], turned[:, t, :], COPY, scale=sm_sb[:, t : t + 1]
                     )
+                    if (u, t) in between:
+                        between[u, t]()
             return hidden, grouped
 
         def quantize_hidden(chunk, tiles):
@@ -224,16 +227,21 @@ def tile_list_msg_silu_none_kernel(
             if last == J:
                 nc.sync.dma_start(out[n_tile * P : (n_tile + 1) * P, :], windows[n_tile][:])
 
-        def scatter(n_tiles, first_chunk, last_chunk, bank, tag=""):
+        def scatter(n_tiles, first_chunk, last_chunk, where, tag=""):
             first, last = first_chunk * CHUNK, last_chunk * CHUNK
             width = last - first
-            prod = psum.tile([P, len(n_tiles), width], F32, name="prod", tag=bank)
+            prod = bank("prod%d_%d" % (n_tiles[0], first), [P, len(n_tiles), width], where)
             for i, n_tile in enumerate(n_tiles):
                 second_layer(prod[:, i, :], n_tile, first, last)
             message = keep.tile([P, len(n_tiles), width], F32, name="y%d_%d" % (n_tiles[0], first), tag=tag, align_bytes=64)
             for i, n_tile in enumerate(n_tiles):
                 nc.scalar.copy(message[:, i, :], prod[:, i, :])
                 place(n_tile, first, last, message[:, i, :])
+
+        def message_part(message, n_tile, first, last, where):
+            prod = bank("part%d_%d" % (n_tile, first), [P, last - first], where)
+            second_layer(prod[:], n_tile, first, last)
+            nc.scalar.copy(message, prod[:])
 
         gather_scales(0, nc.sync)
         for a in range(PASSES):
@@ -245,63 +253,60 @@ def tile_list_msg_silu_none_kernel(
         nc.sync.dma_start(wgo_sb[:], wgo)
 
         idle = psum.tile([P, R], F32, name="idle", tag="f1")
-        for u in range(WARM_UPS):
-            nc.tensor.matmul_mx(
-                idle[:],
-                lhsT=tab_w[0][:, u * UNIT : (u + 1) * UNIT].bitcast(FP8X4),
-                lhsT_scale=tab_sc[:].bitcast(U8)[:, u * UNIT : (u + 1) * UNIT],
-                rhs=wt_w[:, 0, :].bitcast(FP4X4),
-                rhs_scale=wt_sc[:, 0, :].bitcast(U8),
-                start=True,
-                stop=True,
-            )
+
+        def warm_up(words):
+            for u in range(WARM_UPS):
+                nc.tensor.matmul_mx(
+                    idle[:],
+                    lhsT=words[u].bitcast(FP8X4),
+                    lhsT_scale=tab_sc[:].bitcast(U8)[:, u * UNIT : (u + 1) * UNIT],
+                    rhs=wt_w[:, 0, :].bitcast(FP4X4),
+                    rhs_scale=wt_sc[:, 0, :].bitcast(U8),
+                    start=True,
+                    stop=True,
+                )
+
+        warm_up([tab_w[0][:, u * UNIT : (u + 1) * UNIT] for u in range(WARM_UPS)])
         gather_words(((0, DST, 0, HALF), (0, SRC, 0, LAST)))
+        warm_up([picked_w[u, 0, DST] for u in range(WARM_UPS)])
         gather_words(((1, DST, 0, CHUNK), (1, SRC, 0, CHUNK)), offset=0)
         gather_words(((1, DST, CHUNK, J), (1, SRC, CHUNK, HALF)))
 
         act = first_layer(0)
         gather_scales(1, nc.sync)
         gather_words(((1, SRC, HALF, J),), offset=2 * HALF)
-        quantize_hidden(0, scale_hidden(0, act))
+        quantize_hidden(0, scale_hidden(0, act, {}))
         gather_words(((0, DST, HALF, J), (0, SRC, LAST, J)), tag="hidden0")
         for n in range(2):
             windows.append(reuse.tile([P, T], F32, name="window%d" % (n + 2), offset=n * WINDOW_BYTES))
             nc.gpsimd.memset(windows[n + 2][:], 0.0)
         act = first_layer(1)
-        scatter((0,), 0, 1, "f0")
-        scatter((1,), 0, 1, "f1")
-        quantize_hidden(1, scale_hidden(1, act))
-        prod = psum.tile([P, CHUNK], F32, name="prod_first_cover", tag="e1")
-        second_layer(prod[:], 2, 0, CHUNK)
+        first_messages = {(0, 1): lambda: scatter((0,), 0, 1, "a1"), (0, 3): lambda: scatter((1,), 0, 1, "d0")}
+        quantize_hidden(1, scale_hidden(1, act, first_messages))
         message = middle.tile([P, CHUNK], F32, name="y_first_cover", offset=4608, align_bytes=64)
-        nc.scalar.copy(message[:], prod[:])
+        message_part(message[:], 2, 0, CHUNK, "e1")
         place(2, 0, CHUNK, message[:])
         wide = middle.tile([P, HALF], F32, name="y_wide", offset=5632, align_bytes=64)
-        prod = psum.tile([P, CHUNK], F32, name="prod_wide", tag="e0")
-        second_layer(prod[:], 3, 0, CHUNK)
-        nc.scalar.copy(wide[:, :CHUNK], prod[:])
+        message_part(wide[:, :CHUNK], 3, 0, CHUNK, "e0")
         act = first_layer(2)
-        prod = sums.tile([P, CHUNK], F32, name="prod_wide_rest", offset=0)
-        second_layer(prod[:], 3, CHUNK, HALF)
-        nc.scalar.copy(wide[:, CHUNK:], prod[:])
-        place(3, 0, HALF, wide[:])
-        hidden = scale_hidden(2, act)
-        scatter((0,), 1, 2, "d0")
+
+        def finish_wide():
+            message_part(wide[:, CHUNK:], 3, CHUNK, HALF, "a1")
+            place(3, 0, HALF, wide[:])
+
+        hidden = scale_hidden(2, act, {(0, 3): finish_wide})
+        scatter((0,), 1, 2, "a0")
         act = first_layer(3)
         quantize_hidden(2, hidden)
         scatter((1,), 1, 2, "d1", "hidden2")
-        quantize_hidden(3, scale_hidden(3, act))
-        prod = psum.tile([P, CHUNK], F32, name="prod_cover", tag="d0")
-        second_layer(prod[:], 2, CHUNK, HALF)
+        quantize_hidden(3, scale_hidden(3, act, {}))
         message = late.tile([P, CHUNK], F32, name="y_cover", offset=0, align_bytes=64)
-        nc.scalar.copy(message[:], prod[:])
+        message_part(message[:], 2, CHUNK, HALF, "d0")
         place(2, CHUNK, HALF, message[:])
         message = late.tile([P, HALF], F32, name="y_halves", offset=CHUNK * 4, align_bytes=64)
-        for first, bank in ((HALF, "e1"), (LAST, "e0")):
-            prod = psum.tile([P, CHUNK], F32, name="prod_half", tag=bank)
-            second_layer(prod[:], 0, first, first + CHUNK)
-            nc.scalar.copy(message[:, first - HALF : first - HALF + CHUNK], prod[:])
+        message_part(message[:, :CHUNK], 0, HALF, LAST, "f1")
+        message_part(message[:, CHUNK:], 0, LAST, J, "f0")
         place(0, HALF, J, message[:])
-        scatter((1,), 2, 4, "f0")
-        scatter((2,), 2, 4, "f1")
-        scatter((3,), 2, 4, "d1")
+        scatter((1,), 2, 4, "e0")
+        scatter((2,), 2, 4, "e1")
+        scatter((3,), 2, 4, "a1")

@@ -34,7 +34,7 @@ WINDOW_BYTES = T * 4
 GROUPED_BYTES = CHUNK * PACK * 2
 BANK_BYTES = 2048
 LAST = J - CHUNK
-WARM_UPS = 2
+WARM_UPS = 3
 SUM_BANKS = (("a0", "a1"), ("a1", "d0"), ("a1", "d0"), ("e0", "e1"))
 TURN_BANKS = (("d0", "d1"), ("e0", "e1"), ("a0", "d1"), ("f0", "f1"))
 
@@ -160,6 +160,16 @@ def tile_list_msg_silu_none_kernel(
                     start=(a, side) == order[0],
                     stop=(a, side) == order[-1],
                 )
+            if chunk == 0:
+                nc.tensor.matmul_mx(
+                    idle[:],
+                    lhsT=picked_w[u, a, side].bitcast(FP8X4),
+                    lhsT_scale=edge_sc,
+                    rhs=weight,
+                    rhs_scale=weight_sc.bitcast(U8),
+                    start=True,
+                    stop=True,
+                )
             for u in range(UNITS):
                 nc.scalar.activation(act[:, u, :, :], acc[u].rearrange("e (m t) -> e t m", t=PACK), SILU)
             return act
@@ -253,22 +263,17 @@ def tile_list_msg_silu_none_kernel(
         nc.sync.dma_start(wgo_sb[:], wgo)
 
         idle = psum.tile([P, R], F32, name="idle", tag="f1")
-
-        def warm_up(words):
-            for u in range(WARM_UPS):
-                nc.tensor.matmul_mx(
-                    idle[:],
-                    lhsT=words[u].bitcast(FP8X4),
-                    lhsT_scale=tab_sc[:].bitcast(U8)[:, u * UNIT : (u + 1) * UNIT],
-                    rhs=wt_w[:, 0, :].bitcast(FP4X4),
-                    rhs_scale=wt_sc[:, 0, :].bitcast(U8),
-                    start=True,
-                    stop=True,
-                )
-
-        warm_up([tab_w[0][:, u * UNIT : (u + 1) * UNIT] for u in range(WARM_UPS)])
+        for u in range(WARM_UPS):
+            nc.tensor.matmul_mx(
+                idle[:],
+                lhsT=tab_w[0][:, u * UNIT : (u + 1) * UNIT].bitcast(FP8X4),
+                lhsT_scale=tab_sc[:].bitcast(U8)[:, u * UNIT : (u + 1) * UNIT],
+                rhs=wt_w[:, 0, :].bitcast(FP4X4),
+                rhs_scale=wt_sc[:, 0, :].bitcast(U8),
+                start=True,
+                stop=True,
+            )
         gather_words(((0, DST, 0, HALF), (0, SRC, 0, LAST)))
-        warm_up([picked_w[u, 0, DST] for u in range(WARM_UPS)])
         gather_words(((1, DST, 0, CHUNK), (1, SRC, 0, CHUNK)), offset=0)
         gather_words(((1, DST, CHUNK, J), (1, SRC, CHUNK, HALF)))
 

@@ -35,7 +35,7 @@ GROUPED_BYTES = CHUNK * PACK * 2
 BANK_BYTES = 2048
 LAST = J - CHUNK
 WARM_UPS = 3
-SUM_BANKS = (("a0", "a1"), ("a1", "d0"), ("a1", "d0"), ("e0", "e1"))
+SUM_BANKS = (("a0", "a1"), ("a1", "d0"), ("a1", "d0"), ("e1", "d0"))
 TURN_BANKS = (("d0", "d1"), ("e0", "e1"), ("a0", "d1"), ("f0", "f1"))
 
 
@@ -134,14 +134,14 @@ def tile_list_msg_silu_none_kernel(
                 return sums.tile(shape, F32, name=name, offset=int(where[1]) * BANK_BYTES)
             return psum.tile(shape, F32, name=name, tag=where)
 
-        def first_layer(chunk):
+        def first_layer(chunk, units=(0, 1), act=None):
             if chunk == 2:
                 act = middle.tile([P, UNITS, PACK, P], F32, name="act_held", offset=512)
-            else:
+            elif act is None:
                 act = work.tile([P, UNITS, PACK, P], F32, name="act")
-            acc = [bank("acc%d_%d" % (chunk, u), [P, R], SUM_BANKS[chunk][u])[:] for u in range(UNITS)]
+            acc = {u: bank("acc%d_%d" % (chunk, u), [P, R], SUM_BANKS[chunk][u])[:] for u in units}
             order = ((0, DST), (1, DST), (0, SRC), (1, SRC)) if chunk < 2 else ((1, DST), (1, SRC), (0, SRC), (0, DST))
-            steps = [(u, a, side) for u in range(UNITS) for a, side in order]
+            steps = [(u, a, side) for u in units for a, side in order]
             if chunk == 0:
                 steps.insert(1, steps.pop(len(order)))
             for u, a, side in steps:
@@ -170,7 +170,7 @@ def tile_list_msg_silu_none_kernel(
                     start=True,
                     stop=True,
                 )
-            for u in range(UNITS):
+            for u in units:
                 nc.scalar.activation(act[:, u, :, :], acc[u].rearrange("e (m t) -> e t m", t=PACK), SILU)
             return act
 
@@ -200,6 +200,8 @@ def tile_list_msg_silu_none_kernel(
                         MULT,
                     )
                     continue
+                if (u, None) in between:
+                    between[u, None]()
                 for t in range(PACK):
                     nc.scalar.activation(
                         hidden[:, t, u * UNIT : (u + 1) * UNIT], turned[:, t, :], COPY, scale=sm_sb[:, t : t + 1]
@@ -286,32 +288,26 @@ def tile_list_msg_silu_none_kernel(
             windows.append(reuse.tile([P, T], F32, name="window%d" % (n + 2), offset=n * WINDOW_BYTES))
             nc.gpsimd.memset(windows[n + 2][:], 0.0)
         act = first_layer(1)
-        first_messages = {(0, 1): lambda: scatter((0,), 0, 1, "a1"), (0, 3): lambda: scatter((1,), 0, 1, "d0")}
+        first_messages = {(0, None): lambda: scatter((0,), 0, 1, "a1"), (0, 3): lambda: scatter((1,), 0, 1, "d0")}
         quantize_hidden(1, scale_hidden(1, act, first_messages))
-        message = middle.tile([P, CHUNK], F32, name="y_first_cover", offset=4608, align_bytes=64)
-        message_part(message[:], 2, 0, CHUNK, "e1")
-        place(2, 0, CHUNK, message[:])
-        wide = middle.tile([P, HALF], F32, name="y_wide", offset=5632, align_bytes=64)
-        message_part(wide[:, :CHUNK], 3, 0, CHUNK, "e0")
+        message = middle.tile([P, 2, CHUNK], F32, name="y_first_cover", offset=4608, align_bytes=64)
+        pair = bank("pair", [P, 2, CHUNK], "e0")
+        for i in range(2):
+            second_layer(pair[:, i, :], 2 + i, 0, CHUNK)
+        for i in range(2):
+            nc.scalar.copy(message[:, i, :], pair[:, i, :])
+            place(2 + i, 0, CHUNK, message[:, i, :])
         act = first_layer(2)
-
-        def finish_wide():
-            message_part(wide[:, CHUNK:], 3, CHUNK, HALF, "a1")
-            place(3, 0, HALF, wide[:])
-
-        hidden = scale_hidden(2, act, {(0, 3): finish_wide})
-        scatter((0,), 1, 2, "a0")
-        act = first_layer(3)
+        last_act = first_layer(3, (0,))
+        hidden = scale_hidden(2, act, {(0, 3): lambda: scatter((0,), 1, 2, "a1")})
+        first_layer(3, (1,), last_act)
         quantize_hidden(2, hidden)
-        scatter((1,), 1, 2, "d1", "hidden2")
-        quantize_hidden(3, scale_hidden(3, act, {}))
-        message = late.tile([P, CHUNK], F32, name="y_cover", offset=0, align_bytes=64)
-        message_part(message[:], 2, CHUNK, HALF, "d0")
-        place(2, CHUNK, HALF, message[:])
-        message = late.tile([P, HALF], F32, name="y_halves", offset=CHUNK * 4, align_bytes=64)
-        message_part(message[:, :CHUNK], 0, HALF, LAST, "f1")
-        message_part(message[:, CHUNK:], 0, LAST, J, "f0")
-        place(0, HALF, J, message[:])
-        scatter((1,), 2, 4, "e0")
-        scatter((2,), 2, 4, "e1")
-        scatter((3,), 2, 4, "a1")
+        scatter((1, 3), 1, 2, "d1", "hidden2")
+        quantize_hidden(3, scale_hidden(3, last_act, {}))
+        message = late.tile([P, HALF], F32, name="y_cover", offset=0, align_bytes=64)
+        message_part(message[:], 2, CHUNK, LAST, "f1")
+        place(2, CHUNK, LAST, message[:])
+        scatter((0,), 2, 4, "f0")
+        scatter((2,), 3, 4, "a1")
+        scatter((1,), 2, 4, "e1")
+        scatter((3,), 2, 4, "e0")

@@ -23,18 +23,24 @@ PACK = 4
 PASSES = K // (P * PACK)
 QUADS = 4
 ROWS = 4
+GROUP = 16
 UNIT = 128
 CHUNK = 256
 UNITS = CHUNK // UNIT
 HALF = J // 2
-DST, SRC = 0, 1
-SCALE_ROWS = PASSES * QUADS * ROWS
-FIRST_ROW = P - SCALE_ROWS
-WINDOW_BYTES = T * 4
-GROUPED_BYTES = CHUNK * PACK * 2
-BANK_BYTES = 2048
 LAST = J - CHUNK
-WARM_UPS = 3
+DST, SRC = 0, 1
+FIRST_ROW = P - PASSES * QUADS * ROWS
+WINDOW_BYTES = T * 4
+HIDDEN_BYTES = CHUNK * PACK * 2
+ACT_BYTES = UNITS * R * 4
+OVERLAP = 512
+BANK_BYTES = 2048
+WARM_UPS = HALF // UNIT
+
+EARLY_ORDER = ((0, DST), (1, DST), (0, SRC), (1, SRC))
+LATE_ORDER = ((1, DST), (1, SRC), (0, SRC), (0, DST))
+
 SUM_BANKS = (("a0", "a1"), ("a1", "d0"), ("a1", "d0"), ("e1", "d0"))
 TURN_BANKS = (("d0", "d1"), ("e0", "e1"), ("a0", "d1"), ("f0", "f1"))
 
@@ -45,16 +51,16 @@ def tile_list_msg_silu_none_kernel(
     nc = tc.nc
     with ExitStack() as ctx:
         keep = ctx.enter_context(tc.tile_pool(name="keep", bufs=1))
-        reuse = ctx.enter_context(tc.tile_pool(name="reuse", bufs=1))
-        late = ctx.enter_context(tc.tile_pool(name="late", bufs=1))
-        middle = ctx.enter_context(tc.tile_pool(name="middle", bufs=1))
-        early = ctx.enter_context(tc.tile_pool(name="early", bufs=1))
+        after_quantize0 = ctx.enter_context(tc.tile_pool(name="after_quantize0", bufs=1))
+        after_hidden3 = ctx.enter_context(tc.tile_pool(name="after_hidden3", bufs=1))
+        after_hidden1 = ctx.enter_context(tc.tile_pool(name="after_hidden1", bufs=1))
+        after_sums0 = ctx.enter_context(tc.tile_pool(name="after_sums0", bufs=1))
         work = ctx.enter_context(tc.tile_pool(name="work", bufs=2))
         psum = ctx.enter_context(tc.psum_pool(name="psum", bufs=1))
         sums = ctx.enter_context(tc.psum_pool(name="sums", bufs=1))
 
-        dst_list = keep.tile([P, J // 16], U16, name="dst_list")
-        src_list = keep.tile([P, J // 16], U16, name="src_list")
+        dst_list = keep.tile([P, J // GROUP], U16, name="dst_list")
+        src_list = keep.tile([P, J // GROUP], U16, name="src_list")
         lists = (dst_list, src_list)
         tab_sc = keep.tile([P, T // 4], I32, name="tab_sc", align_bytes=64)
         tab_w = [keep.tile([P, T], I32, name="tab_w%d" % a, align_bytes=64) for a in range(PASSES)]
@@ -76,7 +82,7 @@ def tile_list_msg_silu_none_kernel(
             for q in range(QUADS):
                 queue.dma_start(
                     tile[32 * q : 32 * q + ROWS, :, :],
-                    scales[:, 4 * q : 4 * q + 4, :].rearrange("a r n -> r a n").bitcast(I32),
+                    scales[:, ROWS * q : ROWS * (q + 1), :].rearrange("a r n -> r a n").bitcast(I32),
                 )
 
         nc.gpsimd.memset(wt_sc[:], 0)
@@ -100,31 +106,24 @@ def tile_list_msg_silu_none_kernel(
 
         picked_w = {}
 
-        def gather_scales(half, queue):
-            if half == 0:
-                picked = keep.tile([P, 2, HALF], U8, name="picked_sc0", align_bytes=64)
-            else:
-                picked = early.tile([P, 2, HALF], U8, name="picked_sc1", offset=0, align_bytes=64)
-            entries = slice(half * HALF // 16, (half + 1) * HALF // 16)
+        def gather_scales(half, picked):
+            entries = slice(half * HALF // GROUP, (half + 1) * HALF // GROUP)
             for side in (DST, SRC):
                 nc.vector.tensor_copy(picked[:, side, :], tab_sc[:].bitcast(U8).indirect(lists[side][:, entries]))
             for q in range(QUADS):
-                rows = slice(FIRST_ROW + 8 * q, FIRST_ROW + 8 * q + 8)
-                queue.dma_start(
+                rows = slice(FIRST_ROW + PASSES * ROWS * q, FIRST_ROW + PASSES * ROWS * (q + 1))
+                nc.sync.dma_start(
                     planes[half][32 * q : 32 * q + ROWS, :, :],
                     picked[rows, :, :].rearrange("p s e -> p (s e)").bitcast(I32),
                 )
 
-        def gather_words(parts, tag="", offset=None):
+        def gather_words(parts, pool, **place_of_tile):
             total = sum(last - first for a, side, first, last in parts)
-            if offset is None:
-                picked = keep.tile([P, total], U32, name="picked_w%d_%d_%d_%d" % parts[0], tag=tag, align_bytes=64)
-            else:
-                picked = early.tile([P, total], U32, name="picked_w%d_%d_%d_%d" % parts[0], offset=offset, align_bytes=64)
+            picked = pool.tile([P, total], U32, name="picked_w%d_%d_%d_%d" % parts[0], align_bytes=64, **place_of_tile)
             at = 0
             for a, side, first, last in parts:
-                window = tab_w[a][:].bitcast(U32)
-                nc.vector.tensor_copy(picked[:, at : at + last - first], window.indirect(lists[side][:, first // 16 : last // 16]))
+                entries = lists[side][:, first // GROUP : last // GROUP]
+                nc.vector.tensor_copy(picked[:, at : at + last - first], tab_w[a][:].bitcast(U32).indirect(entries))
                 for edge in range(first, last, UNIT):
                     picked_w[edge // UNIT, a, side] = picked[:, at + edge - first : at + edge - first + UNIT]
                 at = at + last - first
@@ -134,13 +133,9 @@ def tile_list_msg_silu_none_kernel(
                 return sums.tile(shape, F32, name=name, offset=int(where[1]) * BANK_BYTES)
             return psum.tile(shape, F32, name=name, tag=where)
 
-        def first_layer(chunk, units=(0, 1), act=None):
-            if chunk == 2:
-                act = middle.tile([P, UNITS, PACK, P], F32, name="act_held", offset=512)
-            elif act is None:
-                act = work.tile([P, UNITS, PACK, P], F32, name="act")
+        def first_layer(chunk, units, act):
             acc = {u: bank("acc%d_%d" % (chunk, u), [P, R], SUM_BANKS[chunk][u])[:] for u in units}
-            order = ((0, DST), (1, DST), (0, SRC), (1, SRC)) if chunk < 2 else ((1, DST), (1, SRC), (0, SRC), (0, DST))
+            order = EARLY_ORDER if chunk * CHUNK < HALF else LATE_ORDER
             steps = [(u, a, side) for u in units for a, side in order]
             if chunk == 0:
                 steps.insert(1, steps.pop(len(order)))
@@ -160,59 +155,22 @@ def tile_list_msg_silu_none_kernel(
                     start=(a, side) == order[0],
                     stop=(a, side) == order[-1],
                 )
-            if chunk == 0:
-                nc.tensor.matmul_mx(
-                    idle[:],
-                    lhsT=picked_w[u, a, side].bitcast(FP8X4),
-                    lhsT_scale=edge_sc,
-                    rhs=weight,
-                    rhs_scale=weight_sc.bitcast(U8),
-                    start=True,
-                    stop=True,
-                )
             for u in units:
                 nc.scalar.activation(act[:, u, :, :], acc[u].rearrange("e (m t) -> e t m", t=PACK), SILU)
-            return act
 
-        def scale_hidden(chunk, act, between):
-            if chunk == 1:
-                hidden = middle.tile([P, PACK, CHUNK], BF16, name="hidden_middle", offset=4096, align_bytes=64)
-            elif chunk == 3:
-                hidden = late.tile([P, PACK, CHUNK], BF16, name="hidden_last", offset=0, align_bytes=64)
-            else:
-                hidden = keep.tile([P, PACK, CHUNK], BF16, name="hidden", tag="hidden%d" % chunk, align_bytes=64)
-            if chunk == 0:
-                offset = WINDOW_BYTES - GROUPED_BYTES // 2
-                grouped = reuse.tile([P, CHUNK, PACK], BF16, name="grouped_first", offset=offset, align_bytes=64)
-            else:
-                grouped = keep.tile([P, CHUNK, PACK], BF16, name="grouped", tag="grouped%d" % chunk, align_bytes=64)
-            for u in range(UNITS):
-                turned = bank("turned%d_%d" % (chunk, u), [P, PACK, UNIT], TURN_BANKS[chunk][u])
-                for t in range(PACK):
-                    nc.tensor.transpose(turned[:, t, :], act[:, u, t, :], ident[:])
-                if chunk == 0 and u == 0:
-                    staged = keep.tile([P, PACK, UNIT], F32, name="staged")
-                    nc.scalar.copy(staged[:], turned[:])
-                    nc.gpsimd.tensor_tensor(
-                        grouped[:, :UNIT, :],
-                        staged[:].rearrange("p t e -> p e t"),
-                        sm_sb[:].unsqueeze(1).to_broadcast([P, UNIT, PACK]),
-                        MULT,
-                    )
-                    continue
-                if (u, None) in between:
-                    between[u, None]()
-                for t in range(PACK):
-                    nc.scalar.activation(
-                        hidden[:, t, u * UNIT : (u + 1) * UNIT], turned[:, t, :], COPY, scale=sm_sb[:, t : t + 1]
-                    )
-                    if (u, t) in between:
-                        between[u, t]()
-            return hidden, grouped
+        def turn(chunk, u, act):
+            turned = bank("turned%d_%d" % (chunk, u), [P, PACK, UNIT], TURN_BANKS[chunk][u])
+            for t in range(PACK):
+                nc.tensor.transpose(turned[:, t, :], act[:, u, t, :], ident[:])
+            return turned
 
-        def quantize_hidden(chunk, tiles):
-            hidden, grouped = tiles
-            first = UNIT if chunk == 0 else 0
+        def scale(hidden, u, turned):
+            for t in range(PACK):
+                nc.scalar.activation(
+                    hidden[:, t, u * UNIT : (u + 1) * UNIT], turned[:, t, :], COPY, scale=sm_sb[:, t : t + 1]
+                )
+
+        def quantize(chunk, hidden, grouped, first):
             nc.scalar.copy(
                 grouped[:, first:, :].rearrange("p (c i) t -> p c t i", i=4),
                 hidden[:, :, first:].rearrange("p t (c i) -> p c t i", i=4),
@@ -220,94 +178,121 @@ def tile_list_msg_silu_none_kernel(
             edges = slice(chunk * CHUNK, (chunk + 1) * CHUNK)
             nc.vector.quantize_mx(h_w[:, edges].bitcast(FP8X4), h_sc[:, edges], grouped[:].rearrange("p n t -> p (n t)"))
 
-        def second_layer(prod, n_tile, first, last):
-            m = slice(n_tile * P, (n_tile + 1) * P)
-            nc.tensor.matmul_mx(
-                prod,
-                lhsT=wd_w[:, m].bitcast(FP8X4),
-                lhsT_scale=wd_sc[:].bitcast(U8)[:, m],
-                rhs=h_w[:, first:last].bitcast(FP8X4),
-                rhs_scale=h_sc[:, first:last],
-                start=True,
-                stop=True,
-            )
-
-        def place(n_tile, first, last, message):
-            nc.vector.tensor_tensor(
-                windows[n_tile][:].indirect(dst_list[:, first // 16 : last // 16]), message, wgo_sb[:, first:last], MULT
-            )
-            if last == J:
-                nc.sync.dma_start(out[n_tile * P : (n_tile + 1) * P, :], windows[n_tile][:])
-
-        def scatter(n_tiles, first_chunk, last_chunk, where, tag=""):
-            first, last = first_chunk * CHUNK, last_chunk * CHUNK
+        def scatter(n_tiles, first, last, where, pool, **place_of_tile):
             width = last - first
             prod = bank("prod%d_%d" % (n_tiles[0], first), [P, len(n_tiles), width], where)
             for i, n_tile in enumerate(n_tiles):
-                second_layer(prod[:, i, :], n_tile, first, last)
-            message = keep.tile([P, len(n_tiles), width], F32, name="y%d_%d" % (n_tiles[0], first), tag=tag, align_bytes=64)
+                rows = slice(n_tile * P, (n_tile + 1) * P)
+                nc.tensor.matmul_mx(
+                    prod[:, i, :],
+                    lhsT=wd_w[:, rows].bitcast(FP8X4),
+                    lhsT_scale=wd_sc[:].bitcast(U8)[:, rows],
+                    rhs=h_w[:, first:last].bitcast(FP8X4),
+                    rhs_scale=h_sc[:, first:last],
+                    start=True,
+                    stop=True,
+                )
+            name = "message%d_%d" % (n_tiles[0], first)
+            message = pool.tile([P, len(n_tiles), width], F32, name=name, align_bytes=64, **place_of_tile)
             for i, n_tile in enumerate(n_tiles):
                 nc.scalar.copy(message[:, i, :], prod[:, i, :])
-                place(n_tile, first, last, message[:, i, :])
+                nc.vector.tensor_tensor(
+                    windows[n_tile][:].indirect(dst_list[:, first // GROUP : last // GROUP]),
+                    message[:, i, :],
+                    wgo_sb[:, first:last],
+                    MULT,
+                )
+                if last == J:
+                    nc.sync.dma_start(out[n_tile * P : (n_tile + 1) * P, :], windows[n_tile][:])
 
-        def message_part(message, n_tile, first, last, where):
-            prod = bank("part%d_%d" % (n_tile, first), [P, last - first], where)
-            second_layer(prod[:], n_tile, first, last)
-            nc.scalar.copy(message, prod[:])
+        def hidden_tile(chunk, pool, **place_of_tile):
+            return pool.tile([P, PACK, CHUNK], BF16, name="hidden%d" % chunk, align_bytes=64, **place_of_tile)
 
-        gather_scales(0, nc.sync)
+        def grouped_tile(chunk):
+            return keep.tile([P, CHUNK, PACK], BF16, name="grouped%d" % chunk, align_bytes=64)
+
+        first_sc = keep.tile([P, 2, HALF], U8, name="picked_sc0", align_bytes=64)
+        gather_scales(0, first_sc)
         for a in range(PASSES):
             nc.sync.dma_start(ws_w[a][:], ws_words[a].rearrange("p r i -> p (r i)").bitcast(I32))
         nc.sync.dma_start(sm_sb[:], sm.rearrange("(p t) -> p t", t=PACK))
         nc.sync.dma_start(wd_w[:], wd_words[0].rearrange("p n i -> p (n i)").bitcast(I32))
         for q in range(QUADS):
-            nc.sync.dma_start(wd_sc[32 * q : 32 * q + ROWS, :], wd_scales[0, 4 * q : 4 * q + 4, :].bitcast(I32))
+            nc.sync.dma_start(
+                wd_sc[32 * q : 32 * q + ROWS, :], wd_scales[0, ROWS * q : ROWS * (q + 1), :].bitcast(I32)
+            )
         nc.sync.dma_start(wgo_sb[:], wgo)
 
+        gather_words(((0, DST, 0, HALF), (0, SRC, 0, LAST)), keep)
         idle = psum.tile([P, R], F32, name="idle", tag="f1")
         for u in range(WARM_UPS):
             nc.tensor.matmul_mx(
                 idle[:],
-                lhsT=tab_w[0][:, u * UNIT : (u + 1) * UNIT].bitcast(FP8X4),
-                lhsT_scale=tab_sc[:].bitcast(U8)[:, u * UNIT : (u + 1) * UNIT],
+                lhsT=picked_w[u, 0, DST].bitcast(FP8X4),
+                lhsT_scale=first_sc[:, DST, u * UNIT : (u + 1) * UNIT],
                 rhs=wt_w[:, 0, :].bitcast(FP4X4),
                 rhs_scale=wt_sc[:, 0, :].bitcast(U8),
                 start=True,
                 stop=True,
             )
-        gather_words(((0, DST, 0, HALF), (0, SRC, 0, LAST)))
-        gather_words(((1, DST, 0, CHUNK), (1, SRC, 0, CHUNK)), offset=0)
-        gather_words(((1, DST, CHUNK, J), (1, SRC, CHUNK, HALF)))
+        gather_words(((1, DST, 0, CHUNK), (1, SRC, 0, CHUNK)), after_sums0, offset=0)
+        gather_words(((1, DST, CHUNK, J), (1, SRC, CHUNK, HALF)), keep)
 
-        act = first_layer(0)
-        gather_scales(1, nc.sync)
-        gather_words(((1, SRC, HALF, J),), offset=2 * HALF)
-        quantize_hidden(0, scale_hidden(0, act, {}))
-        gather_words(((0, DST, HALF, J), (0, SRC, LAST, J)), tag="hidden0")
+        act = work.tile([P, UNITS, PACK, P], F32, name="act")
+        first_layer(0, (0, 1), act)
+        gather_scales(1, after_sums0.tile([P, 2, HALF], U8, name="picked_sc1", offset=0, align_bytes=64))
+        gather_words(((1, SRC, HALF, J),), after_sums0, offset=2 * HALF)
+        hidden = hidden_tile(0, keep, tag="hidden0")
+        offset = WINDOW_BYTES - HIDDEN_BYTES // 2
+        grouped = after_quantize0.tile([P, CHUNK, PACK], BF16, name="grouped0", offset=offset, align_bytes=64)
+        turned = turn(0, 0, act)
+        staged = keep.tile([P, PACK, UNIT], F32, name="staged")
+        nc.scalar.copy(staged[:], turned[:])
+        nc.gpsimd.tensor_tensor(
+            grouped[:, :UNIT, :],
+            staged[:].rearrange("p t e -> p e t"),
+            sm_sb[:].unsqueeze(1).to_broadcast([P, UNIT, PACK]),
+            MULT,
+        )
+        scale(hidden, 1, turn(0, 1, act))
+        quantize(0, hidden, grouped, UNIT)
+        gather_words(((0, DST, HALF, J), (0, SRC, LAST, J)), keep, tag="hidden0")
         for n in range(2):
-            windows.append(reuse.tile([P, T], F32, name="window%d" % (n + 2), offset=n * WINDOW_BYTES))
+            windows.append(after_quantize0.tile([P, T], F32, name="window%d" % (n + 2), offset=n * WINDOW_BYTES))
             nc.gpsimd.memset(windows[n + 2][:], 0.0)
-        act = first_layer(1)
-        first_messages = {(0, None): lambda: scatter((0,), 0, 1, "a1"), (0, 3): lambda: scatter((1,), 0, 1, "d0")}
-        quantize_hidden(1, scale_hidden(1, act, first_messages))
-        message = middle.tile([P, 2, CHUNK], F32, name="y_first_cover", offset=4608, align_bytes=64)
-        pair = bank("pair", [P, 2, CHUNK], "e0")
-        for i in range(2):
-            second_layer(pair[:, i, :], 2 + i, 0, CHUNK)
-        for i in range(2):
-            nc.scalar.copy(message[:, i, :], pair[:, i, :])
-            place(2 + i, 0, CHUNK, message[:, i, :])
-        act = first_layer(2)
-        last_act = first_layer(3, (0,))
-        hidden = scale_hidden(2, act, {(0, 3): lambda: scatter((0,), 1, 2, "a1")})
+
+        act = work.tile([P, UNITS, PACK, P], F32, name="act")
+        first_layer(1, (0, 1), act)
+        hidden = hidden_tile(1, after_hidden1, offset=ACT_BYTES)
+        grouped = grouped_tile(1)
+        turned = turn(1, 0, act)
+        scatter((0,), 0, CHUNK, "a1", keep)
+        scale(hidden, 0, turned)
+        scatter((1,), 0, CHUNK, "d0", keep)
+        scale(hidden, 1, turn(1, 1, act))
+        quantize(1, hidden, grouped, 0)
+        scatter((2, 3), 0, CHUNK, "e0", after_hidden1, offset=ACT_BYTES + OVERLAP)
+
+        act = after_hidden1.tile([P, UNITS, PACK, P], F32, name="act2", offset=OVERLAP)
+        first_layer(2, (0, 1), act)
+        last_act = work.tile([P, UNITS, PACK, P], F32, name="act")
+        first_layer(3, (0,), last_act)
+        hidden = hidden_tile(2, keep, tag="hidden2")
+        grouped = grouped_tile(2)
+        scale(hidden, 0, turn(2, 0, act))
+        scatter((0,), CHUNK, HALF, "a1", keep)
+        scale(hidden, 1, turn(2, 1, act))
         first_layer(3, (1,), last_act)
-        quantize_hidden(2, hidden)
-        scatter((1, 3), 1, 2, "d1", "hidden2")
-        quantize_hidden(3, scale_hidden(3, last_act, {}))
-        message = late.tile([P, HALF], F32, name="y_cover", offset=0, align_bytes=64)
-        message_part(message[:], 2, CHUNK, LAST, "f1")
-        place(2, CHUNK, LAST, message[:])
-        scatter((0,), 2, 4, "f0")
-        scatter((2,), 3, 4, "a1")
-        scatter((1,), 2, 4, "e1")
-        scatter((3,), 2, 4, "e0")
+        quantize(2, hidden, grouped, 0)
+        scatter((1, 3), CHUNK, HALF, "d1", keep, tag="hidden2")
+
+        hidden = hidden_tile(3, after_hidden3, offset=0)
+        grouped = grouped_tile(3)
+        for u in range(UNITS):
+            scale(hidden, u, turn(3, u, last_act))
+        quantize(3, hidden, grouped, 0)
+        scatter((2,), CHUNK, LAST, "f1", after_hidden3, offset=0)
+        scatter((0,), HALF, J, "f0", keep)
+        scatter((2,), LAST, J, "a1", keep)
+        scatter((1,), HALF, J, "e1", keep)
+        scatter((3,), HALF, J, "e0", keep)

from contextlib import ExitStack

import concourse.mybir as mybir
from concourse.masks import make_identity

K, R, N, T, J = 1024, 512, 512, 2048, 1024
FLOPS = 2 * J * (2 * K * R + R * N)

F32 = mybir.dt.float32
BF16 = mybir.dt.bfloat16
I32 = mybir.dt.int32
U32 = mybir.dt.uint32
U16 = mybir.dt.uint16
U8 = mybir.dt.uint8
FP8X4 = mybir.dt.float8_e4m3fn_x4
FP4X4 = mybir.dt.float4_e2m1fn_x4
MULT = mybir.AluOpType.mult
SILU = mybir.ActivationFunctionType.Silu
COPY = mybir.ActivationFunctionType.Copy

P = 128
PACK = 4
PASSES = K // (P * PACK)
QUADS = 4
ROWS = 4
GROUP = 16
UNIT = 128
CHUNK = 256
UNITS = CHUNK // UNIT
HALF = J // 2
LAST = J - CHUNK
DST, SRC = 0, 1
FIRST_ROW = P - PASSES * QUADS * ROWS
WINDOW_BYTES = T * 4
HIDDEN_BYTES = CHUNK * PACK * 2
ACT_BYTES = UNITS * R * 4
OVERLAP = 512
BANK_BYTES = 2048
WARM_UPS = HALF // UNIT

EARLY_ORDER = ((0, DST), (1, DST), (0, SRC), (1, SRC))
LATE_ORDER = ((1, DST), (1, SRC), (0, SRC), (0, DST))

SUM_BANKS = (("a0", "a1"), ("a1", "d0"), ("a1", "d0"), ("e1", "d0"))
TURN_BANKS = (("d0", "d1"), ("e0", "e1"), ("a0", "d1"), ("f0", "f1"))


def tile_list_msg_silu_none_kernel(
    tc, tab_words, tab_scales, ws_words, ws_scales, wt_words, wt_scales, sm, wd_words, wd_scales, wgo, offs, offs2, out
):
    nc = tc.nc
    with ExitStack() as ctx:
        keep = ctx.enter_context(tc.tile_pool(name="keep", bufs=1))
        after_quantize0 = ctx.enter_context(tc.tile_pool(name="after_quantize0", bufs=1))
        after_hidden3 = ctx.enter_context(tc.tile_pool(name="after_hidden3", bufs=1))
        after_hidden1 = ctx.enter_context(tc.tile_pool(name="after_hidden1", bufs=1))
        after_sums0 = ctx.enter_context(tc.tile_pool(name="after_sums0", bufs=1))
        work = ctx.enter_context(tc.tile_pool(name="work", bufs=2))
        psum = ctx.enter_context(tc.psum_pool(name="psum", bufs=1))
        sums = ctx.enter_context(tc.psum_pool(name="sums", bufs=1))

        dst_list = keep.tile([P, J // GROUP], U16, name="dst_list")
        src_list = keep.tile([P, J // GROUP], U16, name="src_list")
        lists = (dst_list, src_list)
        tab_sc = keep.tile([P, T // 4], I32, name="tab_sc", align_bytes=64)
        tab_w = [keep.tile([P, T], I32, name="tab_w%d" % a, align_bytes=64) for a in range(PASSES)]
        ws_w = [keep.tile([P, R], I32, name="ws_w%d" % a, align_bytes=64) for a in range(PASSES)]
        wt_w = keep.tile([P, PASSES, R // 2], I32, name="wt_w", align_bytes=64)
        ws_sc = keep.tile([P, PASSES, R // 4], I32, name="ws_sc", align_bytes=64)
        wt_sc = keep.tile([P, PASSES, R // 4], I32, name="wt_sc", align_bytes=64)
        wd_sc = keep.tile([P, N // 4], I32, name="wd_sc", align_bytes=64)
        planes = [keep.tile([P, PASSES, 2 * HALF // 4], I32, name="planes%d" % h, align_bytes=64) for h in range(2)]
        ident = keep.tile([P, P], F32, name="ident")
        sm_sb = keep.tile([P, PACK], F32, name="sm_sb")
        wgo_sb = keep.tile([P, J], F32, name="wgo_sb")
        wd_w = keep.tile([P, N], I32, name="wd_w", align_bytes=64)
        h_w = keep.tile([P, J], U32, name="h_w", align_bytes=64)
        h_sc = keep.tile([P, J], U8, name="h_sc", align_bytes=64)
        windows = [keep.tile([P, T], F32, name="window%d" % n) for n in range(2)]

        def load_weight_scales(tile, scales, queue):
            for q in range(QUADS):
                queue.dma_start(
                    tile[32 * q : 32 * q + ROWS, :, :],
                    scales[:, ROWS * q : ROWS * (q + 1), :].rearrange("a r n -> r a n").bitcast(I32),
                )

        nc.gpsimd.memset(wt_sc[:], 0)
        nc.gpsimd.memset(ws_sc[:], 0)
        load_weight_scales(ws_sc, ws_scales, nc.gpsimd)
        nc.vector.memset(tab_sc[0:FIRST_ROW, :], 0)
        nc.vector.memset(planes[0][:], 0)
        make_identity(nc, ident[:])
        nc.gpsimd.memset(wd_sc[:], 0)
        nc.gpsimd.memset(planes[1][:], 0)
        for window in windows:
            nc.gpsimd.memset(window[:], 0.0)

        nc.sync.dma_start(tab_sc[FIRST_ROW:P, :], tab_scales.rearrange("a q t -> q a t").bitcast(I32))
        nc.sync.dma_start(dst_list[:], offs2)
        nc.sync.dma_start(src_list[:], offs)
        nc.sync.dma_start(tab_w[0][:], tab_words[0].rearrange("p t i -> p (t i)").bitcast(I32))
        load_weight_scales(wt_sc, wt_scales, nc.sync)
        nc.sync.dma_start(wt_w[:], wt_words.rearrange("a p b -> p a b").bitcast(I32))
        nc.sync.dma_start(tab_w[1][:], tab_words[1].rearrange("p t i -> p (t i)").bitcast(I32))

        picked_w = {}

        def gather_scales(half, picked):
            entries = slice(half * HALF // GROUP, (half + 1) * HALF // GROUP)
            for side in (DST, SRC):
                nc.vector.tensor_copy(picked[:, side, :], tab_sc[:].bitcast(U8).indirect(lists[side][:, entries]))
            for q in range(QUADS):
                rows = slice(FIRST_ROW + PASSES * ROWS * q, FIRST_ROW + PASSES * ROWS * (q + 1))
                nc.sync.dma_start(
                    planes[half][32 * q : 32 * q + ROWS, :, :],
                    picked[rows, :, :].rearrange("p s e -> p (s e)").bitcast(I32),
                )

        def gather_words(parts, pool, **place_of_tile):
            total = sum(last - first for a, side, first, last in parts)
            picked = pool.tile([P, total], U32, name="picked_w%d_%d_%d_%d" % parts[0], align_bytes=64, **place_of_tile)
            at = 0
            for a, side, first, last in parts:
                entries = lists[side][:, first // GROUP : last // GROUP]
                nc.vector.tensor_copy(picked[:, at : at + last - first], tab_w[a][:].bitcast(U32).indirect(entries))
                for edge in range(first, last, UNIT):
                    picked_w[edge // UNIT, a, side] = picked[:, at + edge - first : at + edge - first + UNIT]
                at = at + last - first

        def bank(name, shape, where):
            if where[0] == "a":
                return sums.tile(shape, F32, name=name, offset=int(where[1]) * BANK_BYTES)
            return psum.tile(shape, F32, name=name, tag=where)

        def first_layer(chunk, units, act):
            acc = {u: bank("acc%d_%d" % (chunk, u), [P, R], SUM_BANKS[chunk][u])[:] for u in units}
            order = EARLY_ORDER if chunk * CHUNK < HALF else LATE_ORDER
            steps = [(u, a, side) for u in units for a, side in order]
            if chunk == 0:
                steps.insert(1, steps.pop(len(order)))
            for u, a, side in steps:
                half, start = divmod(chunk * CHUNK + u * UNIT, HALF)
                edge_sc = planes[half][:, a, :].bitcast(U8)[:, side * HALF + start : side * HALF + start + UNIT]
                if side == SRC:
                    weight, weight_sc = ws_w[a][:].bitcast(FP8X4), ws_sc[:, a, :]
                else:
                    weight, weight_sc = wt_w[:, a, :].bitcast(FP4X4), wt_sc[:, a, :]
                nc.tensor.matmul_mx(
                    acc[u],
                    lhsT=picked_w[chunk * UNITS + u, a, side].bitcast(FP8X4),
                    lhsT_scale=edge_sc,
                    rhs=weight,
                    rhs_scale=weight_sc.bitcast(U8),
                    start=(a, side) == order[0],
                    stop=(a, side) == order[-1],
                )
            for u in units:
                nc.scalar.activation(act[:, u, :, :], acc[u].rearrange("e (m t) -> e t m", t=PACK), SILU)

        def turn(chunk, u, act):
            turned = bank("turned%d_%d" % (chunk, u), [P, PACK, UNIT], TURN_BANKS[chunk][u])
            for t in range(PACK):
                nc.tensor.transpose(turned[:, t, :], act[:, u, t, :], ident[:])
            return turned

        def scale(hidden, u, turned):
            for t in range(PACK):
                nc.scalar.activation(
                    hidden[:, t, u * UNIT : (u + 1) * UNIT], turned[:, t, :], COPY, scale=sm_sb[:, t : t + 1]
                )

        def quantize(chunk, hidden, grouped, first):
            nc.scalar.copy(
                grouped[:, first:, :].rearrange("p (c i) t -> p c t i", i=4),
                hidden[:, :, first:].rearrange("p t (c i) -> p c t i", i=4),
            )
            edges = slice(chunk * CHUNK, (chunk + 1) * CHUNK)
            nc.vector.quantize_mx(h_w[:, edges].bitcast(FP8X4), h_sc[:, edges], grouped[:].rearrange("p n t -> p (n t)"))

        def scatter(n_tiles, first, last, where, pool, **place_of_tile):
            width = last - first
            prod = bank("prod%d_%d" % (n_tiles[0], first), [P, len(n_tiles), width], where)
            for i, n_tile in enumerate(n_tiles):
                rows = slice(n_tile * P, (n_tile + 1) * P)
                nc.tensor.matmul_mx(
                    prod[:, i, :],
                    lhsT=wd_w[:, rows].bitcast(FP8X4),
                    lhsT_scale=wd_sc[:].bitcast(U8)[:, rows],
                    rhs=h_w[:, first:last].bitcast(FP8X4),
                    rhs_scale=h_sc[:, first:last],
                    start=True,
                    stop=True,
                )
            name = "message%d_%d" % (n_tiles[0], first)
            message = pool.tile([P, len(n_tiles), width], F32, name=name, align_bytes=64, **place_of_tile)
            for i, n_tile in enumerate(n_tiles):
                nc.scalar.copy(message[:, i, :], prod[:, i, :])
                nc.vector.tensor_tensor(
                    windows[n_tile][:].indirect(dst_list[:, first // GROUP : last // GROUP]),
                    message[:, i, :],
                    wgo_sb[:, first:last],
                    MULT,
                )
                if last == J:
                    nc.sync.dma_start(out[n_tile * P : (n_tile + 1) * P, :], windows[n_tile][:])

        def hidden_tile(chunk, pool, **place_of_tile):
            return pool.tile([P, PACK, CHUNK], BF16, name="hidden%d" % chunk, align_bytes=64, **place_of_tile)

        def grouped_tile(chunk):
            return keep.tile([P, CHUNK, PACK], BF16, name="grouped%d" % chunk, align_bytes=64)

        first_sc = keep.tile([P, 2, HALF], U8, name="picked_sc0", align_bytes=64)
        gather_scales(0, first_sc)
        for a in range(PASSES):
            nc.sync.dma_start(ws_w[a][:], ws_words[a].rearrange("p r i -> p (r i)").bitcast(I32))
        nc.sync.dma_start(sm_sb[:], sm.rearrange("(p t) -> p t", t=PACK))
        nc.sync.dma_start(wd_w[:], wd_words[0].rearrange("p n i -> p (n i)").bitcast(I32))
        for q in range(QUADS):
            nc.sync.dma_start(
                wd_sc[32 * q : 32 * q + ROWS, :], wd_scales[0, ROWS * q : ROWS * (q + 1), :].bitcast(I32)
            )
        nc.sync.dma_start(wgo_sb[:], wgo)

        gather_words(((0, DST, 0, HALF), (0, SRC, 0, LAST)), keep)
        idle = psum.tile([P, R], F32, name="idle", tag="f1")
        for u in range(WARM_UPS):
            nc.tensor.matmul_mx(
                idle[:],
                lhsT=picked_w[u, 0, DST].bitcast(FP8X4),
                lhsT_scale=first_sc[:, DST, u * UNIT : (u + 1) * UNIT],
                rhs=wt_w[:, 0, :].bitcast(FP4X4),
                rhs_scale=wt_sc[:, 0, :].bitcast(U8),
                start=True,
                stop=True,
            )
        gather_words(((1, DST, 0, CHUNK), (1, SRC, 0, CHUNK)), after_sums0, offset=0)
        gather_words(((1, DST, CHUNK, J), (1, SRC, CHUNK, HALF)), keep)

        act = work.tile([P, UNITS, PACK, P], F32, name="act")
        first_layer(0, (0, 1), act)
        gather_scales(1, after_sums0.tile([P, 2, HALF], U8, name="picked_sc1", offset=0, align_bytes=64))
        gather_words(((1, SRC, HALF, J),), after_sums0, offset=2 * HALF)
        hidden = hidden_tile(0, keep, tag="hidden0")
        offset = WINDOW_BYTES - HIDDEN_BYTES // 2
        grouped = after_quantize0.tile([P, CHUNK, PACK], BF16, name="grouped0", offset=offset, align_bytes=64)
        turned = turn(0, 0, act)
        staged = keep.tile([P, PACK, UNIT], F32, name="staged")
        nc.scalar.copy(staged[:], turned[:])
        nc.gpsimd.tensor_tensor(
            grouped[:, :UNIT, :],
            staged[:].rearrange("p t e -> p e t"),
            sm_sb[:].unsqueeze(1).to_broadcast([P, UNIT, PACK]),
            MULT,
        )
        scale(hidden, 1, turn(0, 1, act))
        quantize(0, hidden, grouped, UNIT)
        gather_words(((0, DST, HALF, J), (0, SRC, LAST, J)), keep, tag="hidden0")
        for n in range(2):
            windows.append(after_quantize0.tile([P, T], F32, name="window%d" % (n + 2), offset=n * WINDOW_BYTES))
            nc.gpsimd.memset(windows[n + 2][:], 0.0)

        act = work.tile([P, UNITS, PACK, P], F32, name="act")
        first_layer(1, (0, 1), act)
        hidden = hidden_tile(1, after_hidden1, offset=ACT_BYTES)
        grouped = grouped_tile(1)
        turned = turn(1, 0, act)
        scatter((0,), 0, CHUNK, "a1", keep)
        scale(hidden, 0, turned)
        scatter((1,), 0, CHUNK, "d0", keep)
        scale(hidden, 1, turn(1, 1, act))
        quantize(1, hidden, grouped, 0)
        scatter((2, 3), 0, CHUNK, "e0", after_hidden1, offset=ACT_BYTES + OVERLAP)

        act = after_hidden1.tile([P, UNITS, PACK, P], F32, name="act2", offset=OVERLAP)
        first_layer(2, (0, 1), act)
        last_act = work.tile([P, UNITS, PACK, P], F32, name="act")
        first_layer(3, (0,), last_act)
        hidden = hidden_tile(2, keep, tag="hidden2")
        grouped = grouped_tile(2)
        scale(hidden, 0, turn(2, 0, act))
        scatter((0,), CHUNK, HALF, "a1", keep)
        scale(hidden, 1, turn(2, 1, act))
        first_layer(3, (1,), last_act)
        quantize(2, hidden, grouped, 0)
        scatter((1, 3), CHUNK, HALF, "d1", keep, tag="hidden2")

        hidden = hidden_tile(3, after_hidden3, offset=0)
        grouped = grouped_tile(3)
        for u in range(UNITS):
            scale(hidden, u, turn(3, u, last_act))
        quantize(3, hidden, grouped, 0)
        scatter((2,), CHUNK, LAST, "f1", after_hidden3, offset=0)
        scatter((0,), HALF, J, "f0", keep)
        scatter((2,), LAST, J, "a1", keep)
        scatter((1,), HALF, J, "e1", keep)
        scatter((3,), HALF, J, "e0", keep)
